import numpy as np
import ml_dtypes


def mxq(x, axis, fmt="e4m3"):
    dtype, down = {"e4m3": (ml_dtypes.float8_e4m3fn, 7), "e5m2": (ml_dtypes.float8_e5m2, 14)}[fmt]
    v = np.moveaxis(np.asarray(x, np.float32).astype(ml_dtypes.bfloat16).astype(np.float64), axis, -1)
    blocks = v.reshape(v.shape[:-1] + (-1, 32))
    amax = np.abs(blocks).max(-1, keepdims=True)
    byte = np.maximum(np.where(amax > 0, np.frexp(amax)[1] - 1 + 127, 0) - down, 1)
    scale = np.exp2(byte - 127.0)
    codes = (blocks / scale).astype(np.float32).astype(dtype).astype(np.float64)
    return np.moveaxis((codes * scale).reshape(v.shape), -1, axis)


WIDE = False


def mx_kscale(k):
    if not WIDE:
        return np.ones(k)
    levels = np.array([10, -10, 5, -5, 0])
    if k % 512:
        return np.exp2(np.random.permutation(np.resize(levels, k // 32))).repeat(32)
    a = np.empty((k // 512, 16))
    for p in range(k // 512):
        a[p, :8] = np.random.permutation(np.resize(levels, 8))
        for g in range(8):
            far = levels[np.abs(levels - a[p, g]) >= 10]
            a[p, g + 8] = far[np.random.randint(len(far))]
    return np.exp2(a.ravel()).repeat(32)


def f64(x):
    return np.asarray(x).astype(np.float64)


def striped(idx):
    return np.tile(idx.reshape(-1, 16).T, (8, 1)).astype(np.uint16)


def unstriped(offs):
    return offs[:16].T.reshape(-1).astype(np.int64)


E2M1 = np.array([0.0, 0.5, 1.0, 1.5, 2.0, 3.0, 4.0, 6.0, -0.0, -0.5, -1.0, -1.5, -2.0, -3.0, -4.0, -6.0])


def pack_weight(w, fmt):
    k, n = w.shape
    w = f64(np.asarray(w, np.float32).astype(ml_dtypes.bfloat16)).reshape(k // 32, 32, n)
    amax = np.abs(w).max(1)
    if fmt == "e4m3":
        byte = np.frexp(amax)[1] - 1 + 127 - 7
    else:
        mant, ex = np.frexp(amax / 6.0)
        byte = np.where(mant > 0.5, ex, ex - 1) + 127
    byte = np.clip(np.where(amax > 0, byte, 1), 1, 254)
    scaled = (w * np.exp2(127.0 - byte)[:, None, :]).reshape(k, n).astype(np.float32)
    by_word = np.ascontiguousarray(scaled.reshape(k // 512, 128, 4, n).transpose(0, 1, 3, 2))
    if fmt == "e4m3":
        words = by_word.astype(ml_dtypes.float8_e4m3fn).view(np.uint8)
    else:
        c = by_word.astype(ml_dtypes.float4_e2m1fn).view(np.uint8) & 0xF
        words = (c[..., 0::2] | (c[..., 1::2] << 4)).reshape(k // 512, 128, 2 * n)
    return np.ascontiguousarray(words), np.ascontiguousarray(byte.astype(np.uint8).reshape(k // 512, 16, n))


def unpack_weight(words, scales, fmt):
    g, _, n = scales.shape
    words = np.ascontiguousarray(words).reshape(g, 128, n, -1)
    if fmt == "e4m3":
        vals = words.view(ml_dtypes.float8_e4m3fn).astype(np.float64)
    else:
        nib = np.empty((g, 128, n, 4), np.uint8)
        nib[..., 0::2] = words & 0xF
        nib[..., 1::2] = words >> 4
        vals = E2M1[nib]
    vals = vals * np.repeat(np.exp2(scales.astype(np.float64) - 127.0), 8, axis=1)[..., None]
    return vals.transpose(0, 1, 3, 2).reshape(g * 512, n)


def gelu(v):
    return 0.5 * v * (1.0 + np.tanh(np.sqrt(2.0 / np.pi) * (v + 0.044715 * v**3)))


K, H, T, S, T2, S2 = 1024, 1024, 2048, 512, 4096, 1024

def setup_inputs():
    n = np.random.standard_normal
    s = mx_kscale(K)[:, None]
    u = mx_kscale(H)[:, None]
    tab_words, tab_scales = pack_weight(n((K, T)) * s, "e4m3")
    tab2_words, tab2_scales = pack_weight(n((H, T2)) / u / np.sqrt(H), "e4m3")
    w4_words, w4_scales = pack_weight(n((K, H)) / np.sqrt(K) / s * u.T, "e2m1")
    return {
        "tab_words": tab_words, "tab_scales": tab_scales,
        "offs": striped(np.random.permutation(T)[:S]),
        "w1": (n((K, H)) / np.sqrt(K) / s * u.T).astype(np.float32),
        "b1": (0.4 * n(H) * u[:, 0]).astype(np.float32),
        "w4_words": w4_words, "w4_scales": w4_scales,
        "b4": (0.4 * n(H) * u[:, 0]).astype(np.float32),
        "tab2_words": tab2_words, "tab2_scales": tab2_scales,
        "offs2": striped(np.random.permutation(T2)[:S2]),
        "thr": (1.0 + 0.3 * n(S)).astype(np.float32),
    }

def reference(tab_words, tab_scales, offs, w1, b1, w4_words, w4_scales, b4,
              tab2_words, tab2_scales, offs2, thr):
    v = unpack_weight(tab_words, tab_scales, "e4m3")[:, unstriped(offs)]
    v2 = unpack_weight(tab2_words, tab2_scales, "e4m3")[:, unstriped(offs2)]
    w4 = unpack_weight(w4_words, w4_scales, "e2m1")
    a = (mxq(f64(w1), 0, "e4m3").T @ v) + f64(b1)[:, None]
    c = (w4.T @ v) + f64(b4)[:, None]
    h = np.maximum(a, c)
    y = v2.T @ mxq(h, 0, "e4m3")
    return y - f64(thr)[None, :]

@@ -1,0 +1,237 @@
+from contextlib import ExitStack
+
+import concourse.mybir as mybir
+from concourse.masks import make_identity
+
+K, H, T, S, T2, S2 = 1024, 1024, 2048, 512, 4096, 1024
+FLOPS = 2 * K * H * S * 2 + 2 * H * S2 * S
+
+F32 = mybir.dt.float32
+BF16 = mybir.dt.bfloat16
+I32 = mybir.dt.int32
+U32 = mybir.dt.uint32
+U16 = mybir.dt.uint16
+U8 = mybir.dt.uint8
+FP8X4 = mybir.dt.float8_e4m3fn_x4
+FP4X4 = mybir.dt.float4_e2m1fn_x4
+ALU = mybir.AluOpType
+ACT = mybir.ActivationFunctionType
+
+P = 128
+PACK = 4
+PASS = P * PACK
+NPASS = 2
+
+
+def tile_list_maxout_face_margins_kernel(
+    tc, tab_words, tab_scales, offs, w1, b1, w4_words, w4_scales, b4, tab2_words, tab2_scales, offs2, thr, out
+):
+    nc = tc.nc
+    with ExitStack() as ctx:
+        keep = ctx.enter_context(tc.tile_pool(name="keep", bufs=1))
+        ring = ctx.enter_context(tc.tile_pool(name="ring", bufs=4))
+        psum = ctx.enter_context(tc.psum_pool(name="psum", bufs=8))
+
+        reuse = ctx.enter_context(tc.tile_pool(name="reuse", bufs=1))
+
+        def held(name, shape, dtype, tag=""):
+            return keep.tile(shape, dtype, name=name, tag=tag or name, align_bytes=64)
+
+        def placed(name, shape, dtype, offset):
+            return reuse.tile(shape, dtype, name=name, offset=offset, align_bytes=64)
+
+        idx = keep.tile([P, S // 16], U16, name="idx")
+        idx2 = keep.tile([P, S2 // 16], U16, name="idx2")
+
+        w4s_raw = held("w4s_raw", [P, NPASS * H // 4], I32)
+        tabs = held("tabs", [P, NPASS * T // 4], I32)
+        tab2s = held("tab2s", [P, T2 // 4], I32)
+        nc.vector.memset(tabs[:], 0)
+        nc.vector.memset(w4s_raw[:], 0)
+        nc.vector.memset(tab2s[:], 0)
+
+        w4w_raw = held("w4w_raw", [P, NPASS, H // 2], I32)
+        w1_raw = [[held("w1_raw%d%d" % (g, a), [P, PACK, PASS], F32) for a in range(NPASS)] for g in range(NPASS)]
+        tabw = [held("tabw0", [P, T], I32), placed("tabw1", [P, T], I32, 0)]
+        tab2w = [held("tab2w%d" % a, [P, T2], I32) for a in range(NPASS)]
+        b1_sb = held("b1_sb", [P, NPASS, PACK], F32)
+        b4_sb = held("b4_sb", [P, NPASS, PACK], F32)
+        thr_sb = held("thr_sb", [P, PACK], F32)
+
+        def load_w1(g, a):
+            rows = w1[a * PASS : (a + 1) * PASS, g * PASS : (g + 1) * PASS]
+            nc.sync.dma_start(out=w1_raw[g][a][:], in_=rows.rearrange("(p j) c -> p j c", j=PACK))
+
+        def load_words(dst, words):
+            nc.sync.dma_start(out=dst[:], in_=words.rearrange("p t i -> p (t i)").bitcast(I32))
+
+        nc.sync.dma_start(out=w4w_raw[:], in_=w4_words.bitcast(I32).rearrange("a p n -> p a n"))
+        load_w1(0, 0)
+        nc.sync.dma_start(idx[:], offs)
+        load_w1(0, 1)
+        nc.sync.dma_start(idx2[:], offs2)
+        load_words(tabw[0], tab_words[0])
+        nc.sync.dma_start(out=thr_sb[:], in_=thr.rearrange("(p c) -> p c", c=PACK))
+        load_w1(1, 0)
+        nc.sync.dma_start(out=b1_sb[:], in_=b1.rearrange("(g p t) -> p g t", g=NPASS, t=PACK))
+        nc.sync.dma_start(out=b4_sb[:], in_=b4.rearrange("(g p t) -> p g t", g=NPASS, t=PACK))
+        load_words(tabw[1], tab_words[1])
+        load_w1(1, 1)
+        load_words(tab2w[0], tab2_words[0])
+        load_words(tab2w[1], tab2_words[1])
+
+        for src, dst in ((tab_scales, tabs), (w4_scales, w4s_raw)):
+            for r in range(4):
+                nc.gpsimd.dma_start(
+                    out=dst[r:P:32, :].rearrange("q (a n) -> q a n", a=NPASS),
+                    in_=src.bitcast(I32)[:, r:16:4, :].rearrange("a q n -> q a n"),
+                )
+        for q in range(4):
+            nc.gpsimd.dma_start(out=tab2s[32 * q + 4 : 32 * q + 12, :], in_=tab2_scales.bitcast(I32)[:, 4 * q : 4 * q + 4, :])
+
+        ident = held("ident", [P, P], F32)
+        make_identity(nc, ident[:])
+        thr_ps = psum.tile([P, PACK, P], F32, name="bank")
+        for c in range(PACK):
+            nc.tensor.transpose(thr_ps[:, c, :], thr_sb[:, c : c + 1].to_broadcast([P, P]), ident[:])
+
+        w4w = held("w4w", [P, NPASS, 2 * H], U8)
+        w4s = held("w4s", [P, NPASS, H], U8)
+        for a in range(NPASS):
+            nc.vector.tensor_copy(
+                out=w4w[:, a, :].bitcast(U16).rearrange("p (g t m) -> p g t m", g=NPASS, t=PACK),
+                in_=w4w_raw[:, a, :].bitcast(U16).rearrange("p (g m t) -> p g t m", g=NPASS, t=PACK),
+            )
+        vs = [held("vs%d" % a, [P, S], U8) for a in range(NPASS)]
+        for a in range(NPASS):
+            nc.vector.tensor_copy(vs[a][:], tabs[:].bitcast(U8)[:, a * T : (a + 1) * T].indirect(idx[:]))
+        nc.vector.tensor_copy(
+            out=w4s[:].rearrange("p a (g t m) -> p (a g) t m", g=NPASS, t=PACK),
+            in_=w4s_raw[:].bitcast(U8).rearrange("p (u m t) -> p u t m", u=NPASS * NPASS, t=PACK),
+        )
+
+        w1_bf = [
+            [held("w1_bf00", [P, PASS * PACK], BF16), held("w1_bf01", [P, PASS * PACK], BF16)],
+            [held("w1_bf10", [P, PASS * PACK], BF16), placed("w1_bf11", [P, PASS * PACK], BF16, 2048)],
+        ]
+        w1w = [
+            [held("w1w00", [P, PASS], U32, "tabs"), held("w1w01", [P, PASS], U32, "w4s_raw")],
+            [placed("w1w10", [P, PASS], U32, 0), held("w1w11", [P, PASS], U32)],
+        ]
+        w1s = [[held("w1s%d%d" % (g, a), [P, PASS], U8) for a in range(NPASS)] for g in range(NPASS)]
+
+        def round_w1(g, a, on_vector):
+            dst = w1_bf[g][a][:].rearrange("p (t m j) -> p m t j", t=PACK, j=PACK)
+            src = w1_raw[g][a][:].rearrange("p j (m t) -> p m t j", t=PACK)
+            if on_vector:
+                nc.vector.tensor_copy(out=dst, in_=src)
+            else:
+                nc.scalar.copy(out=dst, in_=src)
+
+        def quantize_w1(g, a):
+            nc.vector.quantize_mx(out=w1w[g][a][:].bitcast(FP8X4), scales=w1s[g][a][:], in_=w1_bf[g][a][:])
+
+        round_w1(0, 0, False)
+        quantize_w1(0, 0)
+        round_w1(0, 1, False)
+        thr_all = held("thr_all", [P, S], F32)
+        nc.scalar.copy(out=thr_all[:].rearrange("q (p c) -> q p c", c=PACK), in_=thr_ps[:].rearrange("q c p -> q p c"))
+        vw = [held("vw0", [P, S], U32, "w1_bf00")]
+        nc.vector.tensor_copy(vw[0][:], tabw[0][:].bitcast(U32).indirect(idx[:]))
+        quantize_w1(0, 1)
+        v2s = held("v2s", [P, S2], U8)
+        nc.vector.tensor_copy(v2s[:], tab2s[:].bitcast(U8).indirect(idx2[:]))
+        vw.append(held("vw1", [P, S], U32, "tab2s"))
+        nc.vector.tensor_copy(vw[1][:], tabw[1][:].bitcast(U32).indirect(idx[:]))
+        round_w1(1, 0, False)
+        quantize_w1(1, 0)
+        round_w1(1, 1, True)
+        quantize_w1(1, 1)
+
+        h_planes = [placed("h_planes0", [P, PACK, S], BF16, 2048), held("h_planes1", [P, PACK, S], BF16)]
+        h_bf = [held("h_bf%d" % g, [P, S * PACK], BF16) for g in range(NPASS)]
+        hw = [held("hw%d" % g, [P, S], U32) for g in range(NPASS)]
+        hs = [held("hs%d" % g, [P, S], U8) for g in range(NPASS)]
+
+        def maxout(g):
+            for t in range(PACK):
+                a_ps = psum.tile([P, S], F32, name="bank")
+                c_ps = psum.tile([P, S], F32, name="bank")
+                col = g * PASS + t * P
+                for a in range(NPASS):
+                    nc.tensor.matmul_mx(
+                        out=a_ps[:],
+                        lhsT=w1w[g][a][:, t * P : (t + 1) * P].bitcast(FP8X4),
+                        lhsT_scale=w1s[g][a][:, t * P : (t + 1) * P],
+                        rhs=vw[a][:].bitcast(FP8X4),
+                        rhs_scale=vs[a][:],
+                        start=(a == 0),
+                        stop=(a == NPASS - 1),
+                    )
+                for a in range(NPASS):
+                    nc.tensor.matmul_mx(
+                        out=c_ps[:],
+                        lhsT=w4w[:, a, 2 * col : 2 * (col + P)].bitcast(FP4X4),
+                        lhsT_scale=w4s[:, a, col : col + P],
+                        rhs=vw[a][:].bitcast(FP8X4),
+                        rhs_scale=vs[a][:],
+                        start=(a == 0),
+                        stop=(a == NPASS - 1),
+                    )
+                a_sb = held("a_sb%d%d" % (g, t), [P, S], F32)
+                nc.scalar.activation(out=a_sb[:], in_=a_ps[:], func=ACT.Identity, bias=b1_sb[:, g, t : t + 1])
+                nc.vector.scalar_tensor_tensor(
+                    out=h_planes[g][:, t, :], in0=c_ps[:], scalar=b4_sb[:, g, t : t + 1], in1=a_sb[:],
+                    op0=ALU.add, op1=ALU.max,
+                )
+
+        def interleave_h(g):
+            dst = h_bf[g][:].rearrange("p (c i t) -> p c t i", i=4, t=PACK)
+            src = h_planes[g][:].rearrange("p t (c i) -> p c t i", i=4)
+            nc.scalar.copy(out=dst, in_=src)
+
+        def quantize_h(g):
+            nc.vector.quantize_mx(out=hw[g][:].bitcast(FP8X4), scales=hs[g][:], in_=h_bf[g][:])
+
+        half = S2 // 2
+
+        def gather_v2(g, u):
+            nc.vector.tensor_copy(
+                v2w[g][:, u * half : (u + 1) * half],
+                tab2w[g][:].bitcast(U32).indirect(idx2[:, u * half // 16 : (u + 1) * half // 16]),
+            )
+
+        maxout(0)
+        maxout(1)
+        interleave_h(0)
+        interleave_h(1)
+        v2w = [held("v2w0", [P, S2], U32, "a_sb13")]
+        gather_v2(0, 0)
+        quantize_h(0)
+        gather_v2(0, 1)
+        v2w.append(held("v2w1", [P, S2], U32, "tab2w0"))
+        gather_v2(1, 0)
+        quantize_h(1)
+        gather_v2(1, 1)
+
+        y_ps = [psum.tile([P, S], F32, name="bank") for i in range(S2 // P)]
+
+        def score(i, g):
+            cols = slice(i * P, (i + 1) * P)
+            nc.tensor.matmul_mx(
+                out=y_ps[i][:],
+                lhsT=v2w[g][:, cols].bitcast(FP8X4),
+                lhsT_scale=v2s[4 + 4 * g : P, cols],
+                rhs=hw[g][:].bitcast(FP8X4),
+                rhs_scale=hs[g][:],
+                start=(g == 0),
+                stop=(g == NPASS - 1),
+            )
+
+        for i in range(S2 // P):
+            score(i, 0)
+        for i in range(S2 // P):
+            score(i, 1)
+            y_sb = ring.tile([P, S], F32, name="y_sb", bufs=8)
+            nc.vector.tensor_tensor(out=y_sb[:], in0=y_ps[i][:], in1=thr_all[:], op=ALU.subtract)
+            nc.sync.dma_start(out=out[i * P : (i + 1) * P, :], in_=y_sb[:])

@@ -30,160 +30,153 @@ def tile_list_maxout_face_margins_kernel(
     with ExitStack() as ctx:
         keep = ctx.enter_context(tc.tile_pool(name="keep", bufs=1))
         ring = ctx.enter_context(tc.tile_pool(name="ring", bufs=4))
-        psum = ctx.enter_context(tc.psum_pool(name="psum", bufs=8))
-
+        psum = ctx.enter_context(tc.psum_pool(name="psum", bufs=1))
         reuse = ctx.enter_context(tc.tile_pool(name="reuse", bufs=1))
-
-        def held(name, shape, dtype, tag=""):
-            return keep.tile(shape, dtype, name=name, tag=tag or name, align_bytes=64)
 
         def placed(name, shape, dtype, offset):
             return reuse.tile(shape, dtype, name=name, offset=offset, align_bytes=64)
 
+
+        def held(name, shape, dtype, tag=""):
+            return keep.tile(shape, dtype, name=name, tag=tag or name, align_bytes=64)
+
         idx = keep.tile([P, S // 16], U16, name="idx")
         idx2 = keep.tile([P, S2 // 16], U16, name="idx2")
 
-        w4s_raw = held("w4s_raw", [P, NPASS * H // 4], I32)
-        tabs = held("tabs", [P, NPASS * T // 4], I32)
-        tab2s = held("tab2s", [P, T2 // 4], I32)
-        nc.vector.memset(tabs[:], 0)
-        nc.vector.memset(w4s_raw[:], 0)
-        nc.vector.memset(tab2s[:], 0)
-
-        w4w_raw = held("w4w_raw", [P, NPASS, H // 2], I32)
-        w1_raw = [[held("w1_raw%d%d" % (g, a), [P, PACK, PASS], F32) for a in range(NPASS)] for g in range(NPASS)]
-        tabw = [held("tabw0", [P, T], I32), placed("tabw1", [P, T], I32, 0)]
-        tab2w = [held("tab2w%d" % a, [P, T2], I32) for a in range(NPASS)]
-        b1_sb = held("b1_sb", [P, NPASS, PACK], F32)
-        b4_sb = held("b4_sb", [P, NPASS, PACK], F32)
-        thr_sb = held("thr_sb", [P, PACK], F32)
-
-        def load_w1(g, a):
+        def load_w1(g, a, raw):
             rows = w1[a * PASS : (a + 1) * PASS, g * PASS : (g + 1) * PASS]
-            nc.sync.dma_start(out=w1_raw[g][a][:], in_=rows.rearrange("(p j) c -> p j c", j=PACK))
+            nc.sync.dma_start(out=raw[:], in_=rows.rearrange("(p j) c -> p j c", j=PACK))
+            return raw
 
         def load_words(dst, words):
             nc.sync.dma_start(out=dst[:], in_=words.rearrange("p t i -> p (t i)").bitcast(I32))
+            return dst
 
+        def round_w1(raw, dst, on_vector):
+            grouped = dst[:].rearrange("p (t m j) -> p m t j", t=PACK, j=PACK)
+            src = raw[:].rearrange("p j (m t) -> p m t j", t=PACK)
+            if on_vector:
+                nc.vector.tensor_copy(out=grouped, in_=src)
+            else:
+                nc.scalar.copy(out=grouped, in_=src)
+
+        w1w = {}
+        w1s = {}
+
+        def quantize_w1(g, a, src, words, scales):
+            w1w.setdefault((g, a), words)
+            w1s.setdefault((g, a), scales)
+            nc.vector.quantize_mx(out=words[:].bitcast(FP8X4), scales=scales[:], in_=src[:])
+
+        tabs = held("tabs", [P, NPASS * T // 4], I32)
+        w4s_raw = placed("w4s_raw", [P, NPASS * H // 4], I32, 0)
+        nc.vector.memset(tabs[:], 0)
+        nc.vector.memset(w4s_raw[:], 0)
+
+        w4w_raw = held("w4w_raw", [P, NPASS, H // 2], I32)
         nc.sync.dma_start(out=w4w_raw[:], in_=w4_words.bitcast(I32).rearrange("a p n -> p a n"))
-        load_w1(0, 0)
         nc.sync.dma_start(idx[:], offs)
-        load_w1(0, 1)
         nc.sync.dma_start(idx2[:], offs2)
-        load_words(tabw[0], tab_words[0])
-        nc.sync.dma_start(out=thr_sb[:], in_=thr.rearrange("(p c) -> p c", c=PACK))
-        load_w1(1, 0)
-        nc.sync.dma_start(out=b1_sb[:], in_=b1.rearrange("(g p t) -> p g t", g=NPASS, t=PACK))
-        nc.sync.dma_start(out=b4_sb[:], in_=b4.rearrange("(g p t) -> p g t", g=NPASS, t=PACK))
-        load_words(tabw[1], tab_words[1])
-        load_w1(1, 1)
-        load_words(tab2w[0], tab2_words[0])
-        load_words(tab2w[1], tab2_words[1])
-
+        raw00 = load_w1(0, 0, held("raw00", [P, PACK, PASS], F32))
+        raw01 = load_w1(0, 1, held("raw01", [P, PACK, PASS], F32))
+        b1_sb = held("b1_sb", [P, NPASS, PACK], F32)
+        b4_sb = held("b4_sb", [P, NPASS, PACK], F32)
+        thr_sb = held("thr_sb", [P, PACK], F32)
+        nc.gpsimd.dma_start(out=thr_sb[:], in_=thr.rearrange("(p c) -> p c", c=PACK))
+        nc.gpsimd.dma_start(out=b1_sb[:], in_=b1.rearrange("(g p t) -> p g t", g=NPASS, t=PACK))
+        nc.gpsimd.dma_start(out=b4_sb[:], in_=b4.rearrange("(g p t) -> p g t", g=NPASS, t=PACK))
         for src, dst in ((tab_scales, tabs), (w4_scales, w4s_raw)):
             for r in range(4):
-                nc.gpsimd.dma_start(
+                nc.sync.dma_start(
                     out=dst[r:P:32, :].rearrange("q (a n) -> q a n", a=NPASS),
                     in_=src.bitcast(I32)[:, r:16:4, :].rearrange("a q n -> q a n"),
                 )
-        for q in range(4):
-            nc.gpsimd.dma_start(out=tab2s[32 * q + 4 : 32 * q + 12, :], in_=tab2_scales.bitcast(I32)[:, 4 * q : 4 * q + 4, :])
-
-        ident = held("ident", [P, P], F32)
-        make_identity(nc, ident[:])
-        thr_ps = psum.tile([P, PACK, P], F32, name="bank")
-        for c in range(PACK):
-            nc.tensor.transpose(thr_ps[:, c, :], thr_sb[:, c : c + 1].to_broadcast([P, P]), ident[:])
 
         w4w = held("w4w", [P, NPASS, 2 * H], U8)
-        w4s = held("w4s", [P, NPASS, H], U8)
         for a in range(NPASS):
             nc.vector.tensor_copy(
                 out=w4w[:, a, :].bitcast(U16).rearrange("p (g t m) -> p g t m", g=NPASS, t=PACK),
                 in_=w4w_raw[:, a, :].bitcast(U16).rearrange("p (g m t) -> p g t m", g=NPASS, t=PACK),
             )
+        raw10 = load_w1(1, 0, held("raw10", [P, PACK, PASS], F32, "w4w_raw"))
         vs = [held("vs%d" % a, [P, S], U8) for a in range(NPASS)]
         for a in range(NPASS):
             nc.vector.tensor_copy(vs[a][:], tabs[:].bitcast(U8)[:, a * T : (a + 1) * T].indirect(idx[:]))
+        w4s = held("w4s", [P, NPASS, H], U8, "tabs")
         nc.vector.tensor_copy(
             out=w4s[:].rearrange("p a (g t m) -> p (a g) t m", g=NPASS, t=PACK),
             in_=w4s_raw[:].bitcast(U8).rearrange("p (u m t) -> p u t m", u=NPASS * NPASS, t=PACK),
         )
 
-        w1_bf = [
-            [held("w1_bf00", [P, PASS * PACK], BF16), held("w1_bf01", [P, PASS * PACK], BF16)],
-            [held("w1_bf10", [P, PASS * PACK], BF16), placed("w1_bf11", [P, PASS * PACK], BF16, 2048)],
-        ]
-        w1w = [
-            [held("w1w00", [P, PASS], U32, "tabs"), held("w1w01", [P, PASS], U32, "w4s_raw")],
-            [placed("w1w10", [P, PASS], U32, 0), held("w1w11", [P, PASS], U32)],
-        ]
-        w1s = [[held("w1s%d%d" % (g, a), [P, PASS], U8) for a in range(NPASS)] for g in range(NPASS)]
+        bf00 = held("bf00", [P, PASS * PACK], BF16)
+        round_w1(raw00, bf00, False)
+        tabw0 = load_words(held("tabw0", [P, T], I32, "raw00"), tab_words[0])
+        quantize_w1(0, 0, bf00, held("w1w00", [P, PASS], U32), held("w1s00", [P, PASS], U8))
+        tabw1 = load_words(held("tabw1", [P, T], I32, "bf00"), tab_words[1])
 
-        def round_w1(g, a, on_vector):
-            dst = w1_bf[g][a][:].rearrange("p (t m j) -> p m t j", t=PACK, j=PACK)
-            src = w1_raw[g][a][:].rearrange("p j (m t) -> p m t j", t=PACK)
-            if on_vector:
-                nc.vector.tensor_copy(out=dst, in_=src)
-            else:
-                nc.scalar.copy(out=dst, in_=src)
+        bf01 = held("bf01", [P, PASS * PACK], BF16)
+        round_w1(raw01, bf01, False)
+        raw11 = load_w1(1, 1, held("raw11", [P, PACK, PASS], F32, "raw01"))
+        quantize_w1(0, 1, bf01, held("w1w01", [P, PASS], U32), placed("w1s01", [P, PASS], U8, 0))
+        tab2s = held("tab2s", [P, T2 // 4], I32, "bf01")
+        nc.vector.memset(tab2s[:], 0)
+        for r in range(4):
+            for a in range(NPASS):
+                nc.sync.dma_start(out=tab2s[4 + 4 * a + r : P : 32, :], in_=tab2_scales.bitcast(I32)[a, r:16:4, :])
 
-        def quantize_w1(g, a):
-            nc.vector.quantize_mx(out=w1w[g][a][:].bitcast(FP8X4), scales=w1s[g][a][:], in_=w1_bf[g][a][:])
-
-        round_w1(0, 0, False)
-        quantize_w1(0, 0)
-        round_w1(0, 1, False)
+        ident = held("ident", [P, P], F32)
+        make_identity(nc, ident[:])
+        thr_ps = psum.tile([P, PACK, P], F32, name="thr_ps", tag="bank7")
+        for c in range(PACK):
+            nc.tensor.transpose(thr_ps[:, c, :], thr_sb[:, c : c + 1].to_broadcast([P, P]), ident[:])
         thr_all = held("thr_all", [P, S], F32)
         nc.scalar.copy(out=thr_all[:].rearrange("q (p c) -> q p c", c=PACK), in_=thr_ps[:].rearrange("q c p -> q p c"))
-        vw = [held("vw0", [P, S], U32, "w1_bf00")]
-        nc.vector.tensor_copy(vw[0][:], tabw[0][:].bitcast(U32).indirect(idx[:]))
-        quantize_w1(0, 1)
-        v2s = held("v2s", [P, S2], U8)
-        nc.vector.tensor_copy(v2s[:], tab2s[:].bitcast(U8).indirect(idx2[:]))
-        vw.append(held("vw1", [P, S], U32, "tab2s"))
-        nc.vector.tensor_copy(vw[1][:], tabw[1][:].bitcast(U32).indirect(idx[:]))
-        round_w1(1, 0, False)
-        quantize_w1(1, 0)
-        round_w1(1, 1, True)
-        quantize_w1(1, 1)
 
-        h_planes = [placed("h_planes0", [P, PACK, S], BF16, 2048), held("h_planes1", [P, PACK, S], BF16)]
+        bf10 = held("bf10", [P, PASS * PACK], BF16)
+        round_w1(raw10, bf10, False)
+        vw = [placed("vw0", [P, S], U32, 1024), held("vw1", [P, S], U32)]
+        nc.vector.tensor_copy(vw[0][:], tabw0[:].bitcast(U32).indirect(idx[:]))
+        nc.vector.tensor_copy(vw[1][:], tabw1[:].bitcast(U32).indirect(idx[:]))
+        quantize_w1(1, 0, bf10, held("w1w10", [P, PASS], U32, "bf00"), held("w1s10", [P, PASS], U8))
+        tab2w = [load_words(held("tab2w0", [P, T2], I32, "bf10"), tab2_words[0])]
+
+        h_planes = [held("h_planes0", [P, PACK, S], BF16)]
         h_bf = [held("h_bf%d" % g, [P, S * PACK], BF16) for g in range(NPASS)]
-        hw = [held("hw%d" % g, [P, S], U32) for g in range(NPASS)]
         hs = [held("hs%d" % g, [P, S], U8) for g in range(NPASS)]
 
-        def maxout(g):
-            for t in range(PACK):
-                a_ps = psum.tile([P, S], F32, name="bank")
-                c_ps = psum.tile([P, S], F32, name="bank")
-                col = g * PASS + t * P
-                for a in range(NPASS):
-                    nc.tensor.matmul_mx(
-                        out=a_ps[:],
-                        lhsT=w1w[g][a][:, t * P : (t + 1) * P].bitcast(FP8X4),
-                        lhsT_scale=w1s[g][a][:, t * P : (t + 1) * P],
-                        rhs=vw[a][:].bitcast(FP8X4),
-                        rhs_scale=vs[a][:],
-                        start=(a == 0),
-                        stop=(a == NPASS - 1),
-                    )
-                for a in range(NPASS):
-                    nc.tensor.matmul_mx(
-                        out=c_ps[:],
-                        lhsT=w4w[:, a, 2 * col : 2 * (col + P)].bitcast(FP4X4),
-                        lhsT_scale=w4s[:, a, col : col + P],
-                        rhs=vw[a][:].bitcast(FP8X4),
-                        rhs_scale=vs[a][:],
-                        start=(a == 0),
-                        stop=(a == NPASS - 1),
-                    )
-                a_sb = held("a_sb%d%d" % (g, t), [P, S], F32)
-                nc.scalar.activation(out=a_sb[:], in_=a_ps[:], func=ACT.Identity, bias=b1_sb[:, g, t : t + 1])
-                nc.vector.scalar_tensor_tensor(
-                    out=h_planes[g][:, t, :], in0=c_ps[:], scalar=b4_sb[:, g, t : t + 1], in1=a_sb[:],
-                    op0=ALU.add, op1=ALU.max,
-                )
+        def project_a(g, t, a, a_ps):
+            nc.tensor.matmul_mx(
+                out=a_ps[:],
+                lhsT=w1w[g, a][:, t * P : (t + 1) * P].bitcast(FP8X4),
+                lhsT_scale=w1s[g, a][:, t * P : (t + 1) * P],
+                rhs=vw[a][:].bitcast(FP8X4),
+                rhs_scale=vs[a][:],
+                start=(a == 0),
+                stop=(a == NPASS - 1),
+            )
+
+        def project_c(g, t, a, c_ps):
+            col = g * PASS + t * P
+            nc.tensor.matmul_mx(
+                out=c_ps[:],
+                lhsT=w4w[:, a, 2 * col : 2 * (col + P)].bitcast(FP4X4),
+                lhsT_scale=w4s[:, a, col : col + P],
+                rhs=vw[a][:].bitcast(FP8X4),
+                rhs_scale=vs[a][:],
+                start=(a == 0),
+                stop=(a == NPASS - 1),
+            )
+
+        def bank(b):
+            return psum.tile([P, S], F32, name="bank", tag="bank%d" % b)
+
+        def take_max(g, t, a_ps, c_ps):
+            a_sb = held("a_sb%d%d" % (g, t), [P, S], F32, "h_planes0" if (g, t) == (1, 0) else "")
+            nc.scalar.activation(out=a_sb[:], in_=a_ps[:], func=ACT.Identity, bias=b1_sb[:, g, t : t + 1])
+            nc.vector.scalar_tensor_tensor(
+                out=h_planes[g][:, t, :], in0=c_ps[:], scalar=b4_sb[:, g, t : t + 1], in1=a_sb[:],
+                op0=ALU.add, op1=ALU.max,
+            )
 
         def interleave_h(g):
             dst = h_bf[g][:].rearrange("p (c i t) -> p c t i", i=4, t=PACK)
@@ -201,20 +194,47 @@ def tile_list_maxout_face_margins_kernel(
                 tab2w[g][:].bitcast(U32).indirect(idx2[:, u * half // 16 : (u + 1) * half // 16]),
             )
 
-        maxout(0)
-        maxout(1)
+        a_ps = [bank(t) for t in range(PACK)]
+        c_ps = [bank(PACK + t) for t in range(PACK)]
+        for t in range(PACK):
+            project_a(0, t, 0, a_ps[t])
+            project_c(0, t, 0, c_ps[t])
+        for t in range(PACK):
+            project_a(0, t, 1, a_ps[t])
+            project_c(0, t, 1, c_ps[t])
+            take_max(0, t, a_ps[t], c_ps[t])
+        tab2w.append(load_words(held("tab2w1", [P, T2], I32, "a_sb00"), tab2_words[1]))
         interleave_h(0)
+
+        bf11 = held("bf11", [P, PASS * PACK], BF16, "a_sb03")
+        round_w1(raw11, bf11, True)
+        quantize_w1(1, 1, bf11, held("w1w11", [P, PASS], U32), held("w1s11", [P, PASS], U8))
+        v2s = held("v2s", [P, S2], U8, "a_sb03")
+        nc.vector.tensor_copy(v2s[:], tab2s[:].bitcast(U8).indirect(idx2[:]))
+        h_planes.append(held("h_planes1", [P, PACK, S], BF16, "bf01"))
+
+        a_ps = [bank(t) for t in range(PACK)]
+        c_ps = [bank(PACK + t) for t in range(PACK)]
+        for t in range(PACK):
+            project_a(1, t, 0, a_ps[t])
+            project_c(1, t, 0, c_ps[t])
+            project_c(1, t, 1, c_ps[t])
+        for t in range(PACK):
+            project_a(1, t, 1, a_ps[t])
+            take_max(1, t, a_ps[t], c_ps[t])
         interleave_h(1)
-        v2w = [held("v2w0", [P, S2], U32, "a_sb13")]
-        gather_v2(0, 0)
+
+        hw = [held("hw0", [P, S], U32, "a_sb13"), held("hw1", [P, S], U32)]
         quantize_h(0)
+        v2w = [held("v2w0", [P, S2], U32, "h_bf0")]
+        gather_v2(0, 0)
         gather_v2(0, 1)
-        v2w.append(held("v2w1", [P, S2], U32, "tab2w0"))
-        gather_v2(1, 0)
         quantize_h(1)
+        v2w.append(held("v2w1", [P, S2], U32, "h_bf1"))
+        gather_v2(1, 0)
         gather_v2(1, 1)
 
-        y_ps = [psum.tile([P, S], F32, name="bank") for i in range(S2 // P)]
+        y_ps = [bank(i) for i in range(S2 // P)]
 
         def score(i, g):
             cols = slice(i * P, (i + 1) * P)

@@ -68,58 +68,70 @@ def tile_list_maxout_face_margins_kernel(
             w1s.setdefault((g, a), scales)
             nc.vector.quantize_mx(out=words[:].bitcast(FP8X4), scales=scales[:], in_=src[:])
 
+        R1, R2, R3, R4, R5, R6, R7 = 0, 16896, 27136, 35328, 43520, 49664, 53760
         tabs = held("tabs", [P, NPASS * T // 4], I32)
-        w4s_raw = placed("w4s_raw", [P, NPASS * H // 4], I32, 0)
         nc.vector.memset(tabs[:], 0)
-        nc.vector.memset(w4s_raw[:], 0)
 
-        w4w_raw = held("w4w_raw", [P, NPASS, H // 2], I32)
-        nc.sync.dma_start(out=w4w_raw[:], in_=w4_words.bitcast(I32).rearrange("a p n -> p a n"))
+        w4w_raw = [placed("w4w_raw0", [P, H // 2], I32, R1), placed("w4w_raw1", [P, H // 2], I32, R2 + 1536)]
+        for a in range(NPASS):
+            nc.sync.dma_start(out=w4w_raw[a][:], in_=w4_words.bitcast(I32)[a])
         nc.sync.dma_start(idx[:], offs)
         nc.sync.dma_start(idx2[:], offs2)
-        raw00 = load_w1(0, 0, held("raw00", [P, PACK, PASS], F32))
-        raw01 = load_w1(0, 1, held("raw01", [P, PACK, PASS], F32))
-        b1_sb = held("b1_sb", [P, NPASS, PACK], F32)
+        raw00 = load_w1(0, 0, placed("raw00", [P, PACK, PASS], F32, R3))
+        b1_sb = [held("b1_sb0", [P, PACK], F32), placed("b1_sb1", [P, PACK], F32, R6)]
         b4_sb = held("b4_sb", [P, NPASS, PACK], F32)
         thr_sb = held("thr_sb", [P, PACK], F32)
+        b1_rows = b1.rearrange("(g p t) -> g p t", g=NPASS, t=PACK)
         nc.gpsimd.dma_start(out=thr_sb[:], in_=thr.rearrange("(p c) -> p c", c=PACK))
-        nc.gpsimd.dma_start(out=b1_sb[:], in_=b1.rearrange("(g p t) -> p g t", g=NPASS, t=PACK))
+        nc.gpsimd.dma_start(out=b1_sb[0][:], in_=b1_rows[0])
         nc.gpsimd.dma_start(out=b4_sb[:], in_=b4.rearrange("(g p t) -> p g t", g=NPASS, t=PACK))
-        for src, dst in ((tab_scales, tabs), (w4_scales, w4s_raw)):
+        nc.gpsimd.dma_start(out=b1_sb[1][:], in_=b1_rows[1])
+
+        def load_scales(dst, src):
             for r in range(4):
                 nc.sync.dma_start(
                     out=dst[r:P:32, :].rearrange("q (a n) -> q a n", a=NPASS),
                     in_=src.bitcast(I32)[:, r:16:4, :].rearrange("a q n -> q a n"),
                 )
 
+        load_scales(tabs, tab_scales)
+
         w4w = held("w4w", [P, NPASS, 2 * H], U8)
         for a in range(NPASS):
             nc.vector.tensor_copy(
                 out=w4w[:, a, :].bitcast(U16).rearrange("p (g t m) -> p g t m", g=NPASS, t=PACK),
-                in_=w4w_raw[:, a, :].bitcast(U16).rearrange("p (g m t) -> p g t m", g=NPASS, t=PACK),
+                in_=w4w_raw[a][:].bitcast(U16).rearrange("p (g m t) -> p g t m", g=NPASS, t=PACK),
             )
-        raw10 = load_w1(1, 0, held("raw10", [P, PACK, PASS], F32, "w4w_raw"))
+        raw01 = load_w1(0, 1, placed("raw01", [P, PACK, PASS], F32, R1))
+        tabw0 = load_words(placed("tabw0", [P, T], I32, R2 + 2048), tab_words[0])
+        w4s_raw = placed("w4s_raw", [P, NPASS * H // 4], I32, R2)
+        nc.vector.memset(w4s_raw[:], 0)
+        load_scales(w4s_raw, w4_scales)
+
         vs = [held("vs%d" % a, [P, S], U8) for a in range(NPASS)]
         for a in range(NPASS):
             nc.vector.tensor_copy(vs[a][:], tabs[:].bitcast(U8)[:, a * T : (a + 1) * T].indirect(idx[:]))
-        w4s = held("w4s", [P, NPASS, H], U8, "tabs")
+
+        bf00 = placed("bf00", [P, PASS * PACK], BF16, R4)
+        round_w1(raw00, bf00, False)
+        raw10 = load_w1(1, 0, placed("raw10", [P, PACK, PASS], F32, R3))
+        quantize_w1(0, 0, bf00, held("w1w00", [P, PASS], U32), held("w1s00", [P, PASS], U8))
+        tabw1 = load_words(placed("tabw1", [P, T], I32, R4), tab_words[1])
+
+        vw = [held("vw0", [P, S], U32, "tabs")]
+        nc.vector.tensor_copy(vw[0][:], tabw0[:].bitcast(U32).indirect(idx[:]))
+        w4s = placed("w4s", [P, NPASS, H], U8, R2 + 2048)
         nc.vector.tensor_copy(
             out=w4s[:].rearrange("p a (g t m) -> p (a g) t m", g=NPASS, t=PACK),
             in_=w4s_raw[:].bitcast(U8).rearrange("p (u m t) -> p u t m", u=NPASS * NPASS, t=PACK),
         )
 
-        bf00 = held("bf00", [P, PASS * PACK], BF16)
-        round_w1(raw00, bf00, False)
-        tabw0 = load_words(held("tabw0", [P, T], I32, "raw00"), tab_words[0])
-        quantize_w1(0, 0, bf00, held("w1w00", [P, PASS], U32), held("w1s00", [P, PASS], U8))
-        tabw1 = load_words(held("tabw1", [P, T], I32, "bf00"), tab_words[1])
-
-        bf01 = held("bf01", [P, PASS * PACK], BF16)
+        bf01 = placed("bf01", [P, PASS * PACK], BF16, R5)
         round_w1(raw01, bf01, False)
-        raw11 = load_w1(1, 1, held("raw11", [P, PACK, PASS], F32, "raw01"))
-        quantize_w1(0, 1, bf01, held("w1w01", [P, PASS], U32), placed("w1s01", [P, PASS], U8, 0))
-        tab2s = held("tab2s", [P, T2 // 4], I32, "bf01")
-        nc.vector.memset(tab2s[:], 0)
+        raw11 = load_w1(1, 1, placed("raw11", [P, PACK, PASS], F32, R1))
+        quantize_w1(0, 1, bf01, held("w1w01", [P, PASS], U32), placed("w1s01", [P, PASS], U8, R2))
+        tab2s = placed("tab2s", [P, T2 // 4], I32, R5 + 2048)
+        nc.gpsimd.memset(tab2s[:], 0)
         for r in range(4):
             for a in range(NPASS):
                 nc.sync.dma_start(out=tab2s[4 + 4 * a + r : P : 32, :], in_=tab2_scales.bitcast(I32)[a, r:16:4, :])
@@ -132,16 +144,20 @@ def tile_list_maxout_face_margins_kernel(
         thr_all = held("thr_all", [P, S], F32)
         nc.scalar.copy(out=thr_all[:].rearrange("q (p c) -> q p c", c=PACK), in_=thr_ps[:].rearrange("q c p -> q p c"))
 
-        bf10 = held("bf10", [P, PASS * PACK], BF16)
+        bf10 = placed("bf10", [P, PASS * PACK], BF16, R7 + 2048)
         round_w1(raw10, bf10, False)
-        vw = [placed("vw0", [P, S], U32, 1024), held("vw1", [P, S], U32)]
-        nc.vector.tensor_copy(vw[0][:], tabw0[:].bitcast(U32).indirect(idx[:]))
+        vw.append(placed("vw1", [P, S], U32, R5))
         nc.vector.tensor_copy(vw[1][:], tabw1[:].bitcast(U32).indirect(idx[:]))
-        quantize_w1(1, 0, bf10, held("w1w10", [P, PASS], U32, "bf00"), held("w1s10", [P, PASS], U8))
-        tab2w = [load_words(held("tab2w0", [P, T2], I32, "bf10"), tab2_words[0])]
+        quantize_w1(1, 0, bf10, placed("w1w10", [P, PASS], U32, R4), held("w1s10", [P, PASS], U8))
+        tab2w = [load_words(placed("tab2w0", [P, T2], I32, R7 + 4096), tab2_words[0])]
+        bf11 = placed("bf11", [P, PASS * PACK], BF16, R7)
+        round_w1(raw11, bf11, True)
+        tab2w.append(load_words(placed("tab2w1", [P, T2], I32, R1), tab2_words[1]))
+        quantize_w1(1, 1, bf11, held("w1w11", [P, PASS], U32), held("w1s11", [P, PASS], U8))
 
-        h_planes = [held("h_planes0", [P, PACK, S], BF16)]
-        h_bf = [held("h_bf%d" % g, [P, S * PACK], BF16) for g in range(NPASS)]
+        h_planes = [placed("h_planes0", [P, PACK, S], BF16, R7), held("h_planes1", [P, PACK, S], BF16)]
+        h_bf = []
+        hw = []
         hs = [held("hs%d" % g, [P, S], U8) for g in range(NPASS)]
 
         def project_a(g, t, a, a_ps):
@@ -171,8 +187,8 @@ def tile_list_maxout_face_margins_kernel(
             return psum.tile([P, S], F32, name="bank", tag="bank%d" % b)
 
         def take_max(g, t, a_ps, c_ps):
-            a_sb = held("a_sb%d%d" % (g, t), [P, S], F32, "h_planes0" if (g, t) == (1, 0) else "")
-            nc.scalar.activation(out=a_sb[:], in_=a_ps[:], func=ACT.Identity, bias=b1_sb[:, g, t : t + 1])
+            a_sb = held("a_sb%d%d" % (g, t), [P, S], F32)
+            nc.scalar.activation(out=a_sb[:], in_=a_ps[:], func=ACT.Identity, bias=b1_sb[g][:, t : t + 1])
             nc.vector.scalar_tensor_tensor(
                 out=h_planes[g][:, t, :], in0=c_ps[:], scalar=b4_sb[:, g, t : t + 1], in1=a_sb[:],
                 op0=ALU.add, op1=ALU.max,
@@ -188,10 +204,12 @@ def tile_list_maxout_face_margins_kernel(
 
         half = S2 // 2
 
-        def gather_v2(g, u):
+        v2w = {}
+
+        def gather_v2(g, u, dst):
+            v2w.setdefault((g, u), dst)
             nc.vector.tensor_copy(
-                v2w[g][:, u * half : (u + 1) * half],
-                tab2w[g][:].bitcast(U32).indirect(idx2[:, u * half // 16 : (u + 1) * half // 16]),
+                dst[:], tab2w[g][:].bitcast(U32).indirect(idx2[:, u * half // 16 : (u + 1) * half // 16])
             )
 
         a_ps = [bank(t) for t in range(PACK)]
@@ -203,45 +221,38 @@ def tile_list_maxout_face_margins_kernel(
             project_a(0, t, 1, a_ps[t])
             project_c(0, t, 1, c_ps[t])
             take_max(0, t, a_ps[t], c_ps[t])
-        tab2w.append(load_words(held("tab2w1", [P, T2], I32, "a_sb00"), tab2_words[1]))
-        interleave_h(0)
-
-        bf11 = held("bf11", [P, PASS * PACK], BF16, "a_sb03")
-        round_w1(raw11, bf11, True)
-        quantize_w1(1, 1, bf11, held("w1w11", [P, PASS], U32), held("w1s11", [P, PASS], U8))
-        v2s = held("v2s", [P, S2], U8, "a_sb03")
-        nc.vector.tensor_copy(v2s[:], tab2s[:].bitcast(U8).indirect(idx2[:]))
-        h_planes.append(held("h_planes1", [P, PACK, S], BF16, "bf01"))
 
         a_ps = [bank(t) for t in range(PACK)]
         c_ps = [bank(PACK + t) for t in range(PACK)]
         for t in range(PACK):
-            project_a(1, t, 0, a_ps[t])
-            project_c(1, t, 0, c_ps[t])
-            project_c(1, t, 1, c_ps[t])
-        for t in range(PACK):
-            project_a(1, t, 1, a_ps[t])
+            for a in range(NPASS):
+                project_a(1, t, a, a_ps[t])
+            for a in range(NPASS):
+                project_c(1, t, a, c_ps[t])
             take_max(1, t, a_ps[t], c_ps[t])
+        h_bf.append(placed("h_bf0", [P, S * PACK], BF16, R6))
+        interleave_h(0)
+        h_bf.append(placed("h_bf1", [P, S * PACK], BF16, R7))
         interleave_h(1)
 
-        hw = [held("hw0", [P, S], U32, "a_sb13"), held("hw1", [P, S], U32)]
+        v2s = held("v2s", [P, S2], U8, "a_sb13")
+        nc.vector.tensor_copy(v2s[:], tab2s[:].bitcast(U8).indirect(idx2[:]))
+        hw.append(placed("hw0", [P, S], U32, R5 + 2048))
         quantize_h(0)
-        v2w = [held("v2w0", [P, S2], U32, "h_bf0")]
-        gather_v2(0, 0)
-        gather_v2(0, 1)
+        gather_v2(0, 0, placed("v2w00", [P, half], U32, R6))
+        gather_v2(0, 1, placed("v2w01", [P, half], U32, R6 + 2048))
+        hw.append(placed("hw1", [P, S], U32, R7 + 4096))
         quantize_h(1)
-        v2w.append(held("v2w1", [P, S2], U32, "h_bf1"))
-        gather_v2(1, 0)
-        gather_v2(1, 1)
+        gather_v2(1, 0, placed("v2w10", [P, half], U32, R7))
+        gather_v2(1, 1, placed("v2w11", [P, half], U32, R7 + 2048))
 
         y_ps = [bank(i) for i in range(S2 // P)]
 
         def score(i, g):
-            cols = slice(i * P, (i + 1) * P)
             nc.tensor.matmul_mx(
                 out=y_ps[i][:],
-                lhsT=v2w[g][:, cols].bitcast(FP8X4),
-                lhsT_scale=v2s[4 + 4 * g : P, cols],
+                lhsT=v2w[g, i // 4][:, (i % 4) * P : (i % 4 + 1) * P].bitcast(FP8X4),
+                lhsT_scale=v2s[4 + 4 * g : P, i * P : (i + 1) * P],
                 rhs=hw[g][:].bitcast(FP8X4),
                 rhs_scale=hs[g][:],
                 start=(g == 0),
@@ -253,5 +264,11 @@ def tile_list_maxout_face_margins_kernel(
         for i in range(S2 // P):
             score(i, 1)
             y_sb = ring.tile([P, S], F32, name="y_sb", bufs=8)
-            nc.vector.tensor_tensor(out=y_sb[:], in0=y_ps[i][:], in1=thr_all[:], op=ALU.subtract)
-            nc.sync.dma_start(out=out[i * P : (i + 1) * P, :], in_=y_sb[:])
+            if i in (1, 3):
+                y_raw = ring.tile([P, S], F32, name="y_raw", bufs=2)
+                nc.scalar.copy(out=y_raw[:], in_=y_ps[i][:])
+                nc.gpsimd.tensor_tensor(out=y_sb[:], in0=y_raw[:], in1=thr_all[:], op=ALU.subtract)
+                nc.scalar.dma_start(out=out[i * P : (i + 1) * P, :], in_=y_sb[:])
+            else:
+                nc.vector.tensor_tensor(out=y_sb[:], in0=y_ps[i][:], in1=thr_all[:], op=ALU.subtract)
+                nc.sync.dma_start(out=out[i * P : (i + 1) * P, :], in_=y_sb[:])

@@ -68,17 +68,33 @@ def tile_list_maxout_face_margins_kernel(
             w1s.setdefault((g, a), scales)
             nc.vector.quantize_mx(out=words[:].bitcast(FP8X4), scales=scales[:], in_=src[:])
 
-        R1, R2, R3, R4, R5, R6, R7 = 0, 16896, 27136, 35328, 43520, 49664, 53760
-        tabs = held("tabs", [P, NPASS * T // 4], I32)
-        nc.vector.memset(tabs[:], 0)
+        RAW00, W4W_RAW, RAW01 = 0, 7168, 10240
+        TABW0, TABS, W4S, RAW10 = 18432, 25600, 26624, 28672
+        TABW1, W4S_RAW, V2S, RAW11 = 36864, 44544, 45056, 46080
+        TAB2W0, TAB2S, VW0, W1S0, TAB2W1 = 54272, 70144, 70656, 72704, 73728
+        STAGE1, STAGE0 = 90112, 94208
 
-        w4w_raw = [placed("w4w_raw0", [P, H // 2], I32, R1), placed("w4w_raw1", [P, H // 2], I32, R2 + 1536)]
-        for a in range(NPASS):
-            nc.sync.dma_start(out=w4w_raw[a][:], in_=w4_words.bitcast(I32)[a])
+        tab2s = placed("tab2s", [P, T2 // 4], I32, TAB2S)
+        tabs = placed("tabs", [P, NPASS * T // 4], I32, TABS)
+        w4s_raw = placed("w4s_raw", [P, NPASS * H // 4], I32, W4S_RAW)
+        nc.gpsimd.memset(tab2s[:], 0)
+        nc.vector.memset(tabs[:], 0)
+        nc.vector.memset(w4s_raw[:], 0)
+
+        w4w_raw = placed("w4w_raw", [P, NPASS, H // 2], I32, W4W_RAW)
+        nc.sync.dma_start(out=w4w_raw[:], in_=w4_words.bitcast(I32).rearrange("a p n -> p a n"))
         nc.sync.dma_start(idx[:], offs)
         nc.sync.dma_start(idx2[:], offs2)
-        raw00 = load_w1(0, 0, placed("raw00", [P, PACK, PASS], F32, R3))
-        b1_sb = [held("b1_sb0", [P, PACK], F32), placed("b1_sb1", [P, PACK], F32, R6)]
+        for r in range(4):
+            for dst, src in ((tabs, tab_scales), (w4s_raw, w4_scales)):
+                nc.sync.dma_start(
+                    out=dst[r:P:32, :].rearrange("q (a n) -> q a n", a=NPASS),
+                    in_=src.bitcast(I32)[:, r:16:4, :].rearrange("a q n -> q a n"),
+                )
+            for a in range(NPASS):
+                nc.sync.dma_start(out=tab2s[4 + 4 * a + r : P : 32, :], in_=tab2_scales.bitcast(I32)[a, r:16:4, :])
+
+        b1_sb = [held("b1_sb0", [P, PACK], F32), placed("b1_sb1", [P, PACK], F32, STAGE0)]
         b4_sb = held("b4_sb", [P, NPASS, PACK], F32)
         thr_sb = held("thr_sb", [P, PACK], F32)
         b1_rows = b1.rearrange("(g p t) -> g p t", g=NPASS, t=PACK)
@@ -86,55 +102,6 @@ def tile_list_maxout_face_margins_kernel(
         nc.gpsimd.dma_start(out=b1_sb[0][:], in_=b1_rows[0])
         nc.gpsimd.dma_start(out=b4_sb[:], in_=b4.rearrange("(g p t) -> p g t", g=NPASS, t=PACK))
         nc.gpsimd.dma_start(out=b1_sb[1][:], in_=b1_rows[1])
-
-        def load_scales(dst, src):
-            for r in range(4):
-                nc.sync.dma_start(
-                    out=dst[r:P:32, :].rearrange("q (a n) -> q a n", a=NPASS),
-                    in_=src.bitcast(I32)[:, r:16:4, :].rearrange("a q n -> q a n"),
-                )
-
-        load_scales(tabs, tab_scales)
-
-        w4w = held("w4w", [P, NPASS, 2 * H], U8)
-        for a in range(NPASS):
-            nc.vector.tensor_copy(
-                out=w4w[:, a, :].bitcast(U16).rearrange("p (g t m) -> p g t m", g=NPASS, t=PACK),
-                in_=w4w_raw[a][:].bitcast(U16).rearrange("p (g m t) -> p g t m", g=NPASS, t=PACK),
-            )
-        raw01 = load_w1(0, 1, placed("raw01", [P, PACK, PASS], F32, R1))
-        tabw0 = load_words(placed("tabw0", [P, T], I32, R2 + 2048), tab_words[0])
-        w4s_raw = placed("w4s_raw", [P, NPASS * H // 4], I32, R2)
-        nc.vector.memset(w4s_raw[:], 0)
-        load_scales(w4s_raw, w4_scales)
-
-        vs = [held("vs%d" % a, [P, S], U8) for a in range(NPASS)]
-        for a in range(NPASS):
-            nc.vector.tensor_copy(vs[a][:], tabs[:].bitcast(U8)[:, a * T : (a + 1) * T].indirect(idx[:]))
-
-        bf00 = placed("bf00", [P, PASS * PACK], BF16, R4)
-        round_w1(raw00, bf00, False)
-        raw10 = load_w1(1, 0, placed("raw10", [P, PACK, PASS], F32, R3))
-        quantize_w1(0, 0, bf00, held("w1w00", [P, PASS], U32), held("w1s00", [P, PASS], U8))
-        tabw1 = load_words(placed("tabw1", [P, T], I32, R4), tab_words[1])
-
-        vw = [held("vw0", [P, S], U32, "tabs")]
-        nc.vector.tensor_copy(vw[0][:], tabw0[:].bitcast(U32).indirect(idx[:]))
-        w4s = placed("w4s", [P, NPASS, H], U8, R2 + 2048)
-        nc.vector.tensor_copy(
-            out=w4s[:].rearrange("p a (g t m) -> p (a g) t m", g=NPASS, t=PACK),
-            in_=w4s_raw[:].bitcast(U8).rearrange("p (u m t) -> p u t m", u=NPASS * NPASS, t=PACK),
-        )
-
-        bf01 = placed("bf01", [P, PASS * PACK], BF16, R5)
-        round_w1(raw01, bf01, False)
-        raw11 = load_w1(1, 1, placed("raw11", [P, PACK, PASS], F32, R1))
-        quantize_w1(0, 1, bf01, held("w1w01", [P, PASS], U32), placed("w1s01", [P, PASS], U8, R2))
-        tab2s = placed("tab2s", [P, T2 // 4], I32, R5 + 2048)
-        nc.gpsimd.memset(tab2s[:], 0)
-        for r in range(4):
-            for a in range(NPASS):
-                nc.sync.dma_start(out=tab2s[4 + 4 * a + r : P : 32, :], in_=tab2_scales.bitcast(I32)[a, r:16:4, :])
 
         ident = held("ident", [P, P], F32)
         make_identity(nc, ident[:])
@@ -144,18 +111,55 @@ def tile_list_maxout_face_margins_kernel(
         thr_all = held("thr_all", [P, S], F32)
         nc.scalar.copy(out=thr_all[:].rearrange("q (p c) -> q p c", c=PACK), in_=thr_ps[:].rearrange("q c p -> q p c"))
 
-        bf10 = placed("bf10", [P, PASS * PACK], BF16, R7 + 2048)
+        w4w = held("w4w", [P, NPASS, 2 * H], U8)
+        for a in range(NPASS):
+            nc.vector.tensor_copy(
+                out=w4w[:, a, :].bitcast(U16).rearrange("p (g t m) -> p g t m", g=NPASS, t=PACK),
+                in_=w4w_raw[:, a, :].bitcast(U16).rearrange("p (g m t) -> p g t m", g=NPASS, t=PACK),
+            )
+        raw00 = load_w1(0, 0, placed("raw00", [P, PACK, PASS], F32, RAW00))
+        raw01 = load_w1(0, 1, placed("raw01", [P, PACK, PASS], F32, RAW01))
+
+        vs = [held("vs%d" % a, [P, S], U8) for a in range(NPASS)]
+        for a in range(NPASS):
+            nc.vector.tensor_copy(vs[a][:], tabs[:].bitcast(U8)[:, a * T : (a + 1) * T].indirect(idx[:]))
+        tabw0 = load_words(placed("tabw0", [P, T], I32, TABW0), tab_words[0])
+        raw10 = load_w1(1, 0, placed("raw10", [P, PACK, PASS], F32, RAW10))
+
+        w4s = placed("w4s", [P, NPASS, H], U8, W4S)
+        nc.vector.tensor_copy(
+            out=w4s[:].rearrange("p a (g t m) -> p (a g) t m", g=NPASS, t=PACK),
+            in_=w4s_raw[:].bitcast(U8).rearrange("p (u m t) -> p u t m", u=NPASS * NPASS, t=PACK),
+        )
+        tabw1 = load_words(placed("tabw1", [P, T], I32, TABW1), tab_words[1])
+        raw11 = load_w1(1, 1, placed("raw11", [P, PACK, PASS], F32, RAW11))
+
+        v2s = placed("v2s", [P, S2], U8, V2S)
+        nc.vector.tensor_copy(v2s[:], tab2s[:].bitcast(U8).indirect(idx2[:]))
+        tab2w = [
+            load_words(placed("tab2w0", [P, T2], I32, TAB2W0), tab2_words[0]),
+            load_words(placed("tab2w1", [P, T2], I32, TAB2W1), tab2_words[1]),
+        ]
+
+        bf00 = held("bf00", [P, PASS * PACK], BF16)
+        round_w1(raw00, bf00, False)
+        quantize_w1(0, 0, bf00, held("w1w00", [P, PASS], U32), placed("w1s00", [P, PASS], U8, W1S0))
+        vw = [placed("vw0", [P, S], U32, VW0)]
+        nc.vector.tensor_copy(vw[0][:], tabw0[:].bitcast(U32).indirect(idx[:]))
+        bf01 = held("bf01", [P, PASS * PACK], BF16)
+        round_w1(raw01, bf01, False)
+        quantize_w1(0, 1, bf01, held("w1w01", [P, PASS], U32), placed("w1s01", [P, PASS], U8, W1S0 + PASS))
+
+        bf10 = placed("bf10", [P, PASS * PACK], BF16, STAGE1)
         round_w1(raw10, bf10, False)
-        vw.append(placed("vw1", [P, S], U32, R5))
+        vw.append(held("vw1", [P, S], U32, "bf01"))
         nc.vector.tensor_copy(vw[1][:], tabw1[:].bitcast(U32).indirect(idx[:]))
-        quantize_w1(1, 0, bf10, placed("w1w10", [P, PASS], U32, R4), held("w1s10", [P, PASS], U8))
-        tab2w = [load_words(placed("tab2w0", [P, T2], I32, R7 + 4096), tab2_words[0])]
-        bf11 = placed("bf11", [P, PASS * PACK], BF16, R7)
+        quantize_w1(1, 0, bf10, placed("w1w10", [P, PASS], U32, TABW1), held("w1s10", [P, PASS], U8))
+        bf11 = placed("bf11", [P, PASS * PACK], BF16, STAGE1)
         round_w1(raw11, bf11, True)
-        tab2w.append(load_words(placed("tab2w1", [P, T2], I32, R1), tab2_words[1]))
         quantize_w1(1, 1, bf11, held("w1w11", [P, PASS], U32), held("w1s11", [P, PASS], U8))
 
-        h_planes = [placed("h_planes0", [P, PACK, S], BF16, R7), held("h_planes1", [P, PACK, S], BF16)]
+        h_planes = [placed("h_planes0", [P, PACK, S], BF16, STAGE1), held("h_planes1", [P, PACK, S], BF16)]
         h_bf = []
         hw = []
         hs = [held("hs%d" % g, [P, S], U8) for g in range(NPASS)]
@@ -230,21 +234,19 @@ def tile_list_maxout_face_margins_kernel(
             for a in range(NPASS):
                 project_c(1, t, a, c_ps[t])
             take_max(1, t, a_ps[t], c_ps[t])
-        h_bf.append(placed("h_bf0", [P, S * PACK], BF16, R6))
+        h_bf.append(placed("h_bf0", [P, S * PACK], BF16, STAGE0))
         interleave_h(0)
-        h_bf.append(placed("h_bf1", [P, S * PACK], BF16, R7))
+        h_bf.append(placed("h_bf1", [P, S * PACK], BF16, STAGE1))
         interleave_h(1)
 
-        v2s = held("v2s", [P, S2], U8, "a_sb13")
-        nc.vector.tensor_copy(v2s[:], tab2s[:].bitcast(U8).indirect(idx2[:]))
-        hw.append(placed("hw0", [P, S], U32, R5 + 2048))
+        gather_v2(0, 0, held("v2w00", [P, half], U32, "a_sb13"))
+        hw.append(held("hw0", [P, S], U32))
         quantize_h(0)
-        gather_v2(0, 0, placed("v2w00", [P, half], U32, R6))
-        gather_v2(0, 1, placed("v2w01", [P, half], U32, R6 + 2048))
-        hw.append(placed("hw1", [P, S], U32, R7 + 4096))
+        gather_v2(0, 1, placed("v2w01", [P, half], U32, STAGE0))
+        hw.append(placed("hw1", [P, S], U32, TAB2W0))
         quantize_h(1)
-        gather_v2(1, 0, placed("v2w10", [P, half], U32, R7))
-        gather_v2(1, 1, placed("v2w11", [P, half], U32, R7 + 2048))
+        gather_v2(1, 0, placed("v2w10", [P, half], U32, STAGE1))
+        gather_v2(1, 1, placed("v2w11", [P, half], U32, STAGE1 + 2048))
 
         y_ps = [bank(i) for i in range(S2 // P)]
 

@@ -21,6 +21,21 @@ P = 128
 PACK = 4
 PASS = P * PACK
 NPASS = 2
+QUADS = 4
+RUN = 4
+OUT_TILES = S2 // P
+HALF = S2 // 2
+HALF_TILES = HALF // P
+GPSIMD_TILES = (1, 3)
+
+W4_WORDS_RAW = 0
+W1_RAW = ((4096, 12288), (28672, 45056))
+TAB_WORDS = (20480, 36864)
+TAB2_WORDS = (53248, 69632)
+TAB_SCALES, W4_SCALES_RAW, TAB2_SCALES = 86016, 90112, 92160
+STAGE_H1, STAGE_H0 = 96256, 100352
+W4_SCALES, V2_SCALES = TAB_SCALES, W4_SCALES_RAW
+V_WORDS0, W1_SCALES00 = TAB2_SCALES, TAB2_SCALES + 4 * S
 
 
 def tile_list_maxout_face_margins_kernel(
@@ -29,72 +44,71 @@ def tile_list_maxout_face_margins_kernel(
     nc = tc.nc
     with ExitStack() as ctx:
         keep = ctx.enter_context(tc.tile_pool(name="keep", bufs=1))
-        ring = ctx.enter_context(tc.tile_pool(name="ring", bufs=4))
+        outs = ctx.enter_context(tc.tile_pool(name="outs", bufs=OUT_TILES))
         psum = ctx.enter_context(tc.psum_pool(name="psum", bufs=1))
         reuse = ctx.enter_context(tc.tile_pool(name="reuse", bufs=1))
 
         def placed(name, shape, dtype, offset):
             return reuse.tile(shape, dtype, name=name, offset=offset, align_bytes=64)
 
+        def held(name, shape, dtype, follows=""):
+            return keep.tile(shape, dtype, name=name, tag=follows or name, align_bytes=64)
 
-        def held(name, shape, dtype, tag=""):
-            return keep.tile(shape, dtype, name=name, tag=tag or name, align_bytes=64)
+        def bank(b):
+            return psum.tile([P, S], F32, name="bank", tag="bank%d" % b)
 
         idx = keep.tile([P, S // 16], U16, name="idx")
         idx2 = keep.tile([P, S2 // 16], U16, name="idx2")
 
-        def load_w1(g, a, raw):
+        def load_w1(g, a):
+            raw = placed("w1_raw%d%d" % (g, a), [P, PACK, PASS], F32, W1_RAW[g][a])
             rows = w1[a * PASS : (a + 1) * PASS, g * PASS : (g + 1) * PASS]
             nc.sync.dma_start(out=raw[:], in_=rows.rearrange("(p j) c -> p j c", j=PACK))
             return raw
 
         def load_words(dst, words):
-            nc.sync.dma_start(out=dst[:], in_=words.rearrange("p t i -> p (t i)").bitcast(I32))
+            nc.sync.dma_start(out=dst[:], in_=words.rearrange("p col j -> p (col j)").bitcast(I32))
             return dst
 
-        def round_w1(raw, dst, on_vector):
+        def round_w1(raw, dst, on_scalar):
             grouped = dst[:].rearrange("p (t m j) -> p m t j", t=PACK, j=PACK)
             src = raw[:].rearrange("p j (m t) -> p m t j", t=PACK)
-            if on_vector:
-                nc.vector.tensor_copy(out=grouped, in_=src)
-            else:
-                nc.scalar.copy(out=grouped, in_=src)
+            if on_scalar > 0:
+                nc.scalar.copy(out=grouped[:, :on_scalar], in_=src[:, :on_scalar])
+            if on_scalar < P:
+                nc.vector.tensor_copy(out=grouped[:, on_scalar:], in_=src[:, on_scalar:])
 
-        w1w = {}
-        w1s = {}
+        w1_codes = {}
+        w1_scales = {}
 
-        def quantize_w1(g, a, src, words, scales):
-            w1w.setdefault((g, a), words)
-            w1s.setdefault((g, a), scales)
-            nc.vector.quantize_mx(out=words[:].bitcast(FP8X4), scales=scales[:], in_=src[:])
+        def quantize_w1(g, a, src, codes, scales):
+            w1_codes.setdefault((g, a), codes)
+            w1_scales.setdefault((g, a), scales)
+            nc.vector.quantize_mx(out=codes[:].bitcast(FP8X4), scales=scales[:], in_=src[:])
 
-        RAW00, W4W_RAW, RAW01 = 0, 7168, 10240
-        TABW0, TABS, W4S, RAW10 = 18432, 25600, 26624, 28672
-        TABW1, W4S_RAW, V2S, RAW11 = 36864, 44544, 45056, 46080
-        TAB2W0, TAB2S, VW0, W1S0, TAB2W1 = 54272, 70144, 70656, 72704, 73728
-        STAGE1, STAGE0 = 90112, 94208
-
-        tab2s = placed("tab2s", [P, T2 // 4], I32, TAB2S)
-        tabs = placed("tabs", [P, NPASS * T // 4], I32, TABS)
-        w4s_raw = placed("w4s_raw", [P, NPASS * H // 4], I32, W4S_RAW)
+        tab2s = placed("tab2s", [P, T2 // 4], I32, TAB2_SCALES)
+        tabs = placed("tabs", [P, NPASS * T // 4], I32, TAB_SCALES)
+        w4s_raw = placed("w4s_raw", [P, NPASS * H // 4], I32, W4_SCALES_RAW)
         nc.gpsimd.memset(tab2s[:], 0)
         nc.vector.memset(tabs[:], 0)
         nc.vector.memset(w4s_raw[:], 0)
 
-        w4w_raw = placed("w4w_raw", [P, NPASS, H // 2], I32, W4W_RAW)
-        nc.sync.dma_start(out=w4w_raw[:], in_=w4_words.bitcast(I32).rearrange("a p n -> p a n"))
+        w4_extent = placed("w4_extent", [P, TAB_SCALES // 4], I32, W4_WORDS_RAW)
+        w4w_raw = w4_extent[:, 0:H].rearrange("p (a col) -> p a col", a=NPASS)
+        nc.sync.dma_start(out=w4w_raw, in_=w4_words.bitcast(I32).rearrange("a p col -> p a col"))
         nc.sync.dma_start(idx[:], offs)
         nc.sync.dma_start(idx2[:], offs2)
-        for r in range(4):
-            for dst, src in ((tabs, tab_scales), (w4s_raw, w4_scales)):
-                nc.sync.dma_start(
-                    out=dst[r:P:32, :].rearrange("q (a n) -> q a n", a=NPASS),
-                    in_=src.bitcast(I32)[:, r:16:4, :].rearrange("a q n -> q a n"),
-                )
-            for a in range(NPASS):
-                nc.sync.dma_start(out=tab2s[4 + 4 * a + r : P : 32, :], in_=tab2_scales.bitcast(I32)[a, r:16:4, :])
+        for n in range(2 * QUADS):
+            dst, src = (tabs, tab_scales) if n < QUADS else (w4s_raw, w4_scales)
+            r = n % QUADS
+            nc.sync.dma_start(
+                out=dst[r:P:32, :].rearrange("quad (a col) -> quad a col", a=NPASS),
+                in_=src.bitcast(I32)[:, r:16:4, :].rearrange("a quad col -> quad a col"),
+            )
+            g, r2 = n % NPASS, n // NPASS
+            nc.sync.dma_start(out=tab2s[4 + 4 * g + r2 : P : 32, :], in_=tab2_scales.bitcast(I32)[g, r2:16:4, :])
 
-        b1_sb = [held("b1_sb0", [P, PACK], F32), placed("b1_sb1", [P, PACK], F32, STAGE0)]
+        b1_sb = [held("b1_sb0", [P, PACK], F32), placed("b1_sb1", [P, PACK], F32, STAGE_H0)]
         b4_sb = held("b4_sb", [P, NPASS, PACK], F32)
         thr_sb = held("thr_sb", [P, PACK], F32)
         b1_rows = b1.rearrange("(g p t) -> g p t", g=NPASS, t=PACK)
@@ -105,11 +119,13 @@ def tile_list_maxout_face_margins_kernel(
 
         ident = held("ident", [P, P], F32)
         make_identity(nc, ident[:])
-        thr_ps = psum.tile([P, PACK, P], F32, name="thr_ps", tag="bank7")
+        thr_ps = psum.tile([P, PACK, P], F32, name="thr_ps", tag="bank%d" % (OUT_TILES - 1))
         for c in range(PACK):
             nc.tensor.transpose(thr_ps[:, c, :], thr_sb[:, c : c + 1].to_broadcast([P, P]), ident[:])
         thr_all = held("thr_all", [P, S], F32)
-        nc.scalar.copy(out=thr_all[:].rearrange("q (p c) -> q p c", c=PACK), in_=thr_ps[:].rearrange("q c p -> q p c"))
+        nc.scalar.copy(
+            out=thr_all[:].rearrange("row (p c) -> row p c", c=PACK), in_=thr_ps[:].rearrange("row c p -> row p c")
+        )
 
         w4w = held("w4w", [P, NPASS, 2 * H], U8)
         for a in range(NPASS):
@@ -117,58 +133,55 @@ def tile_list_maxout_face_margins_kernel(
                 out=w4w[:, a, :].bitcast(U16).rearrange("p (g t m) -> p g t m", g=NPASS, t=PACK),
                 in_=w4w_raw[:, a, :].bitcast(U16).rearrange("p (g m t) -> p g t m", g=NPASS, t=PACK),
             )
-        raw00 = load_w1(0, 0, placed("raw00", [P, PACK, PASS], F32, RAW00))
-        raw01 = load_w1(0, 1, placed("raw01", [P, PACK, PASS], F32, RAW01))
+        w1_raw00 = load_w1(0, 0)
+        w1_raw01 = load_w1(0, 1)
 
         vs = [held("vs%d" % a, [P, S], U8) for a in range(NPASS)]
         for a in range(NPASS):
             nc.vector.tensor_copy(vs[a][:], tabs[:].bitcast(U8)[:, a * T : (a + 1) * T].indirect(idx[:]))
-        tabw0 = load_words(placed("tabw0", [P, T], I32, TABW0), tab_words[0])
-        raw10 = load_w1(1, 0, placed("raw10", [P, PACK, PASS], F32, RAW10))
+        tabw0 = load_words(placed("tabw0", [P, T], I32, TAB_WORDS[0]), tab_words[0])
+        w1_raw10 = load_w1(1, 0)
 
-        w4s = placed("w4s", [P, NPASS, H], U8, W4S)
+        w4s = placed("w4s", [P, NPASS, H], U8, W4_SCALES)
         nc.vector.tensor_copy(
             out=w4s[:].rearrange("p a (g t m) -> p (a g) t m", g=NPASS, t=PACK),
-            in_=w4s_raw[:].bitcast(U8).rearrange("p (u m t) -> p u t m", u=NPASS * NPASS, t=PACK),
+            in_=w4s_raw[:].bitcast(U8).rearrange("p (ag m t) -> p ag t m", ag=NPASS * NPASS, t=PACK),
         )
-        tabw1 = load_words(placed("tabw1", [P, T], I32, TABW1), tab_words[1])
-        raw11 = load_w1(1, 1, placed("raw11", [P, PACK, PASS], F32, RAW11))
+        tabw1 = load_words(placed("tabw1", [P, T], I32, TAB_WORDS[1]), tab_words[1])
+        w1_raw11 = load_w1(1, 1)
 
-        v2s = placed("v2s", [P, S2], U8, V2S)
+        v2s = placed("v2s", [P, S2], U8, V2_SCALES)
         nc.vector.tensor_copy(v2s[:], tab2s[:].bitcast(U8).indirect(idx2[:]))
-        tab2w = [
-            load_words(placed("tab2w0", [P, T2], I32, TAB2W0), tab2_words[0]),
-            load_words(placed("tab2w1", [P, T2], I32, TAB2W1), tab2_words[1]),
-        ]
+        tab2w = [load_words(placed("tab2w%d" % g, [P, T2], I32, TAB2_WORDS[g]), tab2_words[g]) for g in range(NPASS)]
 
-        bf00 = held("bf00", [P, PASS * PACK], BF16)
-        round_w1(raw00, bf00, False)
-        quantize_w1(0, 0, bf00, held("w1w00", [P, PASS], U32), placed("w1s00", [P, PASS], U8, W1S0))
-        vw = [placed("vw0", [P, S], U32, VW0)]
+        w1_bf00 = held("w1_bf00", [P, PASS * PACK], BF16)
+        round_w1(w1_raw00, w1_bf00, P)
+        quantize_w1(0, 0, w1_bf00, held("w1_codes00", [P, PASS], U32), placed("w1_scales00", [P, PASS], U8, W1_SCALES00))
+        vw = [placed("vw0", [P, S], U32, V_WORDS0)]
         nc.vector.tensor_copy(vw[0][:], tabw0[:].bitcast(U32).indirect(idx[:]))
-        bf01 = held("bf01", [P, PASS * PACK], BF16)
-        round_w1(raw01, bf01, False)
-        quantize_w1(0, 1, bf01, held("w1w01", [P, PASS], U32), placed("w1s01", [P, PASS], U8, W1S0 + PASS))
+        w1_bf01 = held("w1_bf01", [P, PASS * PACK], BF16, "w1_bf00")
+        round_w1(w1_raw01, w1_bf01, P // 2)
+        quantize_w1(0, 1, w1_bf01, held("w1_codes01", [P, PASS], U32), held("w1_scales01", [P, PASS], U8))
 
-        bf10 = placed("bf10", [P, PASS * PACK], BF16, STAGE1)
-        round_w1(raw10, bf10, False)
-        vw.append(held("vw1", [P, S], U32, "bf01"))
+        w1_bf10 = placed("w1_bf10", [P, PASS * PACK], BF16, STAGE_H1)
+        round_w1(w1_raw10, w1_bf10, P)
+        vw.append(held("vw1", [P, S], U32, "w1_bf00"))
         nc.vector.tensor_copy(vw[1][:], tabw1[:].bitcast(U32).indirect(idx[:]))
-        quantize_w1(1, 0, bf10, placed("w1w10", [P, PASS], U32, TABW1), held("w1s10", [P, PASS], U8))
-        bf11 = placed("bf11", [P, PASS * PACK], BF16, STAGE1)
-        round_w1(raw11, bf11, True)
-        quantize_w1(1, 1, bf11, held("w1w11", [P, PASS], U32), held("w1s11", [P, PASS], U8))
+        quantize_w1(1, 0, w1_bf10, placed("w1_codes10", [P, PASS], U32, TAB_WORDS[1]), held("w1_scales10", [P, PASS], U8))
+        w1_bf11 = placed("w1_bf11", [P, PASS * PACK], BF16, STAGE_H1)
+        round_w1(w1_raw11, w1_bf11, 0)
+        quantize_w1(1, 1, w1_bf11, held("w1_codes11", [P, PASS], U32), held("w1_scales11", [P, PASS], U8))
 
-        h_planes = [placed("h_planes0", [P, PACK, S], BF16, STAGE1), held("h_planes1", [P, PACK, S], BF16)]
+        h_planes = [placed("h_planes0", [P, PACK, S], BF16, STAGE_H1), held("h_planes1", [P, PACK, S], BF16)]
         h_bf = []
-        hw = []
-        hs = [held("hs%d" % g, [P, S], U8) for g in range(NPASS)]
+        h_codes = []
+        h_scales = [held("h_scales%d" % g, [P, S], U8) for g in range(NPASS)]
 
         def project_a(g, t, a, a_ps):
             nc.tensor.matmul_mx(
                 out=a_ps[:],
-                lhsT=w1w[g, a][:, t * P : (t + 1) * P].bitcast(FP8X4),
-                lhsT_scale=w1s[g, a][:, t * P : (t + 1) * P],
+                lhsT=w1_codes[g, a][:, t * P : (t + 1) * P].bitcast(FP8X4),
+                lhsT_scale=w1_scales[g, a][:, t * P : (t + 1) * P],
                 rhs=vw[a][:].bitcast(FP8X4),
                 rhs_scale=vs[a][:],
                 start=(a == 0),
@@ -187,33 +200,32 @@ def tile_list_maxout_face_margins_kernel(
                 stop=(a == NPASS - 1),
             )
 
-        def bank(b):
-            return psum.tile([P, S], F32, name="bank", tag="bank%d" % b)
-
         def take_max(g, t, a_ps, c_ps):
             a_sb = held("a_sb%d%d" % (g, t), [P, S], F32)
             nc.scalar.activation(out=a_sb[:], in_=a_ps[:], func=ACT.Identity, bias=b1_sb[g][:, t : t + 1])
             nc.vector.scalar_tensor_tensor(
-                out=h_planes[g][:, t, :], in0=c_ps[:], scalar=b4_sb[:, g, t : t + 1], in1=a_sb[:],
-                op0=ALU.add, op1=ALU.max,
+                out=h_planes[g][:, t, :],
+                in0=c_ps[:],
+                scalar=b4_sb[:, g, t : t + 1],
+                in1=a_sb[:],
+                op0=ALU.add,
+                op1=ALU.max,
             )
 
         def interleave_h(g):
-            dst = h_bf[g][:].rearrange("p (c i t) -> p c t i", i=4, t=PACK)
-            src = h_planes[g][:].rearrange("p t (c i) -> p c t i", i=4)
+            dst = h_bf[g][:].rearrange("p (c i t) -> p c t i", i=RUN, t=PACK)
+            src = h_planes[g][:].rearrange("p t (c i) -> p c t i", i=RUN)
             nc.scalar.copy(out=dst, in_=src)
 
         def quantize_h(g):
-            nc.vector.quantize_mx(out=hw[g][:].bitcast(FP8X4), scales=hs[g][:], in_=h_bf[g][:])
-
-        half = S2 // 2
+            nc.vector.quantize_mx(out=h_codes[g][:].bitcast(FP8X4), scales=h_scales[g][:], in_=h_bf[g][:])
 
         v2w = {}
 
-        def gather_v2(g, u, dst):
-            v2w.setdefault((g, u), dst)
+        def gather_v2(g, half, dst):
+            v2w.setdefault((g, half), dst)
             nc.vector.tensor_copy(
-                dst[:], tab2w[g][:].bitcast(U32).indirect(idx2[:, u * half // 16 : (u + 1) * half // 16])
+                dst[:], tab2w[g][:].bitcast(U32).indirect(idx2[:, half * HALF // 16 : (half + 1) * HALF // 16])
             )
 
         a_ps = [bank(t) for t in range(PACK)]
@@ -234,40 +246,42 @@ def tile_list_maxout_face_margins_kernel(
             for a in range(NPASS):
                 project_c(1, t, a, c_ps[t])
             take_max(1, t, a_ps[t], c_ps[t])
-        h_bf.append(placed("h_bf0", [P, S * PACK], BF16, STAGE0))
+
+        h_bf.append(placed("h_bf0", [P, S * PACK], BF16, STAGE_H0))
         interleave_h(0)
-        h_bf.append(placed("h_bf1", [P, S * PACK], BF16, STAGE1))
+        h_bf.append(placed("h_bf1", [P, S * PACK], BF16, STAGE_H1))
         interleave_h(1)
 
-        gather_v2(0, 0, held("v2w00", [P, half], U32, "a_sb13"))
-        hw.append(held("hw0", [P, S], U32))
+        gather_v2(0, 0, held("v2w00", [P, HALF], U32, "a_sb13"))
+        h_codes.append(held("h_codes0", [P, S], U32))
         quantize_h(0)
-        gather_v2(0, 1, placed("v2w01", [P, half], U32, STAGE0))
-        hw.append(placed("hw1", [P, S], U32, TAB2W0))
+        gather_v2(0, 1, placed("v2w01", [P, HALF], U32, STAGE_H0))
+        h_codes.append(placed("h_codes1", [P, S], U32, TAB2_WORDS[0]))
         quantize_h(1)
-        gather_v2(1, 0, placed("v2w10", [P, half], U32, STAGE1))
-        gather_v2(1, 1, placed("v2w11", [P, half], U32, STAGE1 + 2048))
+        gather_v2(1, 0, placed("v2w10", [P, HALF], U32, STAGE_H1))
+        gather_v2(1, 1, placed("v2w11", [P, HALF], U32, STAGE_H1 + 4 * HALF))
 
-        y_ps = [bank(i) for i in range(S2 // P)]
+        y_ps = [bank(i) for i in range(OUT_TILES)]
 
         def score(i, g):
+            col = (i % HALF_TILES) * P
             nc.tensor.matmul_mx(
                 out=y_ps[i][:],
-                lhsT=v2w[g, i // 4][:, (i % 4) * P : (i % 4 + 1) * P].bitcast(FP8X4),
+                lhsT=v2w[g, i // HALF_TILES][:, col : col + P].bitcast(FP8X4),
                 lhsT_scale=v2s[4 + 4 * g : P, i * P : (i + 1) * P],
-                rhs=hw[g][:].bitcast(FP8X4),
-                rhs_scale=hs[g][:],
+                rhs=h_codes[g][:].bitcast(FP8X4),
+                rhs_scale=h_scales[g][:],
                 start=(g == 0),
                 stop=(g == NPASS - 1),
             )
 
-        for i in range(S2 // P):
+        for i in range(OUT_TILES):
             score(i, 0)
-        for i in range(S2 // P):
+        for i in range(OUT_TILES):
             score(i, 1)
-            y_sb = ring.tile([P, S], F32, name="y_sb", bufs=8)
-            if i in (1, 3):
-                y_raw = ring.tile([P, S], F32, name="y_raw", bufs=2)
+            y_sb = outs.tile([P, S], F32, name="y_sb")
+            if i in GPSIMD_TILES:
+                y_raw = outs.tile([P, S], F32, name="y_raw", bufs=len(GPSIMD_TILES))
                 nc.scalar.copy(out=y_raw[:], in_=y_ps[i][:])
                 nc.gpsimd.tensor_tensor(out=y_sb[:], in0=y_raw[:], in1=thr_all[:], op=ALU.subtract)
                 nc.scalar.dma_start(out=out[i * P : (i + 1) * P, :], in_=y_sb[:])

@@ -28,14 +28,14 @@ HALF = S2 // 2
 HALF_TILES = HALF // P
 GPSIMD_TILES = (1, 3)
 
-W4_WORDS_RAW = 0
+W4_WORDS_RAW = 104448
 W1_RAW = ((4096, 12288), (28672, 45056))
 TAB_WORDS = (20480, 36864)
 TAB2_WORDS = (53248, 69632)
-TAB_SCALES, W4_SCALES_RAW, TAB2_SCALES = 86016, 90112, 92160
+TAB2_SCALES, TAB_SCALES, W4_SCALES_RAW = 86016, 90112, 94208
 STAGE_H1, STAGE_H0 = 96256, 100352
 W4_SCALES, V2_SCALES = TAB_SCALES, W4_SCALES_RAW
-V_WORDS0, W1_SCALES00 = TAB2_SCALES, TAB2_SCALES + 4 * S
+V_WORDS0, W1_SCALES00 = W4_SCALES_RAW - 3 * S, W4_SCALES_RAW + 2 * S
 
 
 def tile_list_maxout_face_margins_kernel(
@@ -86,39 +86,48 @@ def tile_list_maxout_face_margins_kernel(
             w1_scales.setdefault((g, a), scales)
             nc.vector.quantize_mx(out=codes[:].bitcast(FP8X4), scales=scales[:], in_=src[:])
 
-        tab2s = placed("tab2s", [P, T2 // 4], I32, TAB2_SCALES)
         tabs = placed("tabs", [P, NPASS * T // 4], I32, TAB_SCALES)
         w4s_raw = placed("w4s_raw", [P, NPASS * H // 4], I32, W4_SCALES_RAW)
-        nc.gpsimd.memset(tab2s[:], 0)
+        v2s = held("v2s", [P, S2 // 4], I32)
         nc.vector.memset(tabs[:], 0)
-        nc.vector.memset(w4s_raw[:], 0)
+        gate = placed("gate", [P, TAB_SCALES // 4], I32, 0)
+        nc.vector.memset(gate[:, 0 : NPASS * H // 4], 0)
+        nc.vector.tensor_copy(out=w4s_raw[:], in_=gate[:, 0 : NPASS * H // 4])
+        tab2s = placed("tab2s", [P, T2 // 4], I32, TAB2_SCALES)
+        nc.vector.memset(tab2s[32:64, :], 0)
+        nc.vector.memset(tab2s[64:P, :], 0)
 
-        w4_extent = placed("w4_extent", [P, TAB_SCALES // 4], I32, W4_WORDS_RAW)
-        w4w_raw = w4_extent[:, 0:H].rearrange("p (a col) -> p a col", a=NPASS)
-        nc.sync.dma_start(out=w4w_raw, in_=w4_words.bitcast(I32).rearrange("a p col -> p a col"))
+        w4w_raw = placed("w4w_raw", [P, NPASS, H // 2], I32, W4_WORDS_RAW)
+        nc.sync.dma_start(out=w4w_raw[:], in_=w4_words.bitcast(I32).rearrange("a p col -> p a col"))
         nc.sync.dma_start(idx[:], offs)
         nc.sync.dma_start(idx2[:], offs2)
-        for n in range(2 * QUADS):
-            dst, src = (tabs, tab_scales) if n < QUADS else (w4s_raw, w4_scales)
-            r = n % QUADS
-            nc.sync.dma_start(
-                out=dst[r:P:32, :].rearrange("quad (a col) -> quad a col", a=NPASS),
-                in_=src.bitcast(I32)[:, r:16:4, :].rearrange("a quad col -> quad a col"),
-            )
-            g, r2 = n % NPASS, n // NPASS
-            nc.sync.dma_start(out=tab2s[4 + 4 * g + r2 : P : 32, :], in_=tab2_scales.bitcast(I32)[g, r2:16:4, :])
+        nc.sync.dma_start(out=tab2s[0:32, :], in_=tab2_scales.bitcast(I32).rearrange("a q col -> (a q) col"))
+        for dst, src in ((tabs, tab_scales), (w4s_raw, w4_scales)):
+            for r in range(QUADS):
+                nc.sync.dma_start(
+                    out=dst[r:P:32, :].rearrange("quad (a col) -> quad a col", a=NPASS),
+                    in_=src.bitcast(I32)[:, r:16:4, :].rearrange("a quad col -> quad a col"),
+                )
+        w1_raw00 = load_w1(0, 0)
+        w1_raw01 = load_w1(0, 1)
+        tabw0 = load_words(placed("tabw0", [P, T], I32, TAB_WORDS[0]), tab_words[0])
+        w1_raw10 = load_w1(1, 0)
+        tabw1 = load_words(placed("tabw1", [P, T], I32, TAB_WORDS[1]), tab_words[1])
+        w1_raw11 = load_w1(1, 1)
+        tab2w = [load_words(placed("tab2w%d" % g, [P, T2], I32, TAB2_WORDS[g]), tab2_words[g]) for g in range(NPASS)]
 
         b1_sb = [held("b1_sb0", [P, PACK], F32), placed("b1_sb1", [P, PACK], F32, STAGE_H0)]
         b4_sb = held("b4_sb", [P, NPASS, PACK], F32)
         thr_sb = held("thr_sb", [P, PACK], F32)
         b1_rows = b1.rearrange("(g p t) -> g p t", g=NPASS, t=PACK)
         nc.gpsimd.dma_start(out=thr_sb[:], in_=thr.rearrange("(p c) -> p c", c=PACK))
+        ident = held("ident", [P, P], F32)
+        make_identity(nc, ident[:])
         nc.gpsimd.dma_start(out=b1_sb[0][:], in_=b1_rows[0])
         nc.gpsimd.dma_start(out=b4_sb[:], in_=b4.rearrange("(g p t) -> p g t", g=NPASS, t=PACK))
         nc.gpsimd.dma_start(out=b1_sb[1][:], in_=b1_rows[1])
 
-        ident = held("ident", [P, P], F32)
-        make_identity(nc, ident[:])
+        nc.gpsimd.memset(v2s[:], 0)
         thr_ps = psum.tile([P, PACK, P], F32, name="thr_ps", tag="bank%d" % (OUT_TILES - 1))
         for c in range(PACK):
             nc.tensor.transpose(thr_ps[:, c, :], thr_sb[:, c : c + 1].to_broadcast([P, P]), ident[:])
@@ -128,31 +137,28 @@ def tile_list_maxout_face_margins_kernel(
         )
 
         w4w = held("w4w", [P, NPASS, 2 * H], U8)
-        for a in range(NPASS):
-            nc.vector.tensor_copy(
-                out=w4w[:, a, :].bitcast(U16).rearrange("p (g t m) -> p g t m", g=NPASS, t=PACK),
-                in_=w4w_raw[:, a, :].bitcast(U16).rearrange("p (g m t) -> p g t m", g=NPASS, t=PACK),
-            )
-        w1_raw00 = load_w1(0, 0)
-        w1_raw01 = load_w1(0, 1)
+        nc.vector.tensor_copy(
+            out=w4w[:].rearrange("p a b -> p (a b)").bitcast(U16).rearrange("p (ag t m) -> p ag t m", ag=NPASS * NPASS, t=PACK),
+            in_=w4w_raw[:].rearrange("p a b -> p (a b)").bitcast(U16).rearrange("p (ag m t) -> p ag t m", ag=NPASS * NPASS, t=PACK),
+        )
+        v2s_picked = placed("v2s_picked", [P, S2], U8, W4_WORDS_RAW)
+        nc.vector.tensor_copy(v2s_picked[:], tab2s[:].bitcast(U8).indirect(idx2[:]))
+        for g in range(NPASS):
+            for quad in range(QUADS):
+                row = 16 * g + 4 * quad
+                nc.gpsimd.dma_start(
+                    out=v2s[32 * quad + 4 * g : 32 * quad + 4 * g + 4, :], in_=v2s_picked[row : row + 4, :].bitcast(I32)
+                )
 
-        vs = [held("vs%d" % a, [P, S], U8) for a in range(NPASS)]
+        vs = [placed("vs%d" % a, [P, S], U8, TAB2_SCALES + 6 * S + a * S) for a in range(NPASS)]
         for a in range(NPASS):
             nc.vector.tensor_copy(vs[a][:], tabs[:].bitcast(U8)[:, a * T : (a + 1) * T].indirect(idx[:]))
-        tabw0 = load_words(placed("tabw0", [P, T], I32, TAB_WORDS[0]), tab_words[0])
-        w1_raw10 = load_w1(1, 0)
 
         w4s = placed("w4s", [P, NPASS, H], U8, W4_SCALES)
         nc.vector.tensor_copy(
             out=w4s[:].rearrange("p a (g t m) -> p (a g) t m", g=NPASS, t=PACK),
             in_=w4s_raw[:].bitcast(U8).rearrange("p (ag m t) -> p ag t m", ag=NPASS * NPASS, t=PACK),
         )
-        tabw1 = load_words(placed("tabw1", [P, T], I32, TAB_WORDS[1]), tab_words[1])
-        w1_raw11 = load_w1(1, 1)
-
-        v2s = placed("v2s", [P, S2], U8, V2_SCALES)
-        nc.vector.tensor_copy(v2s[:], tab2s[:].bitcast(U8).indirect(idx2[:]))
-        tab2w = [load_words(placed("tab2w%d" % g, [P, T2], I32, TAB2_WORDS[g]), tab2_words[g]) for g in range(NPASS)]
 
         w1_bf00 = held("w1_bf00", [P, PASS * PACK], BF16)
         round_w1(w1_raw00, w1_bf00, P)
@@ -268,7 +274,7 @@ def tile_list_maxout_face_margins_kernel(
             nc.tensor.matmul_mx(
                 out=y_ps[i][:],
                 lhsT=v2w[g, i // HALF_TILES][:, col : col + P].bitcast(FP8X4),
-                lhsT_scale=v2s[4 + 4 * g : P, i * P : (i + 1) * P],
+                lhsT_scale=v2s[4 * g : P, :].bitcast(U8)[:, i * P : (i + 1) * P],
                 rhs=h_codes[g][:].bitcast(FP8X4),
                 rhs_scale=h_scales[g][:],
                 start=(g == 0),

@@ -28,14 +28,16 @@ HALF = S2 // 2
 HALF_TILES = HALF // P
 GPSIMD_TILES = (1, 3)
 
-W4_WORDS_RAW = 104448
 W1_RAW = ((4096, 12288), (28672, 45056))
 TAB_WORDS = (20480, 36864)
 TAB2_WORDS = (53248, 69632)
-TAB2_SCALES, TAB_SCALES, W4_SCALES_RAW = 86016, 90112, 94208
+TAB2_SCALES, ZEROS_END = 86016, 90112
+TAB_SCALES, W4_SCALES_RAW = 90112, 94208
 STAGE_H1, STAGE_H0 = 96256, 100352
-W4_SCALES, V2_SCALES = TAB_SCALES, W4_SCALES_RAW
-V_WORDS0, W1_SCALES00 = W4_SCALES_RAW - 3 * S, W4_SCALES_RAW + 2 * S
+W4_WORDS_RAW, B1 = 104448, 108544
+V_SCALES = TAB2_SCALES + 6 * S
+V_WORDS0 = W4_SCALES_RAW - 3 * S
+W1_SCALES00 = W4_SCALES_RAW + 2 * S
 
 
 def tile_list_maxout_face_margins_kernel(
@@ -70,13 +72,11 @@ def tile_list_maxout_face_margins_kernel(
             nc.sync.dma_start(out=dst[:], in_=words.rearrange("p col j -> p (col j)").bitcast(I32))
             return dst
 
-        def round_w1(raw, dst, on_scalar):
-            grouped = dst[:].rearrange("p (t m j) -> p m t j", t=PACK, j=PACK)
-            src = raw[:].rearrange("p j (m t) -> p m t j", t=PACK)
-            if on_scalar > 0:
-                nc.scalar.copy(out=grouped[:, :on_scalar], in_=src[:, :on_scalar])
-            if on_scalar < P:
-                nc.vector.tensor_copy(out=grouped[:, on_scalar:], in_=src[:, on_scalar:])
+        def round_w1(copy, raw, dst):
+            copy(
+                out=dst[:].rearrange("p (t m j) -> p m t j", t=PACK, j=PACK),
+                in_=raw[:].rearrange("p j (m t) -> p m t j", t=PACK),
+            )
 
         w1_codes = {}
         w1_scales = {}
@@ -90,9 +90,9 @@ def tile_list_maxout_face_margins_kernel(
         w4s_raw = placed("w4s_raw", [P, NPASS * H // 4], I32, W4_SCALES_RAW)
         v2s = held("v2s", [P, S2 // 4], I32)
         nc.vector.memset(tabs[:], 0)
-        gate = placed("gate", [P, TAB_SCALES // 4], I32, 0)
-        nc.vector.memset(gate[:, 0 : NPASS * H // 4], 0)
-        nc.vector.tensor_copy(out=w4s_raw[:], in_=gate[:, 0 : NPASS * H // 4])
+        zeros = placed("zeros", [P, ZEROS_END // 4], I32, 0)[:, 0 : NPASS * H // 4]
+        nc.vector.memset(zeros, 0)
+        nc.vector.tensor_copy(out=w4s_raw[:], in_=zeros)
         tab2s = placed("tab2s", [P, T2 // 4], I32, TAB2_SCALES)
         nc.vector.memset(tab2s[32:64, :], 0)
         nc.vector.memset(tab2s[64:P, :], 0)
@@ -116,18 +116,18 @@ def tile_list_maxout_face_margins_kernel(
         w1_raw11 = load_w1(1, 1)
         tab2w = [load_words(placed("tab2w%d" % g, [P, T2], I32, TAB2_WORDS[g]), tab2_words[g]) for g in range(NPASS)]
 
-        b1_sb = [held("b1_sb0", [P, PACK], F32), placed("b1_sb1", [P, PACK], F32, STAGE_H0)]
-        b4_sb = held("b4_sb", [P, NPASS, PACK], F32)
+        b1_sb = placed("b1_sb", [P, NPASS, PACK], F32, B1)
+        b4_sb = [held("b4_sb0", [P, PACK], F32), placed("b4_sb1", [P, PACK], F32, STAGE_H0)]
         thr_sb = held("thr_sb", [P, PACK], F32)
-        b1_rows = b1.rearrange("(g p t) -> g p t", g=NPASS, t=PACK)
+        b4_rows = b4.rearrange("(g p t) -> g p t", g=NPASS, t=PACK)
         nc.gpsimd.dma_start(out=thr_sb[:], in_=thr.rearrange("(p c) -> p c", c=PACK))
         ident = held("ident", [P, P], F32)
         make_identity(nc, ident[:])
-        nc.gpsimd.dma_start(out=b1_sb[0][:], in_=b1_rows[0])
-        nc.gpsimd.dma_start(out=b4_sb[:], in_=b4.rearrange("(g p t) -> p g t", g=NPASS, t=PACK))
-        nc.gpsimd.dma_start(out=b1_sb[1][:], in_=b1_rows[1])
-
+        nc.gpsimd.dma_start(out=b1_sb[:], in_=b1.rearrange("(g p t) -> p g t", g=NPASS, t=PACK))
+        for g in range(NPASS):
+            nc.gpsimd.dma_start(out=b4_sb[g][:], in_=b4_rows[g])
         nc.gpsimd.memset(v2s[:], 0)
+
         thr_ps = psum.tile([P, PACK, P], F32, name="thr_ps", tag="bank%d" % (OUT_TILES - 1))
         for c in range(PACK):
             nc.tensor.transpose(thr_ps[:, c, :], thr_sb[:, c : c + 1].to_broadcast([P, P]), ident[:])
@@ -137,10 +137,13 @@ def tile_list_maxout_face_margins_kernel(
         )
 
         w4w = held("w4w", [P, NPASS, 2 * H], U8)
+        w4w_to = w4w[:].rearrange("p a col -> p (a col)").bitcast(U16)
+        w4w_from = w4w_raw[:].rearrange("p a col -> p (a col)").bitcast(U16)
         nc.vector.tensor_copy(
-            out=w4w[:].rearrange("p a b -> p (a b)").bitcast(U16).rearrange("p (ag t m) -> p ag t m", ag=NPASS * NPASS, t=PACK),
-            in_=w4w_raw[:].rearrange("p a b -> p (a b)").bitcast(U16).rearrange("p (ag m t) -> p ag t m", ag=NPASS * NPASS, t=PACK),
+            out=w4w_to.rearrange("p (ag t m) -> p ag t m", ag=NPASS * NPASS, t=PACK),
+            in_=w4w_from.rearrange("p (ag m t) -> p ag t m", ag=NPASS * NPASS, t=PACK),
         )
+
         v2s_picked = placed("v2s_picked", [P, S2], U8, W4_WORDS_RAW)
         nc.vector.tensor_copy(v2s_picked[:], tab2s[:].bitcast(U8).indirect(idx2[:]))
         for g in range(NPASS):
@@ -150,38 +153,37 @@ def tile_list_maxout_face_margins_kernel(
                     out=v2s[32 * quad + 4 * g : 32 * quad + 4 * g + 4, :], in_=v2s_picked[row : row + 4, :].bitcast(I32)
                 )
 
-        vs = [placed("vs%d" % a, [P, S], U8, TAB2_SCALES + 6 * S + a * S) for a in range(NPASS)]
+        vs = [placed("vs%d" % a, [P, S], U8, V_SCALES + a * S) for a in range(NPASS)]
         for a in range(NPASS):
             nc.vector.tensor_copy(vs[a][:], tabs[:].bitcast(U8)[:, a * T : (a + 1) * T].indirect(idx[:]))
 
-        w4s = placed("w4s", [P, NPASS, H], U8, W4_SCALES)
+        w4s = placed("w4s", [P, NPASS, H], U8, TAB_SCALES)
         nc.vector.tensor_copy(
             out=w4s[:].rearrange("p a (g t m) -> p (a g) t m", g=NPASS, t=PACK),
             in_=w4s_raw[:].bitcast(U8).rearrange("p (ag m t) -> p ag t m", ag=NPASS * NPASS, t=PACK),
         )
 
         w1_bf00 = held("w1_bf00", [P, PASS * PACK], BF16)
-        round_w1(w1_raw00, w1_bf00, P)
+        round_w1(nc.scalar.copy, w1_raw00, w1_bf00)
         quantize_w1(0, 0, w1_bf00, held("w1_codes00", [P, PASS], U32), placed("w1_scales00", [P, PASS], U8, W1_SCALES00))
         vw = [placed("vw0", [P, S], U32, V_WORDS0)]
         nc.vector.tensor_copy(vw[0][:], tabw0[:].bitcast(U32).indirect(idx[:]))
-        w1_bf01 = held("w1_bf01", [P, PASS * PACK], BF16, "w1_bf00")
-        round_w1(w1_raw01, w1_bf01, P // 2)
-        quantize_w1(0, 1, w1_bf01, held("w1_codes01", [P, PASS], U32), held("w1_scales01", [P, PASS], U8))
+        w1_bf01 = held("w1_bf01", [P, PASS * PACK], BF16)
+        round_w1(nc.scalar.copy, w1_raw01, w1_bf01)
+        quantize_w1(0, 1, w1_bf01, placed("w1_codes01", [P, PASS], U32, TAB_WORDS[0]), held("w1_scales01", [P, PASS], U8))
 
         w1_bf10 = placed("w1_bf10", [P, PASS * PACK], BF16, STAGE_H1)
-        round_w1(w1_raw10, w1_bf10, P)
-        vw.append(held("vw1", [P, S], U32, "w1_bf00"))
+        round_w1(nc.scalar.copy, w1_raw10, w1_bf10)
+        vw.append(held("vw1", [P, S], U32, "w1_bf01"))
         nc.vector.tensor_copy(vw[1][:], tabw1[:].bitcast(U32).indirect(idx[:]))
         quantize_w1(1, 0, w1_bf10, placed("w1_codes10", [P, PASS], U32, TAB_WORDS[1]), held("w1_scales10", [P, PASS], U8))
         w1_bf11 = placed("w1_bf11", [P, PASS * PACK], BF16, STAGE_H1)
-        round_w1(w1_raw11, w1_bf11, 0)
+        round_w1(nc.vector.tensor_copy, w1_raw11, w1_bf11)
         quantize_w1(1, 1, w1_bf11, held("w1_codes11", [P, PASS], U32), held("w1_scales11", [P, PASS], U8))
 
         h_planes = [placed("h_planes0", [P, PACK, S], BF16, STAGE_H1), held("h_planes1", [P, PACK, S], BF16)]
         h_bf = []
         h_codes = []
-        h_scales = [held("h_scales%d" % g, [P, S], U8) for g in range(NPASS)]
 
         def project_a(g, t, a, a_ps):
             nc.tensor.matmul_mx(
@@ -206,16 +208,14 @@ def tile_list_maxout_face_margins_kernel(
                 stop=(a == NPASS - 1),
             )
 
-        def take_max(g, t, a_ps, c_ps):
-            a_sb = held("a_sb%d%d" % (g, t), [P, S], F32)
-            nc.scalar.activation(out=a_sb[:], in_=a_ps[:], func=ACT.Identity, bias=b1_sb[g][:, t : t + 1])
+        def bring_out(name, ps, bias):
+            sb = held(name, [P, S], F32)
+            nc.scalar.activation(out=sb[:], in_=ps[:], func=ACT.Identity, bias=bias)
+            return sb
+
+        def take_max(g, t, ps, bias, sb):
             nc.vector.scalar_tensor_tensor(
-                out=h_planes[g][:, t, :],
-                in0=c_ps[:],
-                scalar=b4_sb[:, g, t : t + 1],
-                in1=a_sb[:],
-                op0=ALU.add,
-                op1=ALU.max,
+                out=h_planes[g][:, t, :], in0=ps[:], scalar=bias, in1=sb[:], op0=ALU.add, op1=ALU.max
             )
 
         def interleave_h(g):
@@ -242,30 +242,35 @@ def tile_list_maxout_face_margins_kernel(
         for t in range(PACK):
             project_a(0, t, 1, a_ps[t])
             project_c(0, t, 1, c_ps[t])
-            take_max(0, t, a_ps[t], c_ps[t])
+            a_sb = bring_out("a_sb%d" % t, a_ps[t], b1_sb[:, 0, t : t + 1])
+            take_max(0, t, c_ps[t], b4_sb[0][:, t : t + 1], a_sb)
 
-        a_ps = [bank(t) for t in range(PACK)]
-        c_ps = [bank(PACK + t) for t in range(PACK)]
+        c_ps = [bank(t) for t in range(PACK)]
+        a_ps = [bank(PACK + t) for t in range(PACK)]
+        c_sb = []
+        for t in range(PACK):
+            for a in range(NPASS):
+                project_c(1, t, a, c_ps[t])
+            c_sb.append(bring_out("c_sb%d" % t, c_ps[t], b4_sb[1][:, t : t + 1]))
         for t in range(PACK):
             for a in range(NPASS):
                 project_a(1, t, a, a_ps[t])
-            for a in range(NPASS):
-                project_c(1, t, a, c_ps[t])
-            take_max(1, t, a_ps[t], c_ps[t])
+            take_max(1, t, a_ps[t], b1_sb[:, 1, t : t + 1], c_sb[t])
 
         h_bf.append(placed("h_bf0", [P, S * PACK], BF16, STAGE_H0))
         interleave_h(0)
         h_bf.append(placed("h_bf1", [P, S * PACK], BF16, STAGE_H1))
         interleave_h(1)
 
-        gather_v2(0, 0, held("v2w00", [P, HALF], U32, "a_sb13"))
+        h_scales = [placed("h_scales0", [P, S], U8, B1), held("h_scales1", [P, S], U8)]
+        gather_v2(0, 0, held("v2w00", [P, HALF], U32, "c_sb%d" % (PACK - 1)))
         h_codes.append(held("h_codes0", [P, S], U32))
         quantize_h(0)
         gather_v2(0, 1, placed("v2w01", [P, HALF], U32, STAGE_H0))
         h_codes.append(placed("h_codes1", [P, S], U32, TAB2_WORDS[0]))
+        gather_v2(1, 0, placed("v2w10", [P, HALF], U32, TAB2_WORDS[0] + 4 * S))
         quantize_h(1)
-        gather_v2(1, 0, placed("v2w10", [P, HALF], U32, STAGE_H1))
-        gather_v2(1, 1, placed("v2w11", [P, HALF], U32, STAGE_H1 + 4 * HALF))
+        gather_v2(1, 1, placed("v2w11", [P, HALF], U32, STAGE_H1))
 
         y_ps = [bank(i) for i in range(OUT_TILES)]
 

@@ -28,10 +28,11 @@ HALF = S2 // 2
 HALF_TILES = HALF // P
 GPSIMD_TILES = (1, 3)
 
-W1_RAW = ((4096, 12288), (28672, 45056))
-TAB_WORDS = (20480, 36864)
-TAB2_WORDS = (53248, 69632)
-TAB2_SCALES, ZEROS_END = 86016, 90112
+W1_RAW = ((4096, 20480), (12288, 45056))
+TAB_WORDS = (28672, 36864)
+TAB2_WORDS = (53248, 4096)
+TAB2_SCALES, ZEROS_END = 86016, 86016
+V2S_ROW = 96
 TAB_SCALES, W4_SCALES_RAW = 90112, 94208
 STAGE_H1, STAGE_H0 = 96256, 100352
 W4_WORDS_RAW, B1 = 104448, 108544
@@ -89,19 +90,26 @@ def tile_list_maxout_face_margins_kernel(
         tabs = placed("tabs", [P, NPASS * T // 4], I32, TAB_SCALES)
         w4s_raw = placed("w4s_raw", [P, NPASS * H // 4], I32, W4_SCALES_RAW)
         v2s = held("v2s", [P, S2 // 4], I32)
-        nc.vector.memset(tabs[:], 0)
-        zeros = placed("zeros", [P, ZEROS_END // 4], I32, 0)[:, 0 : NPASS * H // 4]
+        zeros = placed("zeros", [P, ZEROS_END // 4], I32, 0)[:, 0 : S2 // 4]
         nc.vector.memset(zeros, 0)
-        nc.vector.tensor_copy(out=w4s_raw[:], in_=zeros)
+        nc.vector.memset(tabs[:], 0)
+        nc.vector.memset(w4s_raw[:], 0)
+        nc.vector.tensor_copy(out=v2s[:], in_=zeros)
         tab2s = placed("tab2s", [P, T2 // 4], I32, TAB2_SCALES)
-        nc.vector.memset(tab2s[32:64, :], 0)
-        nc.vector.memset(tab2s[64:P, :], 0)
+        nc.vector.memset(tab2s[0:V2S_ROW, :], 0)
 
         w4w_raw = placed("w4w_raw", [P, NPASS, H // 2], I32, W4_WORDS_RAW)
-        nc.sync.dma_start(out=w4w_raw[:], in_=w4_words.bitcast(I32).rearrange("a p col -> p a col"))
-        nc.sync.dma_start(idx[:], offs)
+        b1_sb = placed("b1_sb", [P, NPASS, PACK], F32, B1)
+        b4_all = placed("b4_all", [P, NPASS, PACK], F32, STAGE_H0)
+        b4_sb = [b4_all[:, 0, :], b4_all[:, 1, :]]
+        thr_sb = held("thr_sb", [P, PACK], F32)
         nc.sync.dma_start(idx2[:], offs2)
-        nc.sync.dma_start(out=tab2s[0:32, :], in_=tab2_scales.bitcast(I32).rearrange("a q col -> (a q) col"))
+        nc.scalar.dma_start(out=thr_sb[:], in_=thr.rearrange("(p c) -> p c", c=PACK))
+        nc.sync.dma_start(idx[:], offs)
+        nc.scalar.dma_start(out=b4_all[:], in_=b4.rearrange("(g p t) -> p g t", g=NPASS, t=PACK))
+        nc.sync.dma_start(out=tab2s[V2S_ROW:P, :], in_=tab2_scales.bitcast(I32).rearrange("a q col -> (a q) col"))
+        nc.scalar.dma_start(out=b1_sb[:], in_=b1.rearrange("(g p t) -> p g t", g=NPASS, t=PACK))
+        nc.sync.dma_start(out=w4w_raw[:], in_=w4_words.bitcast(I32).rearrange("a p col -> p a col"))
         for dst, src in ((tabs, tab_scales), (w4s_raw, w4_scales)):
             for r in range(QUADS):
                 nc.sync.dma_start(
@@ -116,17 +124,8 @@ def tile_list_maxout_face_margins_kernel(
         w1_raw11 = load_w1(1, 1)
         tab2w = [load_words(placed("tab2w%d" % g, [P, T2], I32, TAB2_WORDS[g]), tab2_words[g]) for g in range(NPASS)]
 
-        b1_sb = placed("b1_sb", [P, NPASS, PACK], F32, B1)
-        b4_sb = [held("b4_sb0", [P, PACK], F32), placed("b4_sb1", [P, PACK], F32, STAGE_H0)]
-        thr_sb = held("thr_sb", [P, PACK], F32)
-        b4_rows = b4.rearrange("(g p t) -> g p t", g=NPASS, t=PACK)
-        nc.gpsimd.dma_start(out=thr_sb[:], in_=thr.rearrange("(p c) -> p c", c=PACK))
         ident = held("ident", [P, P], F32)
         make_identity(nc, ident[:])
-        nc.gpsimd.dma_start(out=b1_sb[:], in_=b1.rearrange("(g p t) -> p g t", g=NPASS, t=PACK))
-        for g in range(NPASS):
-            nc.gpsimd.dma_start(out=b4_sb[g][:], in_=b4_rows[g])
-        nc.gpsimd.memset(v2s[:], 0)
 
         thr_ps = psum.tile([P, PACK, P], F32, name="thr_ps", tag="bank%d" % (OUT_TILES - 1))
         for c in range(PACK):
@@ -148,7 +147,7 @@ def tile_list_maxout_face_margins_kernel(
         nc.vector.tensor_copy(v2s_picked[:], tab2s[:].bitcast(U8).indirect(idx2[:]))
         for g in range(NPASS):
             for quad in range(QUADS):
-                row = 16 * g + 4 * quad
+                row = V2S_ROW + 16 * g + 4 * quad
                 nc.gpsimd.dma_start(
                     out=v2s[32 * quad + 4 * g : 32 * quad + 4 * g + 4, :], in_=v2s_picked[row : row + 4, :].bitcast(I32)
                 )

@@ -28,17 +28,12 @@ HALF = S2 // 2
 HALF_TILES = HALF // P
 GPSIMD_TILES = (1, 3)
 
-W1_RAW = ((4096, 20480), (12288, 45056))
-TAB_WORDS = (28672, 36864)
-TAB2_WORDS = (53248, 4096)
-TAB2_SCALES, ZEROS_END = 86016, 86016
-V2S_ROW = 96
-TAB_SCALES, W4_SCALES_RAW = 90112, 94208
-STAGE_H1, STAGE_H0 = 96256, 100352
-W4_WORDS_RAW, B1 = 104448, 108544
-V_SCALES = TAB2_SCALES + 6 * S
-V_WORDS0 = W4_SCALES_RAW - 3 * S
-W1_SCALES00 = W4_SCALES_RAW + 2 * S
+ROW0 = 96
+JOINT = S + H
+
+W4_SCALES_RAW, TAB_WORDS1 = 0, 1024
+STAGE_H1, W4_WORDS = 9216, 13312 - 64
+STAGE_H0, B1 = 17408, 21504
 
 
 def tile_list_maxout_face_margins_kernel(
@@ -64,7 +59,7 @@ def tile_list_maxout_face_margins_kernel(
         idx2 = keep.tile([P, S2 // 16], U16, name="idx2")
 
         def load_w1(g, a):
-            raw = placed("w1_raw%d%d" % (g, a), [P, PACK, PASS], F32, W1_RAW[g][a])
+            raw = held("w1_raw%d%d" % (g, a), [P, PACK, PASS], F32)
             rows = w1[a * PASS : (a + 1) * PASS, g * PASS : (g + 1) * PASS]
             nc.sync.dma_start(out=raw[:], in_=rows.rearrange("(p j) c -> p j c", j=PACK))
             return raw
@@ -79,6 +74,12 @@ def tile_list_maxout_face_margins_kernel(
                 in_=raw[:].rearrange("p j (m t) -> p m t j", t=PACK),
             )
 
+        def round_w1_vector(raw, dst):
+            nc.vector.tensor_copy(
+                out=dst[:].rearrange("p (th tl m j) -> p th m tl j", th=2, tl=2, j=PACK),
+                in_=raw[:].rearrange("p j (m th tl) -> p th m tl j", th=2, tl=2),
+            )
+
         w1_codes = {}
         w1_scales = {}
 
@@ -87,43 +88,41 @@ def tile_list_maxout_face_margins_kernel(
             w1_scales.setdefault((g, a), scales)
             nc.vector.quantize_mx(out=codes[:].bitcast(FP8X4), scales=scales[:], in_=src[:])
 
-        tabs = placed("tabs", [P, NPASS * T // 4], I32, TAB_SCALES)
-        w4s_raw = placed("w4s_raw", [P, NPASS * H // 4], I32, W4_SCALES_RAW)
+        tabs = held("tabs", [P, T // 4], I32)
+        w4s_raw = placed("w4s_raw", [P, H // 4], I32, W4_SCALES_RAW)
+        tab2s = held("tab2s", [P, T2 // 4], I32)
+        planes = [held("planes%d" % a, [P, JOINT // 4], I32) for a in range(NPASS)]
         v2s = held("v2s", [P, S2 // 4], I32)
-        zeros = placed("zeros", [P, ZEROS_END // 4], I32, 0)[:, 0 : S2 // 4]
-        nc.vector.memset(zeros, 0)
-        nc.vector.memset(tabs[:], 0)
-        nc.vector.memset(w4s_raw[:], 0)
-        nc.vector.tensor_copy(out=v2s[:], in_=zeros)
-        tab2s = placed("tab2s", [P, T2 // 4], I32, TAB2_SCALES)
-        nc.vector.memset(tab2s[0:V2S_ROW, :], 0)
+        for staged in (tabs, w4s_raw, tab2s):
+            nc.vector.memset(staged[0:ROW0, :], 0)
+        for tile in planes + [v2s]:
+            nc.vector.memset(tile[:], 0)
 
-        w4w_raw = placed("w4w_raw", [P, NPASS, H // 2], I32, W4_WORDS_RAW)
+        def load_scales(dst, src):
+            nc.sync.dma_start(out=dst[ROW0:P, :], in_=src.bitcast(I32).rearrange("a q col -> (a q) col"))
+
+        w4w_raw = held("w4w_raw", [P, NPASS, H // 2], I32)
+        nc.sync.dma_start(idx[:], offs)
+        load_scales(tabs, tab_scales)
+        load_scales(w4s_raw, w4_scales)
+        nc.sync.dma_start(idx2[:], offs2)
+        load_scales(tab2s, tab2_scales)
+        nc.sync.dma_start(out=w4w_raw[:], in_=w4_words.bitcast(I32).rearrange("a p col -> p a col"))
+        w1_raw00 = load_w1(0, 0)
+        w1_raw01 = load_w1(0, 1)
+        tabw0 = load_words(held("tabw0", [P, T], I32), tab_words[0])
+        w1_raw10 = load_w1(1, 0)
+        tabw1 = load_words(placed("tabw1", [P, T], I32, TAB_WORDS1), tab_words[1])
+        w1_raw11 = load_w1(1, 1)
+        tab2w = [load_words(placed("tab2w%d" % g, [P, T2], I32, 24576 + 16384 * g), tab2_words[g]) for g in range(NPASS)]
+
         b1_sb = placed("b1_sb", [P, NPASS, PACK], F32, B1)
         b4_all = placed("b4_all", [P, NPASS, PACK], F32, STAGE_H0)
         b4_sb = [b4_all[:, 0, :], b4_all[:, 1, :]]
         thr_sb = held("thr_sb", [P, PACK], F32)
-        nc.sync.dma_start(idx2[:], offs2)
-        nc.scalar.dma_start(out=thr_sb[:], in_=thr.rearrange("(p c) -> p c", c=PACK))
-        nc.sync.dma_start(idx[:], offs)
-        nc.scalar.dma_start(out=b4_all[:], in_=b4.rearrange("(g p t) -> p g t", g=NPASS, t=PACK))
-        nc.sync.dma_start(out=tab2s[V2S_ROW:P, :], in_=tab2_scales.bitcast(I32).rearrange("a q col -> (a q) col"))
-        nc.scalar.dma_start(out=b1_sb[:], in_=b1.rearrange("(g p t) -> p g t", g=NPASS, t=PACK))
-        nc.sync.dma_start(out=w4w_raw[:], in_=w4_words.bitcast(I32).rearrange("a p col -> p a col"))
-        for dst, src in ((tabs, tab_scales), (w4s_raw, w4_scales)):
-            for r in range(QUADS):
-                nc.sync.dma_start(
-                    out=dst[r:P:32, :].rearrange("quad (a col) -> quad a col", a=NPASS),
-                    in_=src.bitcast(I32)[:, r:16:4, :].rearrange("a quad col -> quad a col"),
-                )
-        w1_raw00 = load_w1(0, 0)
-        w1_raw01 = load_w1(0, 1)
-        tabw0 = load_words(placed("tabw0", [P, T], I32, TAB_WORDS[0]), tab_words[0])
-        w1_raw10 = load_w1(1, 0)
-        tabw1 = load_words(placed("tabw1", [P, T], I32, TAB_WORDS[1]), tab_words[1])
-        w1_raw11 = load_w1(1, 1)
-        tab2w = [load_words(placed("tab2w%d" % g, [P, T2], I32, TAB2_WORDS[g]), tab2_words[g]) for g in range(NPASS)]
-
+        nc.gpsimd.dma_start(out=thr_sb[:], in_=thr.rearrange("(p c) -> p c", c=PACK))
+        nc.gpsimd.dma_start(out=b1_sb[:], in_=b1.rearrange("(g p t) -> p g t", g=NPASS, t=PACK))
+        nc.gpsimd.dma_start(out=b4_all[:], in_=b4.rearrange("(g p t) -> p g t", g=NPASS, t=PACK))
         ident = held("ident", [P, P], F32)
         make_identity(nc, ident[:])
 
@@ -135,7 +134,31 @@ def tile_list_maxout_face_margins_kernel(
             out=thr_all[:].rearrange("row (p c) -> row p c", c=PACK), in_=thr_ps[:].rearrange("row c p -> row p c")
         )
 
-        w4w = held("w4w", [P, NPASS, 2 * H], U8)
+        joint = held("joint", [P, JOINT], U8)
+        vs_picked = held("vs_picked", [P, S], U8)
+        nc.vector.tensor_copy(vs_picked[:], tabs[:].bitcast(U8).indirect(idx[:]))
+        nc.vector.tensor_copy(
+            out=joint[:, S:JOINT].rearrange("p (g t m) -> p g t m", g=NPASS, t=PACK),
+            in_=w4s_raw[:].bitcast(U8).rearrange("p (g m t) -> p g t m", g=NPASS, t=PACK),
+        )
+        nc.vector.tensor_copy(out=joint[:, 0:S].bitcast(I32), in_=vs_picked[:].bitcast(I32))
+        for a in range(NPASS):
+            for quad in range(QUADS):
+                row = ROW0 + 16 * a + 4 * quad
+                nc.gpsimd.dma_start(out=planes[a][32 * quad : 32 * quad + 4, :], in_=joint[row : row + 4, :].bitcast(I32))
+        vs = [planes[a][:].bitcast(U8)[:, 0:S] for a in range(NPASS)]
+        w4s = [planes[a][:].bitcast(U8)[:, S:JOINT] for a in range(NPASS)]
+
+        v2s_picked = placed("v2s_picked", [P, S2], U8, W4_SCALES_RAW)
+        nc.vector.tensor_copy(v2s_picked[:], tab2s[:].bitcast(U8).indirect(idx2[:]))
+        for g in range(NPASS):
+            for quad in range(QUADS):
+                row = ROW0 + 16 * g + 4 * quad
+                nc.gpsimd.dma_start(
+                    out=v2s[32 * quad + 4 * g : 32 * quad + 4 * g + 4, :], in_=v2s_picked[row : row + 4, :].bitcast(I32)
+                )
+
+        w4w = placed("w4w", [P, NPASS, 2 * H], U8, W4_WORDS)
         w4w_to = w4w[:].rearrange("p a col -> p (a col)").bitcast(U16)
         w4w_from = w4w_raw[:].rearrange("p a col -> p (a col)").bitcast(U16)
         nc.vector.tensor_copy(
@@ -143,41 +166,22 @@ def tile_list_maxout_face_margins_kernel(
             in_=w4w_from.rearrange("p (ag m t) -> p ag t m", ag=NPASS * NPASS, t=PACK),
         )
 
-        v2s_picked = placed("v2s_picked", [P, S2], U8, W4_WORDS_RAW)
-        nc.vector.tensor_copy(v2s_picked[:], tab2s[:].bitcast(U8).indirect(idx2[:]))
-        for g in range(NPASS):
-            for quad in range(QUADS):
-                row = V2S_ROW + 16 * g + 4 * quad
-                nc.gpsimd.dma_start(
-                    out=v2s[32 * quad + 4 * g : 32 * quad + 4 * g + 4, :], in_=v2s_picked[row : row + 4, :].bitcast(I32)
-                )
-
-        vs = [placed("vs%d" % a, [P, S], U8, V_SCALES + a * S) for a in range(NPASS)]
-        for a in range(NPASS):
-            nc.vector.tensor_copy(vs[a][:], tabs[:].bitcast(U8)[:, a * T : (a + 1) * T].indirect(idx[:]))
-
-        w4s = placed("w4s", [P, NPASS, H], U8, TAB_SCALES)
-        nc.vector.tensor_copy(
-            out=w4s[:].rearrange("p a (g t m) -> p (a g) t m", g=NPASS, t=PACK),
-            in_=w4s_raw[:].bitcast(U8).rearrange("p (ag m t) -> p ag t m", ag=NPASS * NPASS, t=PACK),
-        )
-
         w1_bf00 = held("w1_bf00", [P, PASS * PACK], BF16)
         round_w1(nc.scalar.copy, w1_raw00, w1_bf00)
-        quantize_w1(0, 0, w1_bf00, held("w1_codes00", [P, PASS], U32), placed("w1_scales00", [P, PASS], U8, W1_SCALES00))
-        vw = [placed("vw0", [P, S], U32, V_WORDS0)]
+        quantize_w1(0, 0, w1_bf00, held("w1_codes00", [P, PASS], U32), held("w1_scales00", [P, PASS], U8))
+        vw = [held("vw0", [P, S], U32)]
         nc.vector.tensor_copy(vw[0][:], tabw0[:].bitcast(U32).indirect(idx[:]))
         w1_bf01 = held("w1_bf01", [P, PASS * PACK], BF16)
         round_w1(nc.scalar.copy, w1_raw01, w1_bf01)
-        quantize_w1(0, 1, w1_bf01, placed("w1_codes01", [P, PASS], U32, TAB_WORDS[0]), held("w1_scales01", [P, PASS], U8))
+        quantize_w1(0, 1, w1_bf01, held("w1_codes01", [P, PASS], U32), held("w1_scales01", [P, PASS], U8))
 
-        w1_bf10 = placed("w1_bf10", [P, PASS * PACK], BF16, STAGE_H1)
+        w1_bf10 = held("w1_bf10", [P, PASS * PACK], BF16)
         round_w1(nc.scalar.copy, w1_raw10, w1_bf10)
-        vw.append(held("vw1", [P, S], U32, "w1_bf01"))
+        vw.append(held("vw1", [P, S], U32))
         nc.vector.tensor_copy(vw[1][:], tabw1[:].bitcast(U32).indirect(idx[:]))
-        quantize_w1(1, 0, w1_bf10, placed("w1_codes10", [P, PASS], U32, TAB_WORDS[1]), held("w1_scales10", [P, PASS], U8))
-        w1_bf11 = placed("w1_bf11", [P, PASS * PACK], BF16, STAGE_H1)
-        round_w1(nc.vector.tensor_copy, w1_raw11, w1_bf11)
+        quantize_w1(1, 0, w1_bf10, placed("w1_codes10", [P, PASS], U32, TAB_WORDS1), held("w1_scales10", [P, PASS], U8))
+        w1_bf11 = placed("w1_bf11", [P, PASS * PACK], BF16, STAGE_H1 - 64)
+        round_w1_vector(w1_raw11, w1_bf11)
         quantize_w1(1, 1, w1_bf11, held("w1_codes11", [P, PASS], U32), held("w1_scales11", [P, PASS], U8))
 
         h_planes = [placed("h_planes0", [P, PACK, S], BF16, STAGE_H1), held("h_planes1", [P, PACK, S], BF16)]
@@ -190,7 +194,7 @@ def tile_list_maxout_face_margins_kernel(
                 lhsT=w1_codes[g, a][:, t * P : (t + 1) * P].bitcast(FP8X4),
                 lhsT_scale=w1_scales[g, a][:, t * P : (t + 1) * P],
                 rhs=vw[a][:].bitcast(FP8X4),
-                rhs_scale=vs[a][:],
+                rhs_scale=vs[a],
                 start=(a == 0),
                 stop=(a == NPASS - 1),
             )
@@ -200,9 +204,9 @@ def tile_list_maxout_face_margins_kernel(
             nc.tensor.matmul_mx(
                 out=c_ps[:],
                 lhsT=w4w[:, a, 2 * col : 2 * (col + P)].bitcast(FP4X4),
-                lhsT_scale=w4s[:, a, col : col + P],
+                lhsT_scale=w4s[a][:, col : col + P],
                 rhs=vw[a][:].bitcast(FP8X4),
-                rhs_scale=vs[a][:],
+                rhs_scale=vs[a],
                 start=(a == 0),
                 stop=(a == NPASS - 1),
             )
@@ -238,19 +242,23 @@ def tile_list_maxout_face_margins_kernel(
         for t in range(PACK):
             project_a(0, t, 0, a_ps[t])
             project_c(0, t, 0, c_ps[t])
+        a_sb = []
         for t in range(PACK):
             project_a(0, t, 1, a_ps[t])
+            a_sb.append(bring_out("a_sb%d" % t, a_ps[t], b1_sb[:, 0, t : t + 1]))
+        for t in range(PACK):
             project_c(0, t, 1, c_ps[t])
-            a_sb = bring_out("a_sb%d" % t, a_ps[t], b1_sb[:, 0, t : t + 1])
-            take_max(0, t, c_ps[t], b4_sb[0][:, t : t + 1], a_sb)
+        c0_ps = c_ps
 
         c_ps = [bank(t) for t in range(PACK)]
-        a_ps = [bank(PACK + t) for t in range(PACK)]
         c_sb = []
         for t in range(PACK):
             for a in range(NPASS):
                 project_c(1, t, a, c_ps[t])
             c_sb.append(bring_out("c_sb%d" % t, c_ps[t], b4_sb[1][:, t : t + 1]))
+        for t in range(PACK):
+            take_max(0, t, c0_ps[t], b4_sb[0][:, t : t + 1], a_sb[t])
+        a_ps = [bank(PACK + t) for t in range(PACK)]
         for t in range(PACK):
             for a in range(NPASS):
                 project_a(1, t, a, a_ps[t])
@@ -266,8 +274,8 @@ def tile_list_maxout_face_margins_kernel(
         h_codes.append(held("h_codes0", [P, S], U32))
         quantize_h(0)
         gather_v2(0, 1, placed("v2w01", [P, HALF], U32, STAGE_H0))
-        h_codes.append(placed("h_codes1", [P, S], U32, TAB2_WORDS[0]))
-        gather_v2(1, 0, placed("v2w10", [P, HALF], U32, TAB2_WORDS[0] + 4 * S))
+        h_codes.append(placed("h_codes1", [P, S], U32, 24576))
+        gather_v2(1, 0, placed("v2w10", [P, HALF], U32, 24576 + 4 * S))
         quantize_h(1)
         gather_v2(1, 1, placed("v2w11", [P, HALF], U32, STAGE_H1))
 

@@ -32,8 +32,9 @@ ROW0 = 96
 JOINT = S + H
 
 W4_SCALES_RAW, TAB_WORDS1 = 0, 1024
-STAGE_H1, W4_WORDS = 9216, 13312 - 64
-STAGE_H0, B1 = 17408, 21504
+STAGE_H1 = 73728
+STAGE_H0, B1 = 81920, 86016
+TAB2_WORDS0, TAB_WORDS0, W1_RAW11, W1_RAW10, W1_RAW00 = 24576, 40960, 49152, 57344, 65536
 
 
 def tile_list_maxout_face_margins_kernel(
@@ -58,8 +59,7 @@ def tile_list_maxout_face_margins_kernel(
         idx = keep.tile([P, S // 16], U16, name="idx")
         idx2 = keep.tile([P, S2 // 16], U16, name="idx2")
 
-        def load_w1(g, a):
-            raw = held("w1_raw%d%d" % (g, a), [P, PACK, PASS], F32)
+        def load_w1(g, a, raw):
             rows = w1[a * PASS : (a + 1) * PASS, g * PASS : (g + 1) * PASS]
             nc.sync.dma_start(out=raw[:], in_=rows.rearrange("(p j) c -> p j c", j=PACK))
             return raw
@@ -107,20 +107,15 @@ def tile_list_maxout_face_margins_kernel(
         load_scales(w4s_raw, w4_scales)
         nc.sync.dma_start(idx2[:], offs2)
         load_scales(tab2s, tab2_scales)
+        thr_sb = held("thr_sb", [P, PACK], F32)
+        nc.sync.dma_start(out=thr_sb[:], in_=thr.rearrange("(p c) -> p c", c=PACK))
         nc.sync.dma_start(out=w4w_raw[:], in_=w4_words.bitcast(I32).rearrange("a p col -> p a col"))
-        w1_raw00 = load_w1(0, 0)
-        w1_raw01 = load_w1(0, 1)
-        tabw0 = load_words(held("tabw0", [P, T], I32), tab_words[0])
-        w1_raw10 = load_w1(1, 0)
-        tabw1 = load_words(placed("tabw1", [P, T], I32, TAB_WORDS1), tab_words[1])
-        w1_raw11 = load_w1(1, 1)
-        tab2w = [load_words(placed("tab2w%d" % g, [P, T2], I32, 24576 + 16384 * g), tab2_words[g]) for g in range(NPASS)]
+        w1_raw00 = load_w1(0, 0, placed("w1_raw00", [P, PACK, PASS], F32, W1_RAW00))
+        w1_raw01 = load_w1(0, 1, held("w1_raw01", [P, PACK, PASS], F32))
 
         b1_sb = placed("b1_sb", [P, NPASS, PACK], F32, B1)
         b4_all = placed("b4_all", [P, NPASS, PACK], F32, STAGE_H0)
         b4_sb = [b4_all[:, 0, :], b4_all[:, 1, :]]
-        thr_sb = held("thr_sb", [P, PACK], F32)
-        nc.gpsimd.dma_start(out=thr_sb[:], in_=thr.rearrange("(p c) -> p c", c=PACK))
         nc.gpsimd.dma_start(out=b1_sb[:], in_=b1.rearrange("(g p t) -> p g t", g=NPASS, t=PACK))
         nc.gpsimd.dma_start(out=b4_all[:], in_=b4.rearrange("(g p t) -> p g t", g=NPASS, t=PACK))
         ident = held("ident", [P, P], F32)
@@ -135,17 +130,30 @@ def tile_list_maxout_face_margins_kernel(
         )
 
         joint = held("joint", [P, JOINT], U8)
-        vs_picked = held("vs_picked", [P, S], U8)
-        nc.vector.tensor_copy(vs_picked[:], tabs[:].bitcast(U8).indirect(idx[:]))
+        vs_picked = placed("vs_picked", [P, W1_RAW00 - TAB_WORDS1], U8, TAB_WORDS1)[:, 0:S]
+        nc.vector.tensor_copy(vs_picked, tabs[:].bitcast(U8).indirect(idx[:]))
         nc.vector.tensor_copy(
             out=joint[:, S:JOINT].rearrange("p (g t m) -> p g t m", g=NPASS, t=PACK),
             in_=w4s_raw[:].bitcast(U8).rearrange("p (g m t) -> p g t m", g=NPASS, t=PACK),
         )
-        nc.vector.tensor_copy(out=joint[:, 0:S].bitcast(I32), in_=vs_picked[:].bitcast(I32))
-        for a in range(NPASS):
-            for quad in range(QUADS):
+        nc.vector.tensor_copy(out=joint[:, 0:S].bitcast(I32), in_=vs_picked.bitcast(I32))
+
+        def move_planes(a, quads):
+            for quad in quads:
                 row = ROW0 + 16 * a + 4 * quad
-                nc.gpsimd.dma_start(out=planes[a][32 * quad : 32 * quad + 4, :], in_=joint[row : row + 4, :].bitcast(I32))
+                nc.sync.dma_start(out=planes[a][32 * quad : 32 * quad + 4, :], in_=joint[row : row + 4, :].bitcast(I32))
+
+        move_planes(0, range(QUADS))
+        tabw0 = load_words(placed("tabw0", [P, T], I32, TAB_WORDS0), tab_words[0])
+        move_planes(1, range(1))
+        w1_raw10 = load_w1(1, 0, placed("w1_raw10", [P, PACK, PASS], F32, W1_RAW10))
+        move_planes(1, range(1, QUADS))
+        tabw1 = load_words(placed("tabw1", [P, T], I32, TAB_WORDS1), tab_words[1])
+        w1_raw11 = load_w1(1, 1, placed("w1_raw11", [P, PACK, PASS], F32, W1_RAW11))
+        tab2w = [
+            load_words(placed("tab2w0", [P, T2], I32, TAB2_WORDS0), tab2_words[0]),
+            load_words(placed("tab2w1", [P, T2], I32, W1_RAW10), tab2_words[1]),
+        ]
         vs = [planes[a][:].bitcast(U8)[:, 0:S] for a in range(NPASS)]
         w4s = [planes[a][:].bitcast(U8)[:, S:JOINT] for a in range(NPASS)]
 
@@ -158,7 +166,7 @@ def tile_list_maxout_face_margins_kernel(
                     out=v2s[32 * quad + 4 * g : 32 * quad + 4 * g + 4, :], in_=v2s_picked[row : row + 4, :].bitcast(I32)
                 )
 
-        w4w = placed("w4w", [P, NPASS, 2 * H], U8, W4_WORDS)
+        w4w = held("w4w", [P, NPASS, 2 * H], U8)
         w4w_to = w4w[:].rearrange("p a col -> p (a col)").bitcast(U16)
         w4w_from = w4w_raw[:].rearrange("p a col -> p (a col)").bitcast(U16)
         nc.vector.tensor_copy(
@@ -173,14 +181,14 @@ def tile_list_maxout_face_margins_kernel(
         nc.vector.tensor_copy(vw[0][:], tabw0[:].bitcast(U32).indirect(idx[:]))
         w1_bf01 = held("w1_bf01", [P, PASS * PACK], BF16)
         round_w1(nc.scalar.copy, w1_raw01, w1_bf01)
-        quantize_w1(0, 1, w1_bf01, held("w1_codes01", [P, PASS], U32), held("w1_scales01", [P, PASS], U8))
+        quantize_w1(0, 1, w1_bf01, placed("w1_codes01", [P, PASS], U32, TAB_WORDS0), held("w1_scales01", [P, PASS], U8))
 
         w1_bf10 = held("w1_bf10", [P, PASS * PACK], BF16)
         round_w1(nc.scalar.copy, w1_raw10, w1_bf10)
         vw.append(held("vw1", [P, S], U32))
         nc.vector.tensor_copy(vw[1][:], tabw1[:].bitcast(U32).indirect(idx[:]))
         quantize_w1(1, 0, w1_bf10, placed("w1_codes10", [P, PASS], U32, TAB_WORDS1), held("w1_scales10", [P, PASS], U8))
-        w1_bf11 = placed("w1_bf11", [P, PASS * PACK], BF16, STAGE_H1 - 64)
+        w1_bf11 = placed("w1_bf11", [P, PASS * PACK], BF16, STAGE_H1)
         round_w1_vector(w1_raw11, w1_bf11)
         quantize_w1(1, 1, w1_bf11, held("w1_codes11", [P, PASS], U32), held("w1_scales11", [P, PASS], U8))
 
@@ -274,8 +282,8 @@ def tile_list_maxout_face_margins_kernel(
         h_codes.append(held("h_codes0", [P, S], U32))
         quantize_h(0)
         gather_v2(0, 1, placed("v2w01", [P, HALF], U32, STAGE_H0))
-        h_codes.append(placed("h_codes1", [P, S], U32, 24576))
-        gather_v2(1, 0, placed("v2w10", [P, HALF], U32, 24576 + 4 * S))
+        h_codes.append(placed("h_codes1", [P, S], U32, TAB2_WORDS0))
+        gather_v2(1, 0, placed("v2w10", [P, HALF], U32, TAB2_WORDS0 + 4 * S))
         quantize_h(1)
         gather_v2(1, 1, placed("v2w11", [P, HALF], U32, STAGE_H1))
 

@@ -29,12 +29,12 @@ HALF_TILES = HALF // P
 GPSIMD_TILES = (1, 3)
 
 ROW0 = 96
-JOINT = S + H
+JOINT = S + H + S2
 
 W4_SCALES_RAW, TAB_WORDS1 = 0, 1024
 STAGE_H1 = 73728
 STAGE_H0, B1 = 81920, 86016
-TAB2_WORDS0, TAB_WORDS0, W1_RAW11, W1_RAW10, W1_RAW00 = 24576, 40960, 49152, 57344, 65536
+TAB2_WORDS0, W1_RAW11, W1_RAW10, TAB2_WORDS1, TAB_WORDS0 = 9216, 25600, 33792, 41984, 58368
 
 
 def tile_list_maxout_face_margins_kernel(
@@ -62,7 +62,7 @@ def tile_list_maxout_face_margins_kernel(
         def load_w1(g, a, raw):
             rows = w1[a * PASS : (a + 1) * PASS, g * PASS : (g + 1) * PASS]
             nc.sync.dma_start(out=raw[:], in_=rows.rearrange("(p j) c -> p j c", j=PACK))
-            return raw
+            return raw[:]
 
         def load_words(dst, words):
             nc.sync.dma_start(out=dst[:], in_=words.rearrange("p col j -> p (col j)").bitcast(I32))
@@ -71,13 +71,13 @@ def tile_list_maxout_face_margins_kernel(
         def round_w1(copy, raw, dst):
             copy(
                 out=dst[:].rearrange("p (t m j) -> p m t j", t=PACK, j=PACK),
-                in_=raw[:].rearrange("p j (m t) -> p m t j", t=PACK),
+                in_=raw.rearrange("p j (m t) -> p m t j", t=PACK),
             )
 
         def round_w1_vector(raw, dst):
             nc.vector.tensor_copy(
                 out=dst[:].rearrange("p (th tl m j) -> p th m tl j", th=2, tl=2, j=PACK),
-                in_=raw[:].rearrange("p j (m th tl) -> p th m tl j", th=2, tl=2),
+                in_=raw.rearrange("p j (m th tl) -> p th m tl j", th=2, tl=2),
             )
 
         w1_codes = {}
@@ -92,10 +92,9 @@ def tile_list_maxout_face_margins_kernel(
         w4s_raw = placed("w4s_raw", [P, H // 4], I32, W4_SCALES_RAW)
         tab2s = held("tab2s", [P, T2 // 4], I32)
         planes = [held("planes%d" % a, [P, JOINT // 4], I32) for a in range(NPASS)]
-        v2s = held("v2s", [P, S2 // 4], I32)
         for staged in (tabs, w4s_raw, tab2s):
             nc.vector.memset(staged[0:ROW0, :], 0)
-        for tile in planes + [v2s]:
+        for tile in planes:
             nc.vector.memset(tile[:], 0)
 
         def load_scales(dst, src):
@@ -110,8 +109,10 @@ def tile_list_maxout_face_margins_kernel(
         thr_sb = held("thr_sb", [P, PACK], F32)
         nc.sync.dma_start(out=thr_sb[:], in_=thr.rearrange("(p c) -> p c", c=PACK))
         nc.sync.dma_start(out=w4w_raw[:], in_=w4_words.bitcast(I32).rearrange("a p col -> p a col"))
-        w1_raw00 = load_w1(0, 0, placed("w1_raw00", [P, PACK, PASS], F32, W1_RAW00))
-        w1_raw01 = load_w1(0, 1, held("w1_raw01", [P, PACK, PASS], F32))
+        w1_raw0 = held("w1_raw0", [P, PACK, H], F32)
+        nc.sync.dma_start(out=w1_raw0[:], in_=w1[0:PASS, :].rearrange("(p j) c -> p j c", j=PACK))
+        w1_raw00, w1_raw10 = w1_raw0[:, :, 0:PASS], w1_raw0[:, :, PASS:H]
+        tabw0 = load_words(placed("tabw0", [P, T], I32, TAB_WORDS0), tab_words[0])
 
         b1_sb = placed("b1_sb", [P, NPASS, PACK], F32, B1)
         b4_all = placed("b4_all", [P, NPASS, PACK], F32, STAGE_H0)
@@ -130,41 +131,35 @@ def tile_list_maxout_face_margins_kernel(
         )
 
         joint = held("joint", [P, JOINT], U8)
-        vs_picked = placed("vs_picked", [P, W1_RAW00 - TAB_WORDS1], U8, TAB_WORDS1)[:, 0:S]
-        nc.vector.tensor_copy(vs_picked, tabs[:].bitcast(U8).indirect(idx[:]))
+        vs_picked = held("vs_picked", [P, S], U8)
+        nc.vector.tensor_copy(vs_picked[:], tabs[:].bitcast(U8).indirect(idx[:]))
         nc.vector.tensor_copy(
-            out=joint[:, S:JOINT].rearrange("p (g t m) -> p g t m", g=NPASS, t=PACK),
+            out=joint[:, S : S + H].rearrange("p (g t m) -> p g t m", g=NPASS, t=PACK),
             in_=w4s_raw[:].bitcast(U8).rearrange("p (g m t) -> p g t m", g=NPASS, t=PACK),
         )
-        nc.vector.tensor_copy(out=joint[:, 0:S].bitcast(I32), in_=vs_picked.bitcast(I32))
+        nc.vector.tensor_copy(out=joint[:, 0:S].bitcast(I32), in_=vs_picked[:].bitcast(I32))
+        v2s_picked = placed("v2s_picked", [P, TAB_WORDS0], U8, W4_SCALES_RAW)[:, 0:S2]
+        nc.vector.tensor_copy(v2s_picked, tab2s[:].bitcast(U8).indirect(idx2[:]))
+        nc.vector.tensor_copy(out=joint[:, S + H : JOINT].bitcast(I32), in_=v2s_picked.bitcast(I32))
 
-        def move_planes(a, quads):
-            for quad in quads:
-                row = ROW0 + 16 * a + 4 * quad
-                nc.sync.dma_start(out=planes[a][32 * quad : 32 * quad + 4, :], in_=joint[row : row + 4, :].bitcast(I32))
+        def move_planes(a, rows):
+            for r in rows:
+                first = ROW0 + 16 * a + r
+                nc.sync.dma_start(out=planes[a][r:P:32, :], in_=joint[first : first + 13 : 4, :].bitcast(I32))
 
-        move_planes(0, range(QUADS))
-        tabw0 = load_words(placed("tabw0", [P, T], I32, TAB_WORDS0), tab_words[0])
+        move_planes(0, range(4))
+        w1_raw01 = load_w1(0, 1, placed("w1_raw01", [P, PACK, PASS], F32, W1_RAW10))
         move_planes(1, range(1))
-        w1_raw10 = load_w1(1, 0, placed("w1_raw10", [P, PACK, PASS], F32, W1_RAW10))
-        move_planes(1, range(1, QUADS))
         tabw1 = load_words(placed("tabw1", [P, T], I32, TAB_WORDS1), tab_words[1])
+        move_planes(1, range(1, 4))
         w1_raw11 = load_w1(1, 1, placed("w1_raw11", [P, PACK, PASS], F32, W1_RAW11))
         tab2w = [
             load_words(placed("tab2w0", [P, T2], I32, TAB2_WORDS0), tab2_words[0]),
-            load_words(placed("tab2w1", [P, T2], I32, W1_RAW10), tab2_words[1]),
+            load_words(placed("tab2w1", [P, T2], I32, TAB2_WORDS1), tab2_words[1]),
         ]
         vs = [planes[a][:].bitcast(U8)[:, 0:S] for a in range(NPASS)]
-        w4s = [planes[a][:].bitcast(U8)[:, S:JOINT] for a in range(NPASS)]
-
-        v2s_picked = placed("v2s_picked", [P, S2], U8, W4_SCALES_RAW)
-        nc.vector.tensor_copy(v2s_picked[:], tab2s[:].bitcast(U8).indirect(idx2[:]))
-        for g in range(NPASS):
-            for quad in range(QUADS):
-                row = ROW0 + 16 * g + 4 * quad
-                nc.gpsimd.dma_start(
-                    out=v2s[32 * quad + 4 * g : 32 * quad + 4 * g + 4, :], in_=v2s_picked[row : row + 4, :].bitcast(I32)
-                )
+        w4s = [planes[a][:].bitcast(U8)[:, S : S + H] for a in range(NPASS)]
+        v2s = [planes[a][:].bitcast(U8)[:, S + H : JOINT] for a in range(NPASS)]
 
         w4w = held("w4w", [P, NPASS, 2 * H], U8)
         w4w_to = w4w[:].rearrange("p a col -> p (a col)").bitcast(U16)
@@ -174,18 +169,17 @@ def tile_list_maxout_face_margins_kernel(
             in_=w4w_from.rearrange("p (ag m t) -> p ag t m", ag=NPASS * NPASS, t=PACK),
         )
 
-        w1_bf00 = held("w1_bf00", [P, PASS * PACK], BF16)
-        round_w1(nc.scalar.copy, w1_raw00, w1_bf00)
-        quantize_w1(0, 0, w1_bf00, held("w1_codes00", [P, PASS], U32), held("w1_scales00", [P, PASS], U8))
         vw = [held("vw0", [P, S], U32)]
         nc.vector.tensor_copy(vw[0][:], tabw0[:].bitcast(U32).indirect(idx[:]))
-        w1_bf01 = held("w1_bf01", [P, PASS * PACK], BF16)
-        round_w1(nc.scalar.copy, w1_raw01, w1_bf01)
-        quantize_w1(0, 1, w1_bf01, placed("w1_codes01", [P, PASS], U32, TAB_WORDS0), held("w1_scales01", [P, PASS], U8))
-
+        w1_bf00 = held("w1_bf00", [P, PASS * PACK], BF16)
+        round_w1(nc.scalar.copy, w1_raw00, w1_bf00)
+        quantize_w1(0, 0, w1_bf00, placed("w1_codes00", [P, PASS], U32, TAB_WORDS0), held("w1_scales00", [P, PASS], U8))
         w1_bf10 = held("w1_bf10", [P, PASS * PACK], BF16)
         round_w1(nc.scalar.copy, w1_raw10, w1_bf10)
-        vw.append(held("vw1", [P, S], U32))
+        w1_bf01 = held("w1_bf01", [P, PASS * PACK], BF16, "w1_bf00")
+        round_w1_vector(w1_raw01, w1_bf01)
+        quantize_w1(0, 1, w1_bf01, held("w1_codes01", [P, PASS], U32), held("w1_scales01", [P, PASS], U8))
+        vw.append(held("vw1", [P, S], U32, "w1_bf00"))
         nc.vector.tensor_copy(vw[1][:], tabw1[:].bitcast(U32).indirect(idx[:]))
         quantize_w1(1, 0, w1_bf10, placed("w1_codes10", [P, PASS], U32, TAB_WORDS1), held("w1_scales10", [P, PASS], U8))
         w1_bf11 = placed("w1_bf11", [P, PASS * PACK], BF16, STAGE_H1)
@@ -294,7 +288,7 @@ def tile_list_maxout_face_margins_kernel(
             nc.tensor.matmul_mx(
                 out=y_ps[i][:],
                 lhsT=v2w[g, i // HALF_TILES][:, col : col + P].bitcast(FP8X4),
-                lhsT_scale=v2s[4 * g : P, :].bitcast(U8)[:, i * P : (i + 1) * P],
+                lhsT_scale=v2s[g][:, i * P : (i + 1) * P],
                 rhs=h_codes[g][:].bitcast(FP8X4),
                 rhs_scale=h_scales[g][:],
                 start=(g == 0),

@@ -28,13 +28,13 @@ HALF = S2 // 2
 HALF_TILES = HALF // P
 GPSIMD_TILES = (1, 3)
 
-ROW0 = 96
-JOINT = S + H + S2
+ROW0, ROW0_V2 = 32, 96
+JOINT = S + H
 
 W4_SCALES_RAW, TAB_WORDS1 = 0, 1024
 STAGE_H1 = 73728
 STAGE_H0, B1 = 81920, 86016
-TAB2_WORDS0, W1_RAW11, W1_RAW10, TAB2_WORDS1, TAB_WORDS0 = 9216, 25600, 33792, 41984, 58368
+TAB2_WORDS0, W1_RAW11, W1_RAW10, TAB_WORDS0, W1_RAW0 = 9216, 25600, 33792, 41984, 50176
 
 
 def tile_list_maxout_face_margins_kernel(
@@ -92,27 +92,29 @@ def tile_list_maxout_face_margins_kernel(
         w4s_raw = placed("w4s_raw", [P, H // 4], I32, W4_SCALES_RAW)
         tab2s = held("tab2s", [P, T2 // 4], I32)
         planes = [held("planes%d" % a, [P, JOINT // 4], I32) for a in range(NPASS)]
-        for staged in (tabs, w4s_raw, tab2s):
+        v2s = held("v2s", [P, S2 // 4], I32)
+        for staged in (tabs, w4s_raw):
             nc.vector.memset(staged[0:ROW0, :], 0)
-        for tile in planes:
+            nc.vector.memset(staged[ROW0 + 32 : P, :], 0)
+        nc.vector.memset(tab2s[0:ROW0_V2, :], 0)
+        for tile in planes + [v2s]:
             nc.vector.memset(tile[:], 0)
 
-        def load_scales(dst, src):
-            nc.sync.dma_start(out=dst[ROW0:P, :], in_=src.bitcast(I32).rearrange("a q col -> (a q) col"))
+        def load_scales(dst, src, row0):
+            nc.sync.dma_start(out=dst[row0 : row0 + 32, :], in_=src.bitcast(I32).rearrange("a q col -> (a q) col"))
 
         w4w_raw = held("w4w_raw", [P, NPASS, H // 2], I32)
         nc.sync.dma_start(idx[:], offs)
-        load_scales(tabs, tab_scales)
-        load_scales(w4s_raw, w4_scales)
+        load_scales(tabs, tab_scales, ROW0)
+        load_scales(tab2s, tab2_scales, ROW0_V2)
+        load_scales(w4s_raw, w4_scales, ROW0)
         nc.sync.dma_start(idx2[:], offs2)
-        load_scales(tab2s, tab2_scales)
         thr_sb = held("thr_sb", [P, PACK], F32)
         nc.sync.dma_start(out=thr_sb[:], in_=thr.rearrange("(p c) -> p c", c=PACK))
         nc.sync.dma_start(out=w4w_raw[:], in_=w4_words.bitcast(I32).rearrange("a p col -> p a col"))
-        w1_raw0 = held("w1_raw0", [P, PACK, H], F32)
+        w1_raw0 = placed("w1_raw0", [P, PACK, H], F32, W1_RAW0)
         nc.sync.dma_start(out=w1_raw0[:], in_=w1[0:PASS, :].rearrange("(p j) c -> p j c", j=PACK))
         w1_raw00, w1_raw10 = w1_raw0[:, :, 0:PASS], w1_raw0[:, :, PASS:H]
-        tabw0 = load_words(placed("tabw0", [P, T], I32, TAB_WORDS0), tab_words[0])
 
         b1_sb = placed("b1_sb", [P, NPASS, PACK], F32, B1)
         b4_all = placed("b4_all", [P, NPASS, PACK], F32, STAGE_H0)
@@ -131,16 +133,13 @@ def tile_list_maxout_face_margins_kernel(
         )
 
         joint = held("joint", [P, JOINT], U8)
-        vs_picked = held("vs_picked", [P, S], U8)
-        nc.vector.tensor_copy(vs_picked[:], tabs[:].bitcast(U8).indirect(idx[:]))
+        vs_picked = placed("vs_picked", [P, W1_RAW0 - TAB_WORDS1], U8, TAB_WORDS1)[:, 0:S]
+        nc.vector.tensor_copy(vs_picked, tabs[:].bitcast(U8).indirect(idx[:]))
         nc.vector.tensor_copy(
             out=joint[:, S : S + H].rearrange("p (g t m) -> p g t m", g=NPASS, t=PACK),
             in_=w4s_raw[:].bitcast(U8).rearrange("p (g m t) -> p g t m", g=NPASS, t=PACK),
         )
-        nc.vector.tensor_copy(out=joint[:, 0:S].bitcast(I32), in_=vs_picked[:].bitcast(I32))
-        v2s_picked = placed("v2s_picked", [P, TAB_WORDS0], U8, W4_SCALES_RAW)[:, 0:S2]
-        nc.vector.tensor_copy(v2s_picked, tab2s[:].bitcast(U8).indirect(idx2[:]))
-        nc.vector.tensor_copy(out=joint[:, S + H : JOINT].bitcast(I32), in_=v2s_picked.bitcast(I32))
+        nc.vector.tensor_copy(out=joint[:, 0:S].bitcast(I32), in_=vs_picked.bitcast(I32))
 
         def move_planes(a, rows):
             for r in rows:
@@ -148,18 +147,26 @@ def tile_list_maxout_face_margins_kernel(
                 nc.sync.dma_start(out=planes[a][r:P:32, :], in_=joint[first : first + 13 : 4, :].bitcast(I32))
 
         move_planes(0, range(4))
-        w1_raw01 = load_w1(0, 1, placed("w1_raw01", [P, PACK, PASS], F32, W1_RAW10))
+        tabw0 = load_words(placed("tabw0", [P, T], I32, TAB_WORDS0), tab_words[0])
         move_planes(1, range(1))
-        tabw1 = load_words(placed("tabw1", [P, T], I32, TAB_WORDS1), tab_words[1])
+        w1_raw01 = load_w1(0, 1, placed("w1_raw01", [P, PACK, PASS], F32, W1_RAW10))
         move_planes(1, range(1, 4))
+        tabw1 = load_words(placed("tabw1", [P, T], I32, TAB_WORDS1), tab_words[1])
         w1_raw11 = load_w1(1, 1, placed("w1_raw11", [P, PACK, PASS], F32, W1_RAW11))
         tab2w = [
             load_words(placed("tab2w0", [P, T2], I32, TAB2_WORDS0), tab2_words[0]),
-            load_words(placed("tab2w1", [P, T2], I32, TAB2_WORDS1), tab2_words[1]),
+            load_words(placed("tab2w1", [P, T2], I32, W1_RAW0), tab2_words[1]),
         ]
         vs = [planes[a][:].bitcast(U8)[:, 0:S] for a in range(NPASS)]
         w4s = [planes[a][:].bitcast(U8)[:, S : S + H] for a in range(NPASS)]
-        v2s = [planes[a][:].bitcast(U8)[:, S + H : JOINT] for a in range(NPASS)]
+
+        v2s_picked = placed("v2s_picked", [P, S2], U8, W4_SCALES_RAW)
+        nc.vector.tensor_copy(v2s_picked[:], tab2s[:].bitcast(U8).indirect(idx2[:]))
+        for g in range(NPASS):
+            for quad in range(QUADS):
+                row = ROW0_V2 + 16 * g + 4 * quad
+                to = 32 * quad + 4 * (g + 1)
+                nc.gpsimd.dma_start(out=v2s[to : to + 4, :], in_=v2s_picked[row : row + 4, :].bitcast(I32))
 
         w4w = held("w4w", [P, NPASS, 2 * H], U8)
         w4w_to = w4w[:].rearrange("p a col -> p (a col)").bitcast(U16)
@@ -288,7 +295,7 @@ def tile_list_maxout_face_margins_kernel(
             nc.tensor.matmul_mx(
                 out=y_ps[i][:],
                 lhsT=v2w[g, i // HALF_TILES][:, col : col + P].bitcast(FP8X4),
-                lhsT_scale=v2s[g][:, i * P : (i + 1) * P],
+                lhsT_scale=v2s[4 * (g + 1) : P, :].bitcast(U8)[:, i * P : (i + 1) * P],
                 rhs=h_codes[g][:].bitcast(FP8X4),
                 rhs_scale=h_scales[g][:],
                 start=(g == 0),

@@ -149,9 +149,9 @@ def tile_list_maxout_face_margins_kernel(
         move_planes(0, range(4))
         tabw0 = load_words(placed("tabw0", [P, T], I32, TAB_WORDS0), tab_words[0])
         move_planes(1, range(1))
-        w1_raw01 = load_w1(0, 1, placed("w1_raw01", [P, PACK, PASS], F32, W1_RAW10))
-        move_planes(1, range(1, 4))
         tabw1 = load_words(placed("tabw1", [P, T], I32, TAB_WORDS1), tab_words[1])
+        move_planes(1, range(1, 4))
+        w1_raw01 = load_w1(0, 1, placed("w1_raw01", [P, PACK, PASS], F32, W1_RAW10))
         w1_raw11 = load_w1(1, 1, placed("w1_raw11", [P, PACK, PASS], F32, W1_RAW11))
         tab2w = [
             load_words(placed("tab2w0", [P, T2], I32, TAB2_WORDS0), tab2_words[0]),
@@ -181,31 +181,30 @@ def tile_list_maxout_face_margins_kernel(
         w1_bf00 = held("w1_bf00", [P, PASS * PACK], BF16)
         round_w1(nc.scalar.copy, w1_raw00, w1_bf00)
         quantize_w1(0, 0, w1_bf00, placed("w1_codes00", [P, PASS], U32, TAB_WORDS0), held("w1_scales00", [P, PASS], U8))
+        vw.append(held("vw1", [P, S], U32))
+        nc.vector.tensor_copy(vw[1][:], tabw1[:].bitcast(U32).indirect(idx[:]))
         w1_bf10 = held("w1_bf10", [P, PASS * PACK], BF16)
         round_w1(nc.scalar.copy, w1_raw10, w1_bf10)
-        w1_bf01 = held("w1_bf01", [P, PASS * PACK], BF16, "w1_bf00")
+        quantize_w1(1, 0, w1_bf10, placed("w1_codes10", [P, PASS], U32, TAB_WORDS1), held("w1_scales10", [P, PASS], U8))
+        w1_bf01 = held("w1_bf01", [P, PASS * PACK], BF16, "w1_bf10")
         round_w1_vector(w1_raw01, w1_bf01)
         quantize_w1(0, 1, w1_bf01, held("w1_codes01", [P, PASS], U32), held("w1_scales01", [P, PASS], U8))
-        vw.append(held("vw1", [P, S], U32, "w1_bf00"))
-        nc.vector.tensor_copy(vw[1][:], tabw1[:].bitcast(U32).indirect(idx[:]))
-        quantize_w1(1, 0, w1_bf10, placed("w1_codes10", [P, PASS], U32, TAB_WORDS1), held("w1_scales10", [P, PASS], U8))
-        w1_bf11 = placed("w1_bf11", [P, PASS * PACK], BF16, STAGE_H1)
+        w1_bf11 = held("w1_bf11", [P, PASS * PACK], BF16)
         round_w1_vector(w1_raw11, w1_bf11)
-        quantize_w1(1, 1, w1_bf11, held("w1_codes11", [P, PASS], U32), held("w1_scales11", [P, PASS], U8))
 
-        h_planes = [placed("h_planes0", [P, PACK, S], BF16, STAGE_H1), held("h_planes1", [P, PACK, S], BF16)]
+        h_planes = [placed("h_planes0", [P, PACK, S], BF16, W1_RAW11), held("h_planes1", [P, PACK, S], BF16)]
         h_bf = []
         h_codes = []
 
-        def project_a(g, t, a, a_ps):
+        def project_a(g, t, a, a_ps, first):
             nc.tensor.matmul_mx(
                 out=a_ps[:],
                 lhsT=w1_codes[g, a][:, t * P : (t + 1) * P].bitcast(FP8X4),
                 lhsT_scale=w1_scales[g, a][:, t * P : (t + 1) * P],
                 rhs=vw[a][:].bitcast(FP8X4),
                 rhs_scale=vs[a],
-                start=(a == 0),
-                stop=(a == NPASS - 1),
+                start=first,
+                stop=not first,
             )
 
         def project_c(g, t, a, c_ps):
@@ -246,36 +245,36 @@ def tile_list_maxout_face_margins_kernel(
                 dst[:], tab2w[g][:].bitcast(U32).indirect(idx2[:, half * HALF // 16 : (half + 1) * HALF // 16])
             )
 
-        a_ps = [bank(t) for t in range(PACK)]
-        c_ps = [bank(PACK + t) for t in range(PACK)]
-        for t in range(PACK):
-            project_a(0, t, 0, a_ps[t])
-            project_c(0, t, 0, c_ps[t])
-        a_sb = []
-        for t in range(PACK):
-            project_a(0, t, 1, a_ps[t])
-            a_sb.append(bring_out("a_sb%d" % t, a_ps[t], b1_sb[:, 0, t : t + 1]))
-        for t in range(PACK):
-            project_c(0, t, 1, c_ps[t])
-        c0_ps = c_ps
-
         c_ps = [bank(t) for t in range(PACK)]
-        c_sb = []
-        for t in range(PACK):
-            for a in range(NPASS):
-                project_c(1, t, a, c_ps[t])
-            c_sb.append(bring_out("c_sb%d" % t, c_ps[t], b4_sb[1][:, t : t + 1]))
-        for t in range(PACK):
-            take_max(0, t, c0_ps[t], b4_sb[0][:, t : t + 1], a_sb[t])
         a_ps = [bank(PACK + t) for t in range(PACK)]
         for t in range(PACK):
+            project_c(0, t, 0, c_ps[t])
+        for t in range(PACK):
+            project_a(0, t, 0, a_ps[t], True)
+        c0_sb = []
+        for t in range(PACK):
+            project_c(0, t, 1, c_ps[t])
+            c0_sb.append(bring_out("c0_sb%d" % t, c_ps[t], b4_sb[0][:, t : t + 1]))
+        for t in range(PACK):
+            project_a(0, t, 1, a_ps[t], False)
+            take_max(0, t, a_ps[t], b1_sb[:, 0, t : t + 1], c0_sb[t])
+            if t == 0:
+                quantize_w1(1, 1, w1_bf11, held("w1_codes11", [P, PASS], U32), held("w1_scales11", [P, PASS], U8))
+        c_sb = []
+        for t in range(PACK):
+            c_ps = bank(t)
             for a in range(NPASS):
-                project_a(1, t, a, a_ps[t])
-            take_max(1, t, a_ps[t], b1_sb[:, 1, t : t + 1], c_sb[t])
+                project_c(1, t, a, c_ps)
+            c_sb.append(bring_out("c_sb%d" % t, c_ps, b4_sb[1][:, t : t + 1]))
+        for t in range(PACK):
+            a_ps = bank(PACK + t)
+            project_a(1, t, 0, a_ps, True)
+            project_a(1, t, 1, a_ps, False)
+            take_max(1, t, a_ps, b1_sb[:, 1, t : t + 1], c_sb[t])
 
         h_bf.append(placed("h_bf0", [P, S * PACK], BF16, STAGE_H0))
         interleave_h(0)
-        h_bf.append(placed("h_bf1", [P, S * PACK], BF16, STAGE_H1))
+        h_bf.append(placed("h_bf1", [P, S * PACK], BF16, W1_RAW11))
         interleave_h(1)
 
         h_scales = [placed("h_scales0", [P, S], U8, B1), held("h_scales1", [P, S], U8)]
@@ -286,7 +285,7 @@ def tile_list_maxout_face_margins_kernel(
         h_codes.append(placed("h_codes1", [P, S], U32, TAB2_WORDS0))
         gather_v2(1, 0, placed("v2w10", [P, HALF], U32, TAB2_WORDS0 + 4 * S))
         quantize_h(1)
-        gather_v2(1, 1, placed("v2w11", [P, HALF], U32, STAGE_H1))
+        gather_v2(1, 1, placed("v2w11", [P, HALF], U32, W1_RAW11))
 
         y_ps = [bank(i) for i in range(OUT_TILES)]
 

@@ -68,24 +68,32 @@ def tile_list_maxout_face_margins_kernel(
             nc.sync.dma_start(out=dst[:], in_=words.rearrange("p col j -> p (col j)").bitcast(I32))
             return dst
 
-        def round_w1(copy, raw, dst):
-            copy(
-                out=dst[:].rearrange("p (t m j) -> p m t j", t=PACK, j=PACK),
-                in_=raw.rearrange("p j (m t) -> p m t j", t=PACK),
+        def round_w1(raw, dst):
+            nc.scalar.copy(
+                out=dst[:].rearrange("p (th tl m j) -> p th m j tl", th=2, tl=2, j=PACK),
+                in_=raw.rearrange("p j (m th tl) -> p th m j tl", th=2, tl=2),
             )
 
-        def round_w1_vector(raw, dst):
-            nc.vector.tensor_copy(
-                out=dst[:].rearrange("p (th tl m j) -> p th m tl j", th=2, tl=2, j=PACK),
-                in_=raw.rearrange("p j (m th tl) -> p th m tl j", th=2, tl=2),
+        def round_half(copy, raw, th, dst):
+            copy(
+                out=dst[:].rearrange("p (tl m j) -> p m j tl", tl=2, j=PACK),
+                in_=raw.rearrange("p j (m th tl) -> p th m j tl", th=2, tl=2)[:, th],
             )
 
         w1_codes = {}
         w1_scales = {}
 
         def quantize_w1(g, a, src, codes, scales):
-            w1_codes.setdefault((g, a), codes)
-            w1_scales.setdefault((g, a), scales)
+            for th in range(2):
+                w1_codes.setdefault((g, a, th), codes[:, th * 2 * P : (th + 1) * 2 * P])
+                w1_scales.setdefault((g, a, th), scales[:, th * 2 * P : (th + 1) * 2 * P])
+            nc.vector.quantize_mx(out=codes[:].bitcast(FP8X4), scales=scales[:], in_=src[:])
+
+        def quantize_half(g, th, src):
+            codes = held("w1_codes%d1%d" % (g, th), [P, 2 * P], U32)
+            scales = held("w1_scales%d1%d" % (g, th), [P, 2 * P], U8)
+            w1_codes.setdefault((g, 1, th), codes[:])
+            w1_scales.setdefault((g, 1, th), scales[:])
             nc.vector.quantize_mx(out=codes[:].bitcast(FP8X4), scales=scales[:], in_=src[:])
 
         tabs = held("tabs", [P, T // 4], I32)
@@ -179,28 +187,29 @@ def tile_list_maxout_face_margins_kernel(
         vw = [held("vw0", [P, S], U32)]
         nc.vector.tensor_copy(vw[0][:], tabw0[:].bitcast(U32).indirect(idx[:]))
         w1_bf00 = held("w1_bf00", [P, PASS * PACK], BF16)
-        round_w1(nc.scalar.copy, w1_raw00, w1_bf00)
+        round_w1(w1_raw00, w1_bf00)
         quantize_w1(0, 0, w1_bf00, placed("w1_codes00", [P, PASS], U32, TAB_WORDS0), held("w1_scales00", [P, PASS], U8))
         vw.append(held("vw1", [P, S], U32))
         nc.vector.tensor_copy(vw[1][:], tabw1[:].bitcast(U32).indirect(idx[:]))
         w1_bf10 = held("w1_bf10", [P, PASS * PACK], BF16)
-        round_w1(nc.scalar.copy, w1_raw10, w1_bf10)
+        round_w1(w1_raw10, w1_bf10)
         quantize_w1(1, 0, w1_bf10, placed("w1_codes10", [P, PASS], U32, TAB_WORDS1), held("w1_scales10", [P, PASS], U8))
-        w1_bf01 = held("w1_bf01", [P, PASS * PACK], BF16, "w1_bf10")
-        round_w1_vector(w1_raw01, w1_bf01)
-        quantize_w1(0, 1, w1_bf01, held("w1_codes01", [P, PASS], U32), held("w1_scales01", [P, PASS], U8))
-        w1_bf11 = held("w1_bf11", [P, PASS * PACK], BF16)
-        round_w1_vector(w1_raw11, w1_bf11)
+        w1_bf01 = [held("w1_bf01%d" % th, [P, 2 * PASS], BF16) for th in range(2)]
+        w1_bf11 = [held("w1_bf11%d" % th, [P, 2 * PASS], BF16) for th in range(2)]
+        for th in range(2):
+            round_half(nc.vector.tensor_copy, w1_raw01, th, w1_bf01[th])
+        for th in range(2):
+            quantize_half(0, th, w1_bf01[th])
 
-        h_planes = [placed("h_planes0", [P, PACK, S], BF16, W1_RAW11), held("h_planes1", [P, PACK, S], BF16)]
+        h_planes = [held("h_planes%d" % g, [P, PACK, S], BF16) for g in range(NPASS)]
         h_bf = []
         h_codes = []
 
         def project_a(g, t, a, a_ps, first):
             nc.tensor.matmul_mx(
                 out=a_ps[:],
-                lhsT=w1_codes[g, a][:, t * P : (t + 1) * P].bitcast(FP8X4),
-                lhsT_scale=w1_scales[g, a][:, t * P : (t + 1) * P],
+                lhsT=w1_codes[g, a, t // 2][:, (t % 2) * P : (t % 2 + 1) * P].bitcast(FP8X4),
+                lhsT_scale=w1_scales[g, a, t // 2][:, (t % 2) * P : (t % 2 + 1) * P],
                 rhs=vw[a][:].bitcast(FP8X4),
                 rhs_scale=vs[a],
                 start=first,
@@ -255,37 +264,40 @@ def tile_list_maxout_face_margins_kernel(
         for t in range(PACK):
             project_c(0, t, 1, c_ps[t])
             c0_sb.append(bring_out("c0_sb%d" % t, c_ps[t], b4_sb[0][:, t : t + 1]))
+        round_half(nc.scalar.copy, w1_raw11, 1, w1_bf11[1])
+        round_half(nc.vector.tensor_copy, w1_raw11, 0, w1_bf11[0])
         for t in range(PACK):
             project_a(0, t, 1, a_ps[t], False)
             take_max(0, t, a_ps[t], b1_sb[:, 0, t : t + 1], c0_sb[t])
-            if t == 0:
-                quantize_w1(1, 1, w1_bf11, held("w1_codes11", [P, PASS], U32), held("w1_scales11", [P, PASS], U8))
+            if t % 2 == 1:
+                quantize_half(1, t // 2, w1_bf11[t // 2])
         c_sb = []
         for t in range(PACK):
-            c_ps = bank(t)
+            c_ps = bank(t if t < 2 else t + 2)
             for a in range(NPASS):
                 project_c(1, t, a, c_ps)
             c_sb.append(bring_out("c_sb%d" % t, c_ps, b4_sb[1][:, t : t + 1]))
         for t in range(PACK):
-            a_ps = bank(PACK + t)
-            project_a(1, t, 0, a_ps, True)
-            project_a(1, t, 1, a_ps, False)
+            a_ps = bank(t + 2 if t < 2 else t + 4)
+            first = 1 if t < 2 else 0
+            project_a(1, t, first, a_ps, True)
+            project_a(1, t, 1 - first, a_ps, False)
             take_max(1, t, a_ps, b1_sb[:, 1, t : t + 1], c_sb[t])
 
         h_bf.append(placed("h_bf0", [P, S * PACK], BF16, STAGE_H0))
         interleave_h(0)
-        h_bf.append(placed("h_bf1", [P, S * PACK], BF16, W1_RAW11))
+        h_bf.append(held("h_bf1", [P, S * PACK], BF16, "h_planes0"))
         interleave_h(1)
 
-        h_scales = [placed("h_scales0", [P, S], U8, B1), held("h_scales1", [P, S], U8)]
-        gather_v2(0, 0, held("v2w00", [P, HALF], U32, "c_sb%d" % (PACK - 1)))
+        h_scales = [held("h_scales%d" % g, [P, S], U8) for g in range(NPASS)]
+        gather_v2(0, 0, held("v2w00", [P, HALF], U32, "c_sb%d" % (PACK - 2)))
         h_codes.append(held("h_codes0", [P, S], U32))
         quantize_h(0)
-        gather_v2(0, 1, placed("v2w01", [P, HALF], U32, STAGE_H0))
-        h_codes.append(placed("h_codes1", [P, S], U32, TAB2_WORDS0))
-        gather_v2(1, 0, placed("v2w10", [P, HALF], U32, TAB2_WORDS0 + 4 * S))
+        gather_v2(0, 1, held("v2w01", [P, HALF], U32, "c_sb%d" % (PACK - 1)))
+        h_codes.append(held("h_codes1", [P, S], U32))
         quantize_h(1)
-        gather_v2(1, 1, placed("v2w11", [P, HALF], U32, W1_RAW11))
+        gather_v2(1, 0, held("v2w10", [P, HALF], U32))
+        gather_v2(1, 1, held("v2w11", [P, HALF], U32))
 
         y_ps = [bank(i) for i in range(OUT_TILES)]
 

@@ -22,6 +22,9 @@ PACK = 4
 PASS = P * PACK
 NPASS = 2
 QUADS = 4
+HALVES = 2
+HALF_COLS = PASS // HALVES
+ROWS = 16
 RUN = 4
 OUT_TILES = S2 // P
 HALF = S2 // 2
@@ -31,10 +34,18 @@ GPSIMD_TILES = (1, 3)
 ROW0, ROW0_V2 = 32, 96
 JOINT = S + H
 
-W4_SCALES_RAW, TAB_WORDS1 = 0, 1024
-STAGE_H1 = 73728
-STAGE_H0, B1 = 81920, 86016
-TAB2_WORDS0, W1_RAW11, W1_RAW10, TAB_WORDS0, W1_RAW0 = 9216, 25600, 33792, 41984, 50176
+W4_SCALES_RAW = 0
+TAB_WORDS1 = W4_SCALES_RAW + H
+W1_RAW11 = TAB_WORDS1 + 4 * T
+W1_RAW01 = W1_RAW11 + 4 * PACK * PASS
+TAB_WORDS0 = W1_RAW01 + 4 * PACK * PASS
+W1_RAW0 = TAB_WORDS0 + 4 * T
+TAB2_WORDS0 = W1_RAW0 + 4 * PACK * H
+H_BF0 = TAB2_WORDS0 + 4 * T2
+
+C1_BANKS = (0, 4, 5, 6)
+A1_BANKS = (1, 2, 3, 7)
+A1_FIRST_PASS = (0, 1, 1, 0)
 
 
 def tile_list_maxout_face_margins_kernel(
@@ -70,46 +81,51 @@ def tile_list_maxout_face_margins_kernel(
 
         def round_w1(raw, dst):
             nc.scalar.copy(
-                out=dst[:].rearrange("p (th tl m j) -> p th m j tl", th=2, tl=2, j=PACK),
-                in_=raw.rearrange("p j (m th tl) -> p th m j tl", th=2, tl=2),
+                out=dst[:].rearrange("p (th tl m j) -> p th m j tl", th=HALVES, tl=2, j=PACK),
+                in_=raw.rearrange("p j (m th tl) -> p th m j tl", th=HALVES, tl=2),
             )
 
         def round_half(copy, raw, th, dst):
             copy(
                 out=dst[:].rearrange("p (tl m j) -> p m j tl", tl=2, j=PACK),
-                in_=raw.rearrange("p j (m th tl) -> p th m j tl", th=2, tl=2)[:, th],
+                in_=raw.rearrange("p j (m th tl) -> p th m j tl", th=HALVES, tl=2)[:, th],
             )
+
+        def gpsimd_copy(out_view, in_view):
+            nc.gpsimd.tensor_scalar(out=out_view, in0=in_view, scalar1=1.0, scalar2=0.0, op0=ALU.mult, op1=ALU.add)
 
         w1_codes = {}
         w1_scales = {}
 
-        def quantize_w1(g, a, src, codes, scales):
-            for th in range(2):
-                w1_codes.setdefault((g, a, th), codes[:, th * 2 * P : (th + 1) * 2 * P])
-                w1_scales.setdefault((g, a, th), scales[:, th * 2 * P : (th + 1) * 2 * P])
+        def quantize_w1(g, src, codes):
+            scales = held("w1_scales%d0" % g, [P, PASS], U8)
+            for th in range(HALVES):
+                w1_codes.setdefault((g, 0, th), codes[:, th * HALF_COLS : (th + 1) * HALF_COLS])
+                w1_scales.setdefault((g, 0, th), scales[:, th * HALF_COLS : (th + 1) * HALF_COLS])
             nc.vector.quantize_mx(out=codes[:].bitcast(FP8X4), scales=scales[:], in_=src[:])
 
         def quantize_half(g, th, src):
-            codes = held("w1_codes%d1%d" % (g, th), [P, 2 * P], U32)
-            scales = held("w1_scales%d1%d" % (g, th), [P, 2 * P], U8)
+            codes = held("w1_codes%d1%d" % (g, th), [P, HALF_COLS], U32)
+            scales = held("w1_scales%d1%d" % (g, th), [P, HALF_COLS], U8)
             w1_codes.setdefault((g, 1, th), codes[:])
             w1_scales.setdefault((g, 1, th), scales[:])
             nc.vector.quantize_mx(out=codes[:].bitcast(FP8X4), scales=scales[:], in_=src[:])
 
         tabs = held("tabs", [P, T // 4], I32)
         w4s_raw = placed("w4s_raw", [P, H // 4], I32, W4_SCALES_RAW)
-        tab2s = held("tab2s", [P, T2 // 4], I32)
+        tab2s = placed("tab2s", [P, T2 // 4], I32, TAB2_WORDS0)
         planes = [held("planes%d" % a, [P, JOINT // 4], I32) for a in range(NPASS)]
         v2s = held("v2s", [P, S2 // 4], I32)
         for staged in (tabs, w4s_raw):
             nc.vector.memset(staged[0:ROW0, :], 0)
-            nc.vector.memset(staged[ROW0 + 32 : P, :], 0)
+            nc.vector.memset(staged[ROW0 + NPASS * ROWS : P, :], 0)
         nc.vector.memset(tab2s[0:ROW0_V2, :], 0)
         for tile in planes + [v2s]:
             nc.vector.memset(tile[:], 0)
 
         def load_scales(dst, src, row0):
-            nc.sync.dma_start(out=dst[row0 : row0 + 32, :], in_=src.bitcast(I32).rearrange("a q col -> (a q) col"))
+            rows = src.bitcast(I32).rearrange("a q col -> (a q) col")
+            nc.sync.dma_start(out=dst[row0 : row0 + NPASS * ROWS, :], in_=rows)
 
         w4w_raw = held("w4w_raw", [P, NPASS, H // 2], I32)
         nc.sync.dma_start(idx[:], offs)
@@ -124,11 +140,10 @@ def tile_list_maxout_face_margins_kernel(
         nc.sync.dma_start(out=w1_raw0[:], in_=w1[0:PASS, :].rearrange("(p j) c -> p j c", j=PACK))
         w1_raw00, w1_raw10 = w1_raw0[:, :, 0:PASS], w1_raw0[:, :, PASS:H]
 
-        b1_sb = placed("b1_sb", [P, NPASS, PACK], F32, B1)
-        b4_all = placed("b4_all", [P, NPASS, PACK], F32, STAGE_H0)
-        b4_sb = [b4_all[:, 0, :], b4_all[:, 1, :]]
+        b1_sb = held("b1_sb", [P, NPASS, PACK], F32)
+        b4_sb = held("b4_sb", [P, NPASS, PACK], F32)
         nc.gpsimd.dma_start(out=b1_sb[:], in_=b1.rearrange("(g p t) -> p g t", g=NPASS, t=PACK))
-        nc.gpsimd.dma_start(out=b4_all[:], in_=b4.rearrange("(g p t) -> p g t", g=NPASS, t=PACK))
+        nc.gpsimd.dma_start(out=b4_sb[:], in_=b4.rearrange("(g p t) -> p g t", g=NPASS, t=PACK))
         ident = held("ident", [P, P], F32)
         make_identity(nc, ident[:])
 
@@ -151,30 +166,29 @@ def tile_list_maxout_face_margins_kernel(
 
         def move_planes(a, rows):
             for r in rows:
-                first = ROW0 + 16 * a + r
-                nc.sync.dma_start(out=planes[a][r:P:32, :], in_=joint[first : first + 13 : 4, :].bitcast(I32))
+                first = ROW0 + ROWS * a + r
+                staged_rows = joint[first : first + ROWS - 3 : 4, :]
+                nc.sync.dma_start(out=planes[a][r:P:32, :], in_=staged_rows.bitcast(I32))
 
         move_planes(0, range(4))
         tabw0 = load_words(placed("tabw0", [P, T], I32, TAB_WORDS0), tab_words[0])
         move_planes(1, range(1))
         tabw1 = load_words(placed("tabw1", [P, T], I32, TAB_WORDS1), tab_words[1])
         move_planes(1, range(1, 4))
-        w1_raw01 = load_w1(0, 1, placed("w1_raw01", [P, PACK, PASS], F32, W1_RAW10))
+        w1_raw01 = load_w1(0, 1, placed("w1_raw01", [P, PACK, PASS], F32, W1_RAW01))
         w1_raw11 = load_w1(1, 1, placed("w1_raw11", [P, PACK, PASS], F32, W1_RAW11))
-        tab2w = [
-            load_words(placed("tab2w0", [P, T2], I32, TAB2_WORDS0), tab2_words[0]),
-            load_words(placed("tab2w1", [P, T2], I32, W1_RAW0), tab2_words[1]),
-        ]
         vs = [planes[a][:].bitcast(U8)[:, 0:S] for a in range(NPASS)]
         w4s = [planes[a][:].bitcast(U8)[:, S : S + H] for a in range(NPASS)]
 
         v2s_picked = placed("v2s_picked", [P, S2], U8, W4_SCALES_RAW)
         nc.vector.tensor_copy(v2s_picked[:], tab2s[:].bitcast(U8).indirect(idx2[:]))
-        for g in range(NPASS):
+        tab2w = []
+        for g, offset in enumerate((TAB2_WORDS0, W1_RAW0)):
             for quad in range(QUADS):
-                row = ROW0_V2 + 16 * g + 4 * quad
+                row = ROW0_V2 + ROWS * g + 4 * quad
                 to = 32 * quad + 4 * (g + 1)
-                nc.gpsimd.dma_start(out=v2s[to : to + 4, :], in_=v2s_picked[row : row + 4, :].bitcast(I32))
+                nc.sync.dma_start(out=v2s[to : to + 4, :], in_=v2s_picked[row : row + 4, :].bitcast(I32))
+            tab2w.append(load_words(placed("tab2w%d" % g, [P, T2], I32, offset), tab2_words[g]))
 
         w4w = held("w4w", [P, NPASS, 2 * H], U8)
         w4w_to = w4w[:].rearrange("p a col -> p (a col)").bitcast(U16)
@@ -188,28 +202,31 @@ def tile_list_maxout_face_margins_kernel(
         nc.vector.tensor_copy(vw[0][:], tabw0[:].bitcast(U32).indirect(idx[:]))
         w1_bf00 = held("w1_bf00", [P, PASS * PACK], BF16)
         round_w1(w1_raw00, w1_bf00)
-        quantize_w1(0, 0, w1_bf00, placed("w1_codes00", [P, PASS], U32, TAB_WORDS0), held("w1_scales00", [P, PASS], U8))
+        quantize_w1(0, w1_bf00, placed("w1_codes00", [P, PASS], U32, TAB_WORDS0))
         vw.append(held("vw1", [P, S], U32))
         nc.vector.tensor_copy(vw[1][:], tabw1[:].bitcast(U32).indirect(idx[:]))
         w1_bf10 = held("w1_bf10", [P, PASS * PACK], BF16)
         round_w1(w1_raw10, w1_bf10)
-        quantize_w1(1, 0, w1_bf10, placed("w1_codes10", [P, PASS], U32, TAB_WORDS1), held("w1_scales10", [P, PASS], U8))
-        w1_bf01 = [held("w1_bf01%d" % th, [P, 2 * PASS], BF16) for th in range(2)]
-        w1_bf11 = [held("w1_bf11%d" % th, [P, 2 * PASS], BF16) for th in range(2)]
-        for th in range(2):
-            round_half(nc.vector.tensor_copy, w1_raw01, th, w1_bf01[th])
-        for th in range(2):
+        quantize_w1(1, w1_bf10, placed("w1_codes10", [P, PASS], U32, TAB_WORDS1))
+        w1_bf01 = [held("w1_bf01%d" % th, [P, HALF_COLS * PACK], BF16) for th in range(HALVES)]
+        for th, copy in enumerate((nc.vector.tensor_copy, nc.scalar.copy)):
+            round_half(copy, w1_raw01, th, w1_bf01[th])
+        for th in range(HALVES):
             quantize_half(0, th, w1_bf01[th])
+        w1_bf11 = [
+            held("w1_bf110", [P, HALF_COLS * PACK], BF16, "w1_bf011"),
+            placed("w1_bf111", [P, HALF_COLS * PACK], BF16, H_BF0),
+        ]
 
         h_planes = [held("h_planes%d" % g, [P, PACK, S], BF16) for g in range(NPASS)]
-        h_bf = []
         h_codes = []
 
         def project_a(g, t, a, a_ps, first):
+            th, tl = divmod(t, 2)
             nc.tensor.matmul_mx(
                 out=a_ps[:],
-                lhsT=w1_codes[g, a, t // 2][:, (t % 2) * P : (t % 2 + 1) * P].bitcast(FP8X4),
-                lhsT_scale=w1_scales[g, a, t // 2][:, (t % 2) * P : (t % 2 + 1) * P],
+                lhsT=w1_codes[g, a, th][:, tl * P : (tl + 1) * P].bitcast(FP8X4),
+                lhsT_scale=w1_scales[g, a, th][:, tl * P : (tl + 1) * P],
                 rhs=vw[a][:].bitcast(FP8X4),
                 rhs_scale=vs[a],
                 start=first,
@@ -228,8 +245,7 @@ def tile_list_maxout_face_margins_kernel(
                 stop=(a == NPASS - 1),
             )
 
-        def bring_out(name, ps, bias):
-            sb = held(name, [P, S], F32)
+        def bring_out(sb, ps, bias):
             nc.scalar.activation(out=sb[:], in_=ps[:], func=ACT.Identity, bias=bias)
             return sb
 
@@ -237,11 +253,6 @@ def tile_list_maxout_face_margins_kernel(
             nc.vector.scalar_tensor_tensor(
                 out=h_planes[g][:, t, :], in0=ps[:], scalar=bias, in1=sb[:], op0=ALU.add, op1=ALU.max
             )
-
-        def interleave_h(g):
-            dst = h_bf[g][:].rearrange("p (c i t) -> p c t i", i=RUN, t=PACK)
-            src = h_planes[g][:].rearrange("p t (c i) -> p c t i", i=RUN)
-            nc.scalar.copy(out=dst, in_=src)
 
         def quantize_h(g):
             nc.vector.quantize_mx(out=h_codes[g][:].bitcast(FP8X4), scales=h_scales[g][:], in_=h_bf[g][:])
@@ -254,47 +265,52 @@ def tile_list_maxout_face_margins_kernel(
                 dst[:], tab2w[g][:].bitcast(U32).indirect(idx2[:, half * HALF // 16 : (half + 1) * HALF // 16])
             )
 
-        c_ps = [bank(t) for t in range(PACK)]
-        a_ps = [bank(PACK + t) for t in range(PACK)]
+        c0_ps = [bank(t) for t in range(PACK)]
+        a0_ps = [bank(PACK + t) for t in range(PACK)]
         for t in range(PACK):
-            project_c(0, t, 0, c_ps[t])
+            project_c(0, t, 0, c0_ps[t])
         for t in range(PACK):
-            project_a(0, t, 0, a_ps[t], True)
+            project_a(0, t, 0, a0_ps[t], True)
         c0_sb = []
         for t in range(PACK):
-            project_c(0, t, 1, c_ps[t])
-            c0_sb.append(bring_out("c0_sb%d" % t, c_ps[t], b4_sb[0][:, t : t + 1]))
+            project_c(0, t, 1, c0_ps[t])
+            sb = placed("c0_sb%d" % t, [P, S], F32, W1_RAW01 + 4 * S * t)
+            c0_sb.append(bring_out(sb, c0_ps[t], b4_sb[:, 0, t : t + 1]))
         round_half(nc.scalar.copy, w1_raw11, 1, w1_bf11[1])
-        round_half(nc.vector.tensor_copy, w1_raw11, 0, w1_bf11[0])
+        gpsimd_copy(
+            w1_bf11[0][:].rearrange("p (tl m j) -> p m tl j", tl=2, j=PACK),
+            w1_raw11.rearrange("p j (m th tl) -> p th m tl j", th=HALVES, tl=2)[:, 0],
+        )
         for t in range(PACK):
-            project_a(0, t, 1, a_ps[t], False)
-            take_max(0, t, a_ps[t], b1_sb[:, 0, t : t + 1], c0_sb[t])
+            project_a(0, t, 1, a0_ps[t], False)
+            take_max(0, t, a0_ps[t], b1_sb[:, 0, t : t + 1], c0_sb[t])
             if t % 2 == 1:
                 quantize_half(1, t // 2, w1_bf11[t // 2])
-        c_sb = []
+        c1_sb = []
         for t in range(PACK):
-            c_ps = bank(t if t < 2 else t + 2)
+            c1_ps = bank(C1_BANKS[t])
             for a in range(NPASS):
-                project_c(1, t, a, c_ps)
-            c_sb.append(bring_out("c_sb%d" % t, c_ps, b4_sb[1][:, t : t + 1]))
+                project_c(1, t, a, c1_ps)
+            c1_sb.append(bring_out(held("c1_sb%d" % t, [P, S], F32), c1_ps, b4_sb[:, 1, t : t + 1]))
         for t in range(PACK):
-            a_ps = bank(t + 2 if t < 2 else t + 4)
-            first = 1 if t < 2 else 0
-            project_a(1, t, first, a_ps, True)
-            project_a(1, t, 1 - first, a_ps, False)
-            take_max(1, t, a_ps, b1_sb[:, 1, t : t + 1], c_sb[t])
+            a1_ps = bank(A1_BANKS[t])
+            project_a(1, t, A1_FIRST_PASS[t], a1_ps, True)
+            project_a(1, t, 1 - A1_FIRST_PASS[t], a1_ps, False)
+            take_max(1, t, a1_ps, b1_sb[:, 1, t : t + 1], c1_sb[t])
 
-        h_bf.append(placed("h_bf0", [P, S * PACK], BF16, STAGE_H0))
-        interleave_h(0)
-        h_bf.append(held("h_bf1", [P, S * PACK], BF16, "h_planes0"))
-        interleave_h(1)
+        h_bf = [placed("h_bf0", [P, S * PACK], BF16, H_BF0), held("h_bf1", [P, S * PACK], BF16)]
+        gpsimd_copy(h_bf[0][:].rearrange("p (n t) -> p n t", t=PACK), h_planes[0][:].rearrange("p t n -> p n t"))
+        nc.scalar.copy(
+            out=h_bf[1][:].rearrange("p (c i t) -> p c t i", i=RUN, t=PACK),
+            in_=h_planes[1][:].rearrange("p t (c i) -> p c t i", i=RUN),
+        )
 
         h_scales = [held("h_scales%d" % g, [P, S], U8) for g in range(NPASS)]
-        gather_v2(0, 0, held("v2w00", [P, HALF], U32, "c_sb%d" % (PACK - 2)))
+        gather_v2(0, 0, held("v2w00", [P, HALF], U32, "c1_sb%d" % (PACK - 2)))
         h_codes.append(held("h_codes0", [P, S], U32))
         quantize_h(0)
-        gather_v2(0, 1, held("v2w01", [P, HALF], U32, "c_sb%d" % (PACK - 1)))
-        h_codes.append(held("h_codes1", [P, S], U32))
+        gather_v2(0, 1, held("v2w01", [P, HALF], U32, "c1_sb%d" % (PACK - 1)))
+        h_codes.append(placed("h_codes1", [P, S], U32, TAB2_WORDS0))
         quantize_h(1)
         gather_v2(1, 0, held("v2w10", [P, HALF], U32))
         gather_v2(1, 1, held("v2w11", [P, HALF], U32))

@@ -184,10 +184,11 @@ def tile_list_maxout_face_margins_kernel(
         nc.vector.tensor_copy(v2s_picked[:], tab2s[:].bitcast(U8).indirect(idx2[:]))
         tab2w = []
         for g, offset in enumerate((TAB2_WORDS0, W1_RAW0)):
-            for quad in range(QUADS):
-                row = ROW0_V2 + ROWS * g + 4 * quad
-                to = 32 * quad + 4 * (g + 1)
-                nc.sync.dma_start(out=v2s[to : to + 4, :], in_=v2s_picked[row : row + 4, :].bitcast(I32))
+            for r in (2 * g, 2 * g + 1):
+                for a in range(NPASS):
+                    first = ROW0_V2 + ROWS * a + r
+                    staged_rows = v2s_picked[first : first + ROWS - 3 : 4, :]
+                    nc.sync.dma_start(out=v2s[4 * (a + 1) + r : P : 32, :], in_=staged_rows.bitcast(I32))
             tab2w.append(load_words(placed("tab2w%d" % g, [P, T2], I32, offset), tab2_words[g]))
 
         w4w = held("w4w", [P, NPASS, 2 * H], U8)

@@ -31,7 +31,7 @@ HALF = S2 // 2
 HALF_TILES = HALF // P
 GPSIMD_TILES = (1, 3)
 
-ROW0, ROW0_V2 = 32, 96
+ROW0 = 32
 JOINT = S + H
 
 W4_SCALES_RAW = 0
@@ -116,10 +116,10 @@ def tile_list_maxout_face_margins_kernel(
         tab2s = placed("tab2s", [P, T2 // 4], I32, TAB2_WORDS0)
         planes = [held("planes%d" % a, [P, JOINT // 4], I32) for a in range(NPASS)]
         v2s = held("v2s", [P, S2 // 4], I32)
+        nc.vector.memset(tab2s[:], 0)
         for staged in (tabs, w4s_raw):
             nc.vector.memset(staged[0:ROW0, :], 0)
             nc.vector.memset(staged[ROW0 + NPASS * ROWS : P, :], 0)
-        nc.vector.memset(tab2s[0:ROW0_V2, :], 0)
         for tile in planes + [v2s]:
             nc.vector.memset(tile[:], 0)
 
@@ -130,7 +130,7 @@ def tile_list_maxout_face_margins_kernel(
         w4w_raw = held("w4w_raw", [P, NPASS, H // 2], I32)
         nc.sync.dma_start(idx[:], offs)
         load_scales(tabs, tab_scales, ROW0)
-        load_scales(tab2s, tab2_scales, ROW0_V2)
+        nc.scalar.dma_start(out=tab2s[0:P:4, :], in_=tab2_scales.bitcast(I32).rearrange("a q col -> (a q) col"))
         load_scales(w4s_raw, w4_scales, ROW0)
         nc.sync.dma_start(idx2[:], offs2)
         thr_sb = held("thr_sb", [P, PACK], F32)
@@ -172,9 +172,8 @@ def tile_list_maxout_face_margins_kernel(
 
         move_planes(0, range(4))
         tabw0 = load_words(placed("tabw0", [P, T], I32, TAB_WORDS0), tab_words[0])
-        move_planes(1, range(1))
         tabw1 = load_words(placed("tabw1", [P, T], I32, TAB_WORDS1), tab_words[1])
-        move_planes(1, range(1, 4))
+        move_planes(1, range(4))
         w1_raw01 = load_w1(0, 1, placed("w1_raw01", [P, PACK, PASS], F32, W1_RAW01))
         w1_raw11 = load_w1(1, 1, placed("w1_raw11", [P, PACK, PASS], F32, W1_RAW11))
         vs = [planes[a][:].bitcast(U8)[:, 0:S] for a in range(NPASS)]
@@ -186,8 +185,8 @@ def tile_list_maxout_face_margins_kernel(
         for g, offset in enumerate((TAB2_WORDS0, W1_RAW0)):
             for r in (2 * g, 2 * g + 1):
                 for a in range(NPASS):
-                    first = ROW0_V2 + ROWS * a + r
-                    staged_rows = v2s_picked[first : first + ROWS - 3 : 4, :]
+                    first = 4 * (ROWS * a + r)
+                    staged_rows = v2s_picked[first : first + 4 * (ROWS - 3) : 16, :]
                     nc.sync.dma_start(out=v2s[4 * (a + 1) + r : P : 32, :], in_=staged_rows.bitcast(I32))
             tab2w.append(load_words(placed("tab2w%d" % g, [P, T2], I32, offset), tab2_words[g]))
 
@@ -311,7 +310,7 @@ def tile_list_maxout_face_margins_kernel(
         h_codes.append(held("h_codes0", [P, S], U32))
         quantize_h(0)
         gather_v2(0, 1, held("v2w01", [P, HALF], U32, "c1_sb%d" % (PACK - 1)))
-        h_codes.append(placed("h_codes1", [P, S], U32, TAB2_WORDS0))
+        h_codes.append(placed("h_codes1", [P, S], U32, H_BF0))
         quantize_h(1)
         gather_v2(1, 0, held("v2w10", [P, HALF], U32))
         gather_v2(1, 1, held("v2w11", [P, HALF], U32))

@@ -125,16 +125,16 @@ def tile_list_maxout_face_margins_kernel(
 
         def load_scales(dst, src, row0):
             rows = src.bitcast(I32).rearrange("a q col -> (a q) col")
-            nc.sync.dma_start(out=dst[row0 : row0 + NPASS * ROWS, :], in_=rows)
+            nc.scalar.dma_start(out=dst[row0 : row0 + NPASS * ROWS, :], in_=rows)
 
         w4w_raw = held("w4w_raw", [P, NPASS, H // 2], I32)
         nc.sync.dma_start(idx[:], offs)
         load_scales(tabs, tab_scales, ROW0)
-        nc.scalar.dma_start(out=tab2s[0:P:4, :], in_=tab2_scales.bitcast(I32).rearrange("a q col -> (a q) col"))
         load_scales(w4s_raw, w4_scales, ROW0)
+        nc.scalar.dma_start(out=tab2s[0:P:4, :], in_=tab2_scales.bitcast(I32).rearrange("a q col -> (a q) col"))
         nc.sync.dma_start(idx2[:], offs2)
         thr_sb = held("thr_sb", [P, PACK], F32)
-        nc.sync.dma_start(out=thr_sb[:], in_=thr.rearrange("(p c) -> p c", c=PACK))
+        nc.scalar.dma_start(out=thr_sb[:], in_=thr.rearrange("(p c) -> p c", c=PACK))
         nc.sync.dma_start(out=w4w_raw[:], in_=w4_words.bitcast(I32).rearrange("a p col -> p a col"))
         w1_raw0 = placed("w1_raw0", [P, PACK, H], F32, W1_RAW0)
         nc.sync.dma_start(out=w1_raw0[:], in_=w1[0:PASS, :].rearrange("(p j) c -> p j c", j=PACK))

@@ -338,7 +338,7 @@ def tile_list_maxout_face_margins_kernel(
                 y_raw = outs.tile([P, S], F32, name="y_raw", bufs=len(GPSIMD_TILES))
                 nc.scalar.copy(out=y_raw[:], in_=y_ps[i][:])
                 nc.gpsimd.tensor_tensor(out=y_sb[:], in0=y_raw[:], in1=thr_all[:], op=ALU.subtract)
-                nc.scalar.dma_start(out=out[i * P : (i + 1) * P, :], in_=y_sb[:])
             else:
                 nc.vector.tensor_tensor(out=y_sb[:], in0=y_ps[i][:], in1=thr_all[:], op=ALU.subtract)
-                nc.sync.dma_start(out=out[i * P : (i + 1) * P, :], in_=y_sb[:])
+            queue = nc.scalar if i in (2, 4, 5, 7) else nc.sync
+            queue.dma_start(out=out[i * P : (i + 1) * P, :], in_=y_sb[:])

@@ -25,6 +25,8 @@ QUADS = 4
 HALVES = 2
 HALF_COLS = PASS // HALVES
 ROWS = 16
+GPSIMD_PROBES = 384
+SCALAR_M = 96
 RUN = 4
 OUT_TILES = S2 // P
 HALF = S2 // 2
@@ -199,7 +201,11 @@ def tile_list_maxout_face_margins_kernel(
         )
 
         vw = [held("vw0", [P, S], U32)]
-        nc.vector.tensor_copy(vw[0][:], tabw0[:].bitcast(U32).indirect(idx[:]))
+        for half in range(2):
+            nc.vector.tensor_copy(
+                vw[0][:, half * S // 2 : (half + 1) * S // 2],
+                tabw0[:].bitcast(U32).indirect(idx[:, half * S // 32 : (half + 1) * S // 32]),
+            )
         w1_bf00 = held("w1_bf00", [P, PASS * PACK], BF16)
         round_w1(w1_raw00, w1_bf00)
         quantize_w1(0, w1_bf00, placed("w1_codes00", [P, PASS], U32, TAB_WORDS0))
@@ -233,15 +239,15 @@ def tile_list_maxout_face_margins_kernel(
                 stop=not first,
             )
 
-        def project_c(g, t, a, c_ps):
+        def project_c(g, t, a, c_ps, probes=slice(0, S)):
             col = g * PASS + t * P
             nc.tensor.matmul_mx(
-                out=c_ps[:],
+                out=c_ps[:, probes],
                 lhsT=w4w[:, a, 2 * col : 2 * (col + P)].bitcast(FP4X4),
                 lhsT_scale=w4s[a][:, col : col + P],
-                rhs=vw[a][:].bitcast(FP8X4),
-                rhs_scale=vs[a],
-                start=(a == 0),
+                rhs=vw[a][:, probes].bitcast(FP8X4),
+                rhs_scale=vs[a][:, probes],
+                start=(a == 0 and probes.start == 0),
                 stop=(a == NPASS - 1),
             )
 
@@ -267,8 +273,9 @@ def tile_list_maxout_face_margins_kernel(
 
         c0_ps = [bank(t) for t in range(PACK)]
         a0_ps = [bank(PACK + t) for t in range(PACK)]
-        for t in range(PACK):
-            project_c(0, t, 0, c0_ps[t])
+        for half in range(2):
+            for t in range(PACK):
+                project_c(0, t, 0, c0_ps[t], slice(half * S // 2, (half + 1) * S // 2))
         for t in range(PACK):
             project_a(0, t, 0, a0_ps[t], True)
         c0_sb = []
@@ -276,16 +283,20 @@ def tile_list_maxout_face_margins_kernel(
             project_c(0, t, 1, c0_ps[t])
             sb = placed("c0_sb%d" % t, [P, S], F32, W1_RAW01 + 4 * S * t)
             c0_sb.append(bring_out(sb, c0_ps[t], b4_sb[:, 0, t : t + 1]))
-        round_half(nc.scalar.copy, w1_raw11, 1, w1_bf11[1])
-        gpsimd_copy(
-            w1_bf11[0][:].rearrange("p (tl m j) -> p m tl j", tl=2, j=PACK),
-            w1_raw11.rearrange("p j (m th tl) -> p th m tl j", th=HALVES, tl=2)[:, 0],
+        nc.scalar.copy(
+            out=w1_bf11[1][:].rearrange("p (tl m j) -> p m j tl", tl=2, j=PACK)[:, 0:SCALAR_M],
+            in_=w1_raw11.rearrange("p j (m th tl) -> p th m j tl", th=HALVES, tl=2)[:, 1, 0:SCALAR_M],
         )
+        for th, first in ((1, SCALAR_M), (0, 0)):
+            gpsimd_copy(
+                w1_bf11[th][:].rearrange("p (tl m j) -> p m tl j", tl=2, j=PACK)[:, first:P],
+                w1_raw11.rearrange("p j (m th tl) -> p th m tl j", th=HALVES, tl=2)[:, th, first:P],
+            )
         for t in range(PACK):
             project_a(0, t, 1, a0_ps[t], False)
             take_max(0, t, a0_ps[t], b1_sb[:, 0, t : t + 1], c0_sb[t])
-            if t % 2 == 1:
-                quantize_half(1, t // 2, w1_bf11[t // 2])
+            if t >= 2:
+                quantize_half(1, t - 2, w1_bf11[t - 2])
         c1_sb = []
         for t in range(PACK):
             c1_ps = bank(C1_BANKS[t])
@@ -299,7 +310,14 @@ def tile_list_maxout_face_margins_kernel(
             take_max(1, t, a1_ps, b1_sb[:, 1, t : t + 1], c1_sb[t])
 
         h_bf = [placed("h_bf0", [P, S * PACK], BF16, H_BF0), held("h_bf1", [P, S * PACK], BF16)]
-        gpsimd_copy(h_bf[0][:].rearrange("p (n t) -> p n t", t=PACK), h_planes[0][:].rearrange("p t n -> p n t"))
+        gpsimd_copy(
+            h_bf[0][:].rearrange("p (n t) -> p n t", t=PACK)[:, 0:GPSIMD_PROBES],
+            h_planes[0][:].rearrange("p t n -> p n t")[:, 0:GPSIMD_PROBES],
+        )
+        nc.scalar.copy(
+            out=h_bf[0][:, GPSIMD_PROBES * PACK :].rearrange("p (c i t) -> p c t i", i=RUN, t=PACK),
+            in_=h_planes[0][:, :, GPSIMD_PROBES:].rearrange("p t (c i) -> p c t i", i=RUN),
+        )
         nc.scalar.copy(
             out=h_bf[1][:].rearrange("p (c i t) -> p c t i", i=RUN, t=PACK),
             in_=h_planes[1][:].rearrange("p t (c i) -> p c t i", i=RUN),

from contextlib import ExitStack

import concourse.mybir as mybir
from concourse.masks import make_identity

K, H, T, S, T2, S2 = 1024, 1024, 2048, 512, 4096, 1024
FLOPS = 2 * K * H * S * 2 + 2 * H * S2 * S

F32 = mybir.dt.float32
BF16 = mybir.dt.bfloat16
I32 = mybir.dt.int32
U32 = mybir.dt.uint32
U16 = mybir.dt.uint16
U8 = mybir.dt.uint8
FP8X4 = mybir.dt.float8_e4m3fn_x4
FP4X4 = mybir.dt.float4_e2m1fn_x4
ALU = mybir.AluOpType
ACT = mybir.ActivationFunctionType

P = 128
PACK = 4
PASS = P * PACK
NPASS = 2
QUADS = 4
HALVES = 2
HALF_COLS = PASS // HALVES
ROWS = 16
GPSIMD_PROBES = 384
SCALAR_M = 96
RUN = 4
OUT_TILES = S2 // P
HALF = S2 // 2
HALF_TILES = HALF // P
GPSIMD_TILES = (1, 3)

ROW0 = 32
JOINT = S + H

W4_SCALES_RAW = 0
TAB_WORDS1 = W4_SCALES_RAW + H
W1_RAW11 = TAB_WORDS1 + 4 * T
W1_RAW01 = W1_RAW11 + 4 * PACK * PASS
TAB_WORDS0 = W1_RAW01 + 4 * PACK * PASS
W1_RAW0 = TAB_WORDS0 + 4 * T
TAB2_WORDS0 = W1_RAW0 + 4 * PACK * H
H_BF0 = TAB2_WORDS0 + 4 * T2

C1_BANKS = (0, 4, 5, 6)
A1_BANKS = (1, 2, 3, 7)
A1_FIRST_PASS = (0, 1, 1, 0)


def tile_list_maxout_face_margins_kernel(
    tc, tab_words, tab_scales, offs, w1, b1, w4_words, w4_scales, b4, tab2_words, tab2_scales, offs2, thr, out
):
    nc = tc.nc
    with ExitStack() as ctx:
        keep = ctx.enter_context(tc.tile_pool(name="keep", bufs=1))
        outs = ctx.enter_context(tc.tile_pool(name="outs", bufs=OUT_TILES))
        psum = ctx.enter_context(tc.psum_pool(name="psum", bufs=1))
        reuse = ctx.enter_context(tc.tile_pool(name="reuse", bufs=1))

        def placed(name, shape, dtype, offset):
            return reuse.tile(shape, dtype, name=name, offset=offset, align_bytes=64)

        def held(name, shape, dtype, follows=""):
            return keep.tile(shape, dtype, name=name, tag=follows or name, align_bytes=64)

        def bank(b):
            return psum.tile([P, S], F32, name="bank", tag="bank%d" % b)

        idx = keep.tile([P, S // 16], U16, name="idx")
        idx2 = keep.tile([P, S2 // 16], U16, name="idx2")

        def load_w1(g, a, raw):
            rows = w1[a * PASS : (a + 1) * PASS, g * PASS : (g + 1) * PASS]
            nc.sync.dma_start(out=raw[:], in_=rows.rearrange("(p j) c -> p j c", j=PACK))
            return raw[:]

        def load_words(dst, words):
            nc.sync.dma_start(out=dst[:], in_=words.rearrange("p col j -> p (col j)").bitcast(I32))
            return dst

        def round_w1(raw, dst):
            nc.scalar.copy(
                out=dst[:].rearrange("p (th tl m j) -> p th m j tl", th=HALVES, tl=2, j=PACK),
                in_=raw.rearrange("p j (m th tl) -> p th m j tl", th=HALVES, tl=2),
            )

        def round_half(copy, raw, th, dst):
            copy(
                out=dst[:].rearrange("p (tl m j) -> p m j tl", tl=2, j=PACK),
                in_=raw.rearrange("p j (m th tl) -> p th m j tl", th=HALVES, tl=2)[:, th],
            )

        def gpsimd_copy(out_view, in_view):
            nc.gpsimd.tensor_scalar(out=out_view, in0=in_view, scalar1=1.0, scalar2=0.0, op0=ALU.mult, op1=ALU.add)

        w1_codes = {}
        w1_scales = {}

        def quantize_w1(g, src, codes):
            scales = held("w1_scales%d0" % g, [P, PASS], U8)
            for th in range(HALVES):
                w1_codes.setdefault((g, 0, th), codes[:, th * HALF_COLS : (th + 1) * HALF_COLS])
                w1_scales.setdefault((g, 0, th), scales[:, th * HALF_COLS : (th + 1) * HALF_COLS])
            nc.vector.quantize_mx(out=codes[:].bitcast(FP8X4), scales=scales[:], in_=src[:])

        def quantize_half(g, th, src):
            codes = held("w1_codes%d1%d" % (g, th), [P, HALF_COLS], U32)
            scales = held("w1_scales%d1%d" % (g, th), [P, HALF_COLS], U8)
            w1_codes.setdefault((g, 1, th), codes[:])
            w1_scales.setdefault((g, 1, th), scales[:])
            nc.vector.quantize_mx(out=codes[:].bitcast(FP8X4), scales=scales[:], in_=src[:])

        tabs = held("tabs", [P, T // 4], I32)
        w4s_raw = placed("w4s_raw", [P, H // 4], I32, W4_SCALES_RAW)
        tab2s = placed("tab2s", [P, T2 // 4], I32, TAB2_WORDS0)
        planes = [held("planes%d" % a, [P, JOINT // 4], I32) for a in range(NPASS)]
        v2s = held("v2s", [P, S2 // 4], I32)
        nc.vector.memset(tab2s[:], 0)
        for staged in (tabs, w4s_raw):
            nc.vector.memset(staged[0:ROW0, :], 0)
            nc.vector.memset(staged[ROW0 + NPASS * ROWS : P, :], 0)
        for tile in planes + [v2s]:
            nc.vector.memset(tile[:], 0)

        def load_scales(dst, src, row0):
            rows = src.bitcast(I32).rearrange("a q col -> (a q) col")
            nc.scalar.dma_start(out=dst[row0 : row0 + NPASS * ROWS, :], in_=rows)

        w4w_raw = held("w4w_raw", [P, NPASS, H // 2], I32)
        nc.sync.dma_start(idx[:], offs)
        load_scales(tabs, tab_scales, ROW0)
        load_scales(w4s_raw, w4_scales, ROW0)
        nc.scalar.dma_start(out=tab2s[0:P:4, :], in_=tab2_scales.bitcast(I32).rearrange("a q col -> (a q) col"))
        nc.sync.dma_start(idx2[:], offs2)
        thr_sb = held("thr_sb", [P, PACK], F32)
        nc.scalar.dma_start(out=thr_sb[:], in_=thr.rearrange("(p c) -> p c", c=PACK))
        nc.sync.dma_start(out=w4w_raw[:], in_=w4_words.bitcast(I32).rearrange("a p col -> p a col"))
        w1_raw0 = placed("w1_raw0", [P, PACK, H], F32, W1_RAW0)
        nc.sync.dma_start(out=w1_raw0[:], in_=w1[0:PASS, :].rearrange("(p j) c -> p j c", j=PACK))
        w1_raw00, w1_raw10 = w1_raw0[:, :, 0:PASS], w1_raw0[:, :, PASS:H]

        b1_sb = held("b1_sb", [P, NPASS, PACK], F32)
        b4_sb = held("b4_sb", [P, NPASS, PACK], F32)
        nc.gpsimd.dma_start(out=b1_sb[:], in_=b1.rearrange("(g p t) -> p g t", g=NPASS, t=PACK))
        nc.gpsimd.dma_start(out=b4_sb[:], in_=b4.rearrange("(g p t) -> p g t", g=NPASS, t=PACK))
        ident = held("ident", [P, P], F32)
        make_identity(nc, ident[:])

        thr_ps = psum.tile([P, PACK, P], F32, name="thr_ps", tag="bank%d" % (OUT_TILES - 1))
        for c in range(PACK):
            nc.tensor.transpose(thr_ps[:, c, :], thr_sb[:, c : c + 1].to_broadcast([P, P]), ident[:])
        thr_all = held("thr_all", [P, S], F32)
        nc.scalar.copy(
            out=thr_all[:].rearrange("row (p c) -> row p c", c=PACK), in_=thr_ps[:].rearrange("row c p -> row p c")
        )

        joint = held("joint", [P, JOINT], U8)
        vs_picked = placed("vs_picked", [P, W1_RAW0 - TAB_WORDS1], U8, TAB_WORDS1)[:, 0:S]
        nc.vector.tensor_copy(vs_picked, tabs[:].bitcast(U8).indirect(idx[:]))
        nc.vector.tensor_copy(
            out=joint[:, S : S + H].rearrange("p (g t m) -> p g t m", g=NPASS, t=PACK),
            in_=w4s_raw[:].bitcast(U8).rearrange("p (g m t) -> p g t m", g=NPASS, t=PACK),
        )
        nc.vector.tensor_copy(out=joint[:, 0:S].bitcast(I32), in_=vs_picked.bitcast(I32))

        def move_planes(a, rows):
            for r in rows:
                first = ROW0 + ROWS * a + r
                staged_rows = joint[first : first + ROWS - 3 : 4, :]
                nc.sync.dma_start(out=planes[a][r:P:32, :], in_=staged_rows.bitcast(I32))

        move_planes(0, range(4))
        tabw0 = load_words(placed("tabw0", [P, T], I32, TAB_WORDS0), tab_words[0])
        tabw1 = load_words(placed("tabw1", [P, T], I32, TAB_WORDS1), tab_words[1])
        move_planes(1, range(4))
        w1_raw01 = load_w1(0, 1, placed("w1_raw01", [P, PACK, PASS], F32, W1_RAW01))
        w1_raw11 = load_w1(1, 1, placed("w1_raw11", [P, PACK, PASS], F32, W1_RAW11))
        vs = [planes[a][:].bitcast(U8)[:, 0:S] for a in range(NPASS)]
        w4s = [planes[a][:].bitcast(U8)[:, S : S + H] for a in range(NPASS)]

        v2s_picked = placed("v2s_picked", [P, S2], U8, W4_SCALES_RAW)
        nc.vector.tensor_copy(v2s_picked[:], tab2s[:].bitcast(U8).indirect(idx2[:]))
        tab2w = []
        for g, offset in enumerate((TAB2_WORDS0, W1_RAW0)):
            for r in (2 * g, 2 * g + 1):
                for a in range(NPASS):
                    first = 4 * (ROWS * a + r)
                    staged_rows = v2s_picked[first : first + 4 * (ROWS - 3) : 16, :]
                    nc.sync.dma_start(out=v2s[4 * (a + 1) + r : P : 32, :], in_=staged_rows.bitcast(I32))
            tab2w.append(load_words(placed("tab2w%d" % g, [P, T2], I32, offset), tab2_words[g]))

        w4w = held("w4w", [P, NPASS, 2 * H], U8)
        w4w_to = w4w[:].rearrange("p a col -> p (a col)").bitcast(U16)
        w4w_from = w4w_raw[:].rearrange("p a col -> p (a col)").bitcast(U16)
        nc.vector.tensor_copy(
            out=w4w_to.rearrange("p (ag t m) -> p ag t m", ag=NPASS * NPASS, t=PACK),
            in_=w4w_from.rearrange("p (ag m t) -> p ag t m", ag=NPASS * NPASS, t=PACK),
        )

        vw = [held("vw0", [P, S], U32)]
        for half in range(2):
            nc.vector.tensor_copy(
                vw[0][:, half * S // 2 : (half + 1) * S // 2],
                tabw0[:].bitcast(U32).indirect(idx[:, half * S // 32 : (half + 1) * S // 32]),
            )
        w1_bf00 = held("w1_bf00", [P, PASS * PACK], BF16)
        round_w1(w1_raw00, w1_bf00)
        quantize_w1(0, w1_bf00, placed("w1_codes00", [P, PASS], U32, TAB_WORDS0))
        vw.append(held("vw1", [P, S], U32))
        nc.vector.tensor_copy(vw[1][:], tabw1[:].bitcast(U32).indirect(idx[:]))
        w1_bf10 = held("w1_bf10", [P, PASS * PACK], BF16)
        round_w1(w1_raw10, w1_bf10)
        quantize_w1(1, w1_bf10, placed("w1_codes10", [P, PASS], U32, TAB_WORDS1))
        w1_bf01 = [held("w1_bf01%d" % th, [P, HALF_COLS * PACK], BF16) for th in range(HALVES)]
        for th, copy in enumerate((nc.vector.tensor_copy, nc.scalar.copy)):
            round_half(copy, w1_raw01, th, w1_bf01[th])
        for th in range(HALVES):
            quantize_half(0, th, w1_bf01[th])
        w1_bf11 = [
            held("w1_bf110", [P, HALF_COLS * PACK], BF16, "w1_bf011"),
            placed("w1_bf111", [P, HALF_COLS * PACK], BF16, H_BF0),
        ]

        h_planes = [held("h_planes%d" % g, [P, PACK, S], BF16) for g in range(NPASS)]
        h_codes = []

        def project_a(g, t, a, a_ps, first):
            th, tl = divmod(t, 2)
            nc.tensor.matmul_mx(
                out=a_ps[:],
                lhsT=w1_codes[g, a, th][:, tl * P : (tl + 1) * P].bitcast(FP8X4),
                lhsT_scale=w1_scales[g, a, th][:, tl * P : (tl + 1) * P],
                rhs=vw[a][:].bitcast(FP8X4),
                rhs_scale=vs[a],
                start=first,
                stop=not first,
            )

        def project_c(g, t, a, c_ps, probes=slice(0, S)):
            col = g * PASS + t * P
            nc.tensor.matmul_mx(
                out=c_ps[:, probes],
                lhsT=w4w[:, a, 2 * col : 2 * (col + P)].bitcast(FP4X4),
                lhsT_scale=w4s[a][:, col : col + P],
                rhs=vw[a][:, probes].bitcast(FP8X4),
                rhs_scale=vs[a][:, probes],
                start=(a == 0 and probes.start == 0),
                stop=(a == NPASS - 1),
            )

        def bring_out(sb, ps, bias):
            nc.scalar.activation(out=sb[:], in_=ps[:], func=ACT.Identity, bias=bias)
            return sb

        def take_max(g, t, ps, bias, sb):
            nc.vector.scalar_tensor_tensor(
                out=h_planes[g][:, t, :], in0=ps[:], scalar=bias, in1=sb[:], op0=ALU.add, op1=ALU.max
            )

        def quantize_h(g):
            nc.vector.quantize_mx(out=h_codes[g][:].bitcast(FP8X4), scales=h_scales[g][:], in_=h_bf[g][:])

        v2w = {}

        def gather_v2(g, half, dst):
            v2w.setdefault((g, half), dst)
            nc.vector.tensor_copy(
                dst[:], tab2w[g][:].bitcast(U32).indirect(idx2[:, half * HALF // 16 : (half + 1) * HALF // 16])
            )

        c0_ps = [bank(t) for t in range(PACK)]
        a0_ps = [bank(PACK + t) for t in range(PACK)]
        for half in range(2):
            for t in range(PACK):
                project_c(0, t, 0, c0_ps[t], slice(half * S // 2, (half + 1) * S // 2))
        for t in range(PACK):
            project_a(0, t, 0, a0_ps[t], True)
        c0_sb = []
        for t in range(PACK):
            project_c(0, t, 1, c0_ps[t])
            sb = placed("c0_sb%d" % t, [P, S], F32, W1_RAW01 + 4 * S * t)
            c0_sb.append(bring_out(sb, c0_ps[t], b4_sb[:, 0, t : t + 1]))
        nc.scalar.copy(
            out=w1_bf11[1][:].rearrange("p (tl m j) -> p m j tl", tl=2, j=PACK)[:, 0:SCALAR_M],
            in_=w1_raw11.rearrange("p j (m th tl) -> p th m j tl", th=HALVES, tl=2)[:, 1, 0:SCALAR_M],
        )
        for th, first in ((1, SCALAR_M), (0, 0)):
            gpsimd_copy(
                w1_bf11[th][:].rearrange("p (tl m j) -> p m tl j", tl=2, j=PACK)[:, first:P],
                w1_raw11.rearrange("p j (m th tl) -> p th m tl j", th=HALVES, tl=2)[:, th, first:P],
            )
        for t in range(PACK):
            project_a(0, t, 1, a0_ps[t], False)
            take_max(0, t, a0_ps[t], b1_sb[:, 0, t : t + 1], c0_sb[t])
            if t >= 2:
                quantize_half(1, t - 2, w1_bf11[t - 2])
        c1_sb = []
        for t in range(PACK):
            c1_ps = bank(C1_BANKS[t])
            for a in range(NPASS):
                project_c(1, t, a, c1_ps)
            c1_sb.append(bring_out(held("c1_sb%d" % t, [P, S], F32), c1_ps, b4_sb[:, 1, t : t + 1]))
        for t in range(PACK):
            a1_ps = bank(A1_BANKS[t])
            project_a(1, t, A1_FIRST_PASS[t], a1_ps, True)
            project_a(1, t, 1 - A1_FIRST_PASS[t], a1_ps, False)
            take_max(1, t, a1_ps, b1_sb[:, 1, t : t + 1], c1_sb[t])

        h_bf = [placed("h_bf0", [P, S * PACK], BF16, H_BF0), held("h_bf1", [P, S * PACK], BF16)]
        gpsimd_copy(
            h_bf[0][:].rearrange("p (n t) -> p n t", t=PACK)[:, 0:GPSIMD_PROBES],
            h_planes[0][:].rearrange("p t n -> p n t")[:, 0:GPSIMD_PROBES],
        )
        nc.scalar.copy(
            out=h_bf[0][:, GPSIMD_PROBES * PACK :].rearrange("p (c i t) -> p c t i", i=RUN, t=PACK),
            in_=h_planes[0][:, :, GPSIMD_PROBES:].rearrange("p t (c i) -> p c t i", i=RUN),
        )
        nc.scalar.copy(
            out=h_bf[1][:].rearrange("p (c i t) -> p c t i", i=RUN, t=PACK),
            in_=h_planes[1][:].rearrange("p t (c i) -> p c t i", i=RUN),
        )

        h_scales = [held("h_scales%d" % g, [P, S], U8) for g in range(NPASS)]
        gather_v2(0, 0, held("v2w00", [P, HALF], U32, "c1_sb%d" % (PACK - 2)))
        h_codes.append(held("h_codes0", [P, S], U32))
        quantize_h(0)
        gather_v2(0, 1, held("v2w01", [P, HALF], U32, "c1_sb%d" % (PACK - 1)))
        h_codes.append(placed("h_codes1", [P, S], U32, H_BF0))
        quantize_h(1)
        gather_v2(1, 0, held("v2w10", [P, HALF], U32))
        gather_v2(1, 1, held("v2w11", [P, HALF], U32))

        y_ps = [bank(i) for i in range(OUT_TILES)]

        def score(i, g):
            col = (i % HALF_TILES) * P
            nc.tensor.matmul_mx(
                out=y_ps[i][:],
                lhsT=v2w[g, i // HALF_TILES][:, col : col + P].bitcast(FP8X4),
                lhsT_scale=v2s[4 * (g + 1) : P, :].bitcast(U8)[:, i * P : (i + 1) * P],
                rhs=h_codes[g][:].bitcast(FP8X4),
                rhs_scale=h_scales[g][:],
                start=(g == 0),
                stop=(g == NPASS - 1),
            )

        for i in range(OUT_TILES):
            score(i, 0)
        for i in range(OUT_TILES):
            score(i, 1)
            y_sb = outs.tile([P, S], F32, name="y_sb")
            if i in GPSIMD_TILES:
                y_raw = outs.tile([P, S], F32, name="y_raw", bufs=len(GPSIMD_TILES))
                nc.scalar.copy(out=y_raw[:], in_=y_ps[i][:])
                nc.gpsimd.tensor_tensor(out=y_sb[:], in0=y_raw[:], in1=thr_all[:], op=ALU.subtract)
            else:
                nc.vector.tensor_tensor(out=y_sb[:], in0=y_ps[i][:], in1=thr_all[:], op=ALU.subtract)
            queue = nc.scalar if i in (2, 4, 5, 7) else nc.sync
            queue.dma_start(out=out[i * P : (i + 1) * P, :], in_=y_sb[:])
